import numpy as np
import ml_dtypes


def mxq(x, axis, fmt="e4m3"):
    dtype, down = {"e4m3": (ml_dtypes.float8_e4m3fn, 7), "e5m2": (ml_dtypes.float8_e5m2, 14)}[fmt]
    v = np.moveaxis(np.asarray(x, np.float32).astype(ml_dtypes.bfloat16).astype(np.float64), axis, -1)
    blocks = v.reshape(v.shape[:-1] + (-1, 32))
    amax = np.abs(blocks).max(-1, keepdims=True)
    byte = np.maximum(np.where(amax > 0, np.frexp(amax)[1] - 1 + 127, 0) - down, 1)
    scale = np.exp2(byte - 127.0)
    codes = (blocks / scale).astype(np.float32).astype(dtype).astype(np.float64)
    return np.moveaxis((codes * scale).reshape(v.shape), -1, axis)


WIDE = False


def mx_kscale(k):
    if not WIDE:
        return np.ones(k)
    levels = np.array([10, -10, 5, -5, 0])
    if k % 512:
        return np.exp2(np.random.permutation(np.resize(levels, k // 32))).repeat(32)
    a = np.empty((k // 512, 16))
    for p in range(k // 512):
        a[p, :8] = np.random.permutation(np.resize(levels, 8))
        for g in range(8):
            far = levels[np.abs(levels - a[p, g]) >= 10]
            a[p, g + 8] = far[np.random.randint(len(far))]
    return np.exp2(a.ravel()).repeat(32)


def f64(x):
    return np.asarray(x).astype(np.float64)


def striped(idx):
    return np.tile(idx.reshape(-1, 16).T, (8, 1)).astype(np.uint16)


def unstriped(offs):
    return offs[:16].T.reshape(-1).astype(np.int64)


E2M1 = np.array([0.0, 0.5, 1.0, 1.5, 2.0, 3.0, 4.0, 6.0, -0.0, -0.5, -1.0, -1.5, -2.0, -3.0, -4.0, -6.0])


def pack_weight(w, fmt):
    k, n = w.shape
    w = f64(np.asarray(w, np.float32).astype(ml_dtypes.bfloat16)).reshape(k // 32, 32, n)
    amax = np.abs(w).max(1)
    if fmt == "e4m3":
        byte = np.frexp(amax)[1] - 1 + 127 - 7
    else:
        mant, ex = np.frexp(amax / 6.0)
        byte = np.where(mant > 0.5, ex, ex - 1) + 127
    byte = np.clip(np.where(amax > 0, byte, 1), 1, 254)
    scaled = (w * np.exp2(127.0 - byte)[:, None, :]).reshape(k, n).astype(np.float32)
    by_word = np.ascontiguousarray(scaled.reshape(k // 512, 128, 4, n).transpose(0, 1, 3, 2))
    if fmt == "e4m3":
        words = by_word.astype(ml_dtypes.float8_e4m3fn).view(np.uint8)
    else:
        c = by_word.astype(ml_dtypes.float4_e2m1fn).view(np.uint8) & 0xF
        words = (c[..., 0::2] | (c[..., 1::2] << 4)).reshape(k // 512, 128, 2 * n)
    return np.ascontiguousarray(words), np.ascontiguousarray(byte.astype(np.uint8).reshape(k // 512, 16, n))


def unpack_weight(words, scales, fmt):
    g, _, n = scales.shape
    words = np.ascontiguousarray(words).reshape(g, 128, n, -1)
    if fmt == "e4m3":
        vals = words.view(ml_dtypes.float8_e4m3fn).astype(np.float64)
    else:
        nib = np.empty((g, 128, n, 4), np.uint8)
        nib[..., 0::2] = words & 0xF
        nib[..., 1::2] = words >> 4
        vals = E2M1[nib]
    vals = vals * np.repeat(np.exp2(scales.astype(np.float64) - 127.0), 8, axis=1)[..., None]
    return vals.transpose(0, 1, 3, 2).reshape(g * 512, n)


def gelu(v):
    return 0.5 * v * (1.0 + np.tanh(np.sqrt(2.0 / np.pi) * (v + 0.044715 * v**3)))


K, H, T, S, P = 1536, 1024, 2048, 1024, 512

def setup_inputs():
    n = np.random.standard_normal
    s = mx_kscale(K)[:, None]
    u = mx_kscale(H)[:, None]
    tab_words, tab_scales = pack_weight(n((K, T)) * s, "e4m3")
    w4_words, w4_scales = pack_weight(n((H, H)) / np.sqrt(H) / u, "e2m1")
    return {
        "tab_words": tab_words, "tab_scales": tab_scales,
        "offs": striped(np.random.permutation(T)[:S]),
        "pos1": striped(np.random.permutation(S)[:P]),
        "pos2": striped(np.random.permutation(S)[:P]),
        "w1": (n((K, H)) / np.sqrt(K) / s * u.T).astype(np.float32),
        "lossw": np.exp(0.3 * n(H)).astype(np.float32),
        "w4_words": w4_words, "w4_scales": w4_scales,
        "d": (np.random.uniform(0.4, 1.0, H) / u[:, 0]).astype(np.float32),
    }

def reference(tab_words, tab_scales, offs, pos1, pos2, w1, lossw, w4_words, w4_scales, d):
    v = unpack_weight(tab_words, tab_scales, "e4m3")[:, unstriped(offs)]
    h = mxq(f64(w1), 0, "e4m3").T @ v
    x = f64(lossw)[:, None] * h[:, unstriped(pos1)]
    w4 = unpack_weight(w4_words, w4_scales, "e2m1")
    y = w4.T @ mxq(x, 0, "e4m3")
    th = np.tanh(f64(d)[:, None] * h[:, unstriped(pos2)])
    out = y * (1.0 - np.square(th))
    return out

@@ -1,0 +1,274 @@
+from contextlib import ExitStack
+
+import concourse.mybir as mybir
+
+K, H, T, S, M = 1536, 1024, 2048, 1024, 512
+FLOPS = 2 * K * H * S + 2 * H * H * M
+
+F32 = mybir.dt.float32
+BF16 = mybir.dt.bfloat16
+I32 = mybir.dt.int32
+U32 = mybir.dt.uint32
+U16 = mybir.dt.uint16
+U8 = mybir.dt.uint8
+FP8X4 = mybir.dt.float8_e4m3fn_x4
+FP4X4 = mybir.dt.float4_e2m1fn_x4
+ACT = mybir.ActivationFunctionType
+ALU = mybir.AluOpType
+
+P = 128
+PACK = 4
+KP = P * PACK
+K_PASSES = K // KP
+R_PASSES = H // KP
+BANK = 512
+QUADS = 4
+
+
+def tile_list_glockenspiel_backward_sweep_kernel(
+    tc, tab_words, tab_scales, offs, pos1, pos2, w1, lossw, w4_words, w4_scales, d, out
+):
+    nc = tc.nc
+    with ExitStack() as ctx:
+        keep = ctx.enter_context(tc.tile_pool(name="keep", bufs=1))
+        ring = ctx.enter_context(tc.tile_pool(name="ring", bufs=3))
+        psum = ctx.enter_context(tc.psum_pool(name="psum", bufs=8))
+
+        offs_sb = keep.tile([P, S // 16], U16, name="offs_sb")
+        pos1_sb = keep.tile([P, M // 16], U16, name="pos1_sb")
+        pos2_sb = keep.tile([P, M // 16], U16, name="pos2_sb")
+
+        tab_sc = keep.tile([P, T], U8, name="tab_sc", align_bytes=64)
+        nc.vector.memset(tab_sc[:].bitcast(I32), 0)
+        w4_sc_raw = keep.tile([P, R_PASSES * H], U8, name="w4_sc_raw", align_bytes=64)
+        nc.gpsimd.memset(w4_sc_raw[:].bitcast(I32), 0)
+        for q in range(QUADS):
+            nc.gpsimd.dma_start(
+                out=w4_sc_raw[32 * q : 32 * q + 4, :].bitcast(I32).rearrange("r (a n) -> r a n", a=R_PASSES),
+                in_=w4_scales[:, 4 * q : 4 * q + 4, :].bitcast(I32).rearrange("a r n -> r a n"),
+            )
+        d_sb = keep.tile([P, R_PASSES, PACK], F32, name="d_sb")
+        nc.gpsimd.dma_start(out=d_sb[:], in_=d.rearrange("(b p t) -> p b t", p=P, t=PACK))
+
+        tab_sb = [keep.tile([P, T], I32, name=f"tab_sb{a}") for a in range(K_PASSES)]
+        raw = {}
+
+        def load_tab(a):
+            nc.sync.dma_start(out=tab_sb[a][:], in_=tab_words[a].rearrange("p t i -> p (t i)").bitcast(I32))
+
+        def load_w1(a, b, parts):
+            width = KP // parts
+            raw[a, b] = []
+            for u in range(parts):
+                piece = keep.tile([P, PACK, width], F32, name=f"raw{a}{b}{u}")
+                c0 = b * KP + u * width
+                nc.sync.dma_start(
+                    out=piece[:],
+                    in_=w1[a * KP : (a + 1) * KP, c0 : c0 + width].rearrange("(p j) c -> p j c", j=PACK),
+                )
+                raw[a, b].append(piece)
+
+        nc.sync.dma_start(offs_sb[:], offs)
+        load_tab(0)
+        load_w1(0, 0, 1)
+        for q in range(QUADS):
+            nc.sync.dma_start(
+                out=tab_sc[32 * q : 32 * q + 4 * K_PASSES, :].bitcast(I32),
+                in_=tab_scales[:, 4 * q : 4 * q + 4, :].bitcast(I32),
+            )
+        loss_sb = keep.tile([P, R_PASSES, PACK], F32, name="loss_sb")
+        nc.sync.dma_start(out=loss_sb[:], in_=lossw.rearrange("(b p t) -> p b t", p=P, t=PACK))
+        load_tab(1)
+        load_tab(2)
+        load_w1(1, 0, 1)
+        load_w1(2, 0, 2)
+        nc.sync.dma_start(pos1_sb[:], pos1)
+        nc.sync.dma_start(pos2_sb[:], pos2)
+        w4_raw = keep.tile([P, R_PASSES * H // 2], I32, name="w4_raw", align_bytes=64)
+        nc.sync.dma_start(
+            out=w4_raw[:].rearrange("p (a n) -> p a n", a=R_PASSES),
+            in_=w4_words.bitcast(I32).rearrange("a p n -> p a n"),
+        )
+        load_w1(0, 1, 1)
+        load_w1(1, 1, 1)
+        load_w1(2, 1, 2)
+
+        v_words = [keep.tile([P, S], U32, name=f"v_words{a}", align_bytes=64) for a in range(K_PASSES)]
+        v_sc = keep.tile([P, S], U8, name="v_sc", align_bytes=64)
+
+        def gather_words(a):
+            nc.vector.tensor_copy(v_words[a][:], tab_sb[a][:].bitcast(U32).indirect(offs_sb[:]))
+
+        w1_q = {}
+
+        def round_w1(a, b, engines):
+            grouped = ring.tile([P, KP * PACK], BF16, name="w1_grouped", align_bytes=64)
+            by_slot = grouped[:].rearrange("p (t m j) -> p m j t", t=PACK, j=PACK)
+            rows = P // len(raw[a, b])
+            for u, piece in enumerate(raw[a, b]):
+                src = piece[:].rearrange("p j (m t) -> p m j t", t=PACK)
+                dst = by_slot[:, u * rows : (u + 1) * rows]
+                if engines[u] == "scalar":
+                    nc.scalar.copy(out=dst, in_=src)
+                else:
+                    nc.vector.tensor_copy(out=dst, in_=src)
+            codes = keep.tile([P, KP], U32, name=f"w1_codes{a}{b}", align_bytes=64)
+            scales = keep.tile([P, KP], U8, name=f"w1_scales{a}{b}", align_bytes=64)
+            nc.vector.quantize_mx(out=codes[:].bitcast(FP8X4), scales=scales[:], in_=grouped[:])
+            w1_q[a, b] = (codes, scales)
+
+        h_acc = {}
+
+        def h_pass(a, b, t):
+            codes, scales = w1_q[a, b]
+            for half in range(S // BANK):
+                if a == 0:
+                    h_acc[b, t, half] = psum.tile([P, BANK], F32, name="acc")
+                cols = slice(half * BANK, (half + 1) * BANK)
+                nc.tensor.matmul_mx(
+                    out=h_acc[b, t, half][:],
+                    lhsT=codes[:, t * P : (t + 1) * P].bitcast(FP8X4),
+                    lhsT_scale=scales[:, t * P : (t + 1) * P],
+                    rhs=v_words[a][:, cols].bitcast(FP8X4),
+                    rhs_scale=v_sc[4 * a : P, cols],
+                    start=(a == 0),
+                    stop=(a == K_PASSES - 1),
+                )
+
+        h_sb = {}
+
+        def h_out(b, t, engines):
+            h_sb[b, t] = keep.tile([P, S], F32, name=f"h_sb{b}{t}")
+            for half in range(S // BANK):
+                dst = h_sb[b, t][:, half * BANK : (half + 1) * BANK]
+                if engines[half] == "scalar":
+                    nc.scalar.copy(out=dst, in_=h_acc[b, t, half][:])
+                else:
+                    nc.vector.tensor_copy(out=dst, in_=h_acc[b, t, half][:])
+
+        x_f32 = [keep.tile([P, PACK, M], F32, name=f"x_f32{b}") for b in range(R_PASSES)]
+
+        def pick_x(b, t):
+            nc.vector.tensor_tensor(x_f32[b][:, t, :], h_sb[b, t][:].indirect(pos1_sb[:]), neg_loss[b][:, t, :], ALU.mult)
+
+        picked = {}
+
+        def pick_h(b, t, dst):
+            picked[b, t] = dst
+            nc.vector.tensor_copy(dst, h_sb[b, t][:].indirect(pos2_sb[:]))
+
+        def tanh_squared(b, t):
+            dst = picked[b, t]
+            nc.scalar.activation(out=dst, in_=dst, func=ACT.Tanh, scale=d_sb[:, b, t : t + 1])
+            nc.scalar.activation(out=dst, in_=dst, func=ACT.Square)
+
+        x_q = {}
+
+        def round_x(b, engine):
+            grouped = keep.tile([P, M * PACK], BF16, name=f"x_grouped{b}", tag=f"xg{b}", align_bytes=64)
+            dst = grouped[:].rearrange("p (c i t) -> p c t i", i=4, t=PACK)
+            src = x_f32[b][:].rearrange("p t (c i) -> p c t i", i=4)
+            if engine == "scalar":
+                nc.scalar.copy(out=dst, in_=src)
+            else:
+                nc.vector.tensor_copy(out=dst, in_=src)
+            return grouped
+
+        def quantize_x(b, grouped):
+            codes = keep.tile([P, M], U32, name=f"x_codes{b}", align_bytes=64)
+            scales = keep.tile([P, M], U8, name=f"x_scales{b}", align_bytes=64)
+            nc.vector.quantize_mx(out=codes[:].bitcast(FP8X4), scales=scales[:], in_=grouped[:])
+            x_q[b] = (codes, scales)
+
+        w4_sb = keep.tile([P, R_PASSES * H * 2], U8, name="w4_sb", align_bytes=64)
+        w4_sc = keep.tile([P, R_PASSES * H], U8, name="w4_sc", align_bytes=64)
+        y_acc = {}
+
+        def y_pass(a, b, t):
+            if a == 0:
+                y_acc[b, t] = psum.tile([P, M], F32, name="acc")
+            c0 = a * H + (b * PACK + t) * P
+            codes, scales = x_q[a]
+            nc.tensor.matmul_mx(
+                out=y_acc[b, t][:],
+                lhsT=w4_sb[:, 2 * c0 : 2 * (c0 + P)].bitcast(FP4X4),
+                lhsT_scale=w4_sc[:, c0 : c0 + P],
+                rhs=codes[:].bitcast(FP8X4),
+                rhs_scale=scales[:],
+                start=(a == 0),
+                stop=(a == R_PASSES - 1),
+            )
+
+        out_rows = out.rearrange("(b p t) m -> b t p m", p=P, t=PACK)
+
+        def finish(b, t):
+            dst = picked[b, t]
+            nc.vector.scalar_tensor_tensor(
+                out=dst, in0=dst, scalar=1.0, in1=y_acc[b, t][:], op0=ALU.subtract, op1=ALU.mult
+            )
+            nc.sync.dma_start(out=out_rows[b, t], in_=dst)
+
+        gather_words(0)
+        nc.vector.tensor_copy(v_sc[:], tab_sc[:].indirect(offs_sb[:]))
+        round_w1(0, 0, ["scalar"])
+        neg_loss = []
+        for b in range(R_PASSES):
+            tile = keep.tile([P, PACK, M], F32, name=f"neg_loss{b}", tag=f"slot{b}", align_bytes=64)
+            for t in range(PACK):
+                nc.scalar.activation(
+                    out=tile[:, t, :], in_=loss_sb[:, b, t : t + 1].to_broadcast([P, M]), func=ACT.Copy, scale=-1.0
+                )
+            neg_loss.append(tile)
+
+        gather_words(1)
+        gather_words(2)
+        for g in range(R_PASSES * R_PASSES):
+            nc.gpsimd.tensor_copy(
+                out=w4_sc[:, g * KP : (g + 1) * KP].rearrange("p (t m) -> p t m", t=PACK),
+                in_=w4_sc_raw[:, g * KP : (g + 1) * KP].rearrange("p (m t) -> p t m", t=PACK),
+            )
+        for t in range(PACK):
+            h_pass(0, 0, t)
+        round_w1(1, 0, ["scalar"])
+        for t in range(PACK):
+            h_pass(1, 0, t)
+        round_w1(2, 0, ["vector", "vector"])
+        for t in range(PACK):
+            h_pass(2, 0, t)
+        nc.vector.tensor_copy(
+            out=w4_sb[:].bitcast(U16).rearrange("p (g t m) -> p g t m", t=PACK, m=P),
+            in_=w4_raw[:].bitcast(U16).rearrange("p (g m t) -> p g t m", t=PACK, m=P),
+        )
+        picked0 = keep.tile([P, PACK, M], F32, name="picked0")
+        for t in range(PACK):
+            h_out(0, t, ["vector", "scalar"] if t == 0 else ["scalar", "scalar"])
+            pick_x(0, t)
+            pick_h(0, t, picked0[:, t, :])
+            if t >= 1:
+                a = t - 1
+                round_w1(a, 1, ["scalar", "vector"] if a == K_PASSES - 1 else ["scalar"])
+                for u in range(PACK):
+                    h_pass(a, 1, u)
+        quantize_x(0, round_x(0, "vector"))
+
+        for t in range(PACK):
+            h_out(1, t, ["scalar", "scalar"])
+            pick_x(1, t)
+        for b in range(R_PASSES):
+            for t in range(PACK):
+                y_pass(0, b, t)
+        grouped = round_x(1, "scalar")
+        early = keep.tile([P, 2, M], F32, name="picked_early", tag="slot1", align_bytes=64)
+        for t in range(2):
+            pick_h(1, t, early[:, t, :])
+        quantize_x(1, grouped)
+        late = keep.tile([P, 2, M], F32, name="picked_late", tag="xg1", align_bytes=64)
+        for t in range(2, PACK):
+            pick_h(1, t, late[:, t - 2, :])
+        for b in range(R_PASSES):
+            for t in range(PACK):
+                y_pass(1, b, t)
+        for b in range(R_PASSES):
+            for t in range(PACK):
+                tanh_squared(b, t)
+                finish(b, t)

@@ -31,26 +31,20 @@ def tile_list_glockenspiel_backward_sweep_kernel(
     nc = tc.nc
     with ExitStack() as ctx:
         keep = ctx.enter_context(tc.tile_pool(name="keep", bufs=1))
-        ring = ctx.enter_context(tc.tile_pool(name="ring", bufs=3))
         psum = ctx.enter_context(tc.psum_pool(name="psum", bufs=8))
 
         offs_sb = keep.tile([P, S // 16], U16, name="offs_sb")
         pos1_sb = keep.tile([P, M // 16], U16, name="pos1_sb")
         pos2_sb = keep.tile([P, M // 16], U16, name="pos2_sb")
 
+        loss_sb = keep.tile([P, R_PASSES, PACK], F32, name="loss_sb")
+        nc.scalar.dma_start(out=loss_sb[:], in_=lossw.rearrange("(b p t) -> p b t", p=P, t=PACK))
         tab_sc = keep.tile([P, T], U8, name="tab_sc", align_bytes=64)
         nc.vector.memset(tab_sc[:].bitcast(I32), 0)
         w4_sc_raw = keep.tile([P, R_PASSES * H], U8, name="w4_sc_raw", align_bytes=64)
-        nc.gpsimd.memset(w4_sc_raw[:].bitcast(I32), 0)
-        for q in range(QUADS):
-            nc.gpsimd.dma_start(
-                out=w4_sc_raw[32 * q : 32 * q + 4, :].bitcast(I32).rearrange("r (a n) -> r a n", a=R_PASSES),
-                in_=w4_scales[:, 4 * q : 4 * q + 4, :].bitcast(I32).rearrange("a r n -> r a n"),
-            )
-        d_sb = keep.tile([P, R_PASSES, PACK], F32, name="d_sb")
-        nc.gpsimd.dma_start(out=d_sb[:], in_=d.rearrange("(b p t) -> p b t", p=P, t=PACK))
+        nc.vector.memset(w4_sc_raw[:].bitcast(I32), 0)
 
-        tab_sb = [keep.tile([P, T], I32, name=f"tab_sb{a}") for a in range(K_PASSES)]
+        tab_sb = [keep.tile([P, T], I32, name=f"tab_sb{a}", tag=f"tab{a}", align_bytes=64) for a in range(K_PASSES)]
         raw = {}
 
         def load_tab(a):
@@ -60,7 +54,7 @@ def tile_list_glockenspiel_backward_sweep_kernel(
             width = KP // parts
             raw[a, b] = []
             for u in range(parts):
-                piece = keep.tile([P, PACK, width], F32, name=f"raw{a}{b}{u}")
+                piece = keep.tile([P, PACK, width], F32, name=f"raw{a}{b}{u}", tag=f"raw{a}{b}{u}")
                 c0 = b * KP + u * width
                 nc.sync.dma_start(
                     out=piece[:],
@@ -76,11 +70,14 @@ def tile_list_glockenspiel_backward_sweep_kernel(
                 out=tab_sc[32 * q : 32 * q + 4 * K_PASSES, :].bitcast(I32),
                 in_=tab_scales[:, 4 * q : 4 * q + 4, :].bitcast(I32),
             )
-        loss_sb = keep.tile([P, R_PASSES, PACK], F32, name="loss_sb")
-        nc.sync.dma_start(out=loss_sb[:], in_=lossw.rearrange("(b p t) -> p b t", p=P, t=PACK))
         load_tab(1)
-        load_tab(2)
         load_w1(1, 0, 1)
+        for q in range(QUADS):
+            nc.sync.dma_start(
+                out=w4_sc_raw[32 * q : 32 * q + 4, :].bitcast(I32).rearrange("r (a n) -> r a n", a=R_PASSES),
+                in_=w4_scales[:, 4 * q : 4 * q + 4, :].bitcast(I32).rearrange("a r n -> r a n"),
+            )
+        load_tab(2)
         load_w1(2, 0, 2)
         nc.sync.dma_start(pos1_sb[:], pos1)
         nc.sync.dma_start(pos2_sb[:], pos2)
@@ -91,30 +88,50 @@ def tile_list_glockenspiel_backward_sweep_kernel(
         )
         load_w1(0, 1, 1)
         load_w1(1, 1, 1)
-        load_w1(2, 1, 2)
+        load_w1(2, 1, 1)
+        d_sb = keep.tile([P, R_PASSES, PACK], F32, name="d_sb")
+        nc.sync.dma_start(out=d_sb[:], in_=d.rearrange("(b p t) -> p b t", p=P, t=PACK))
 
-        v_words = [keep.tile([P, S], U32, name=f"v_words{a}", align_bytes=64) for a in range(K_PASSES)]
+
+        neg_loss = {}
+        for b in range(R_PASSES):
+            for t in range(PACK):
+                neg_loss[b, t] = keep.tile([P, M], F32, name=f"neg_loss{b}{t}", tag=f"loss{b}{t}", align_bytes=64)
+                nc.scalar.activation(
+                    out=neg_loss[b, t][:], in_=loss_sb[:, b, t : t + 1].to_broadcast([P, M]), func=ACT.Copy, scale=-1.0
+                )
+
+        v_words = {}
         v_sc = keep.tile([P, S], U8, name="v_sc", align_bytes=64)
 
-        def gather_words(a):
+        def gather_words(a, tag):
+            v_words[a] = keep.tile([P, S], U32, name=f"v_words{a}", tag=tag, align_bytes=64)
             nc.vector.tensor_copy(v_words[a][:], tab_sb[a][:].bitcast(U32).indirect(offs_sb[:]))
 
         w1_q = {}
 
-        def round_w1(a, b, engines):
-            grouped = ring.tile([P, KP * PACK], BF16, name="w1_grouped", align_bytes=64)
-            by_slot = grouped[:].rearrange("p (t m j) -> p m j t", t=PACK, j=PACK)
+        def round_w1(a, b, engines, tag):
+            grouped = keep.tile([P, KP * PACK], BF16, name=f"w1_grouped{a}{b}", tag=tag, align_bytes=64)
+            by_slot = grouped[:].rearrange("p (s e m j) -> p s m j e", s=2, e=2, j=PACK)
             rows = P // len(raw[a, b])
             for u, piece in enumerate(raw[a, b]):
-                src = piece[:].rearrange("p j (m t) -> p m j t", t=PACK)
-                dst = by_slot[:, u * rows : (u + 1) * rows]
+                src = piece[:].rearrange("p j (m s e) -> p s m j e", s=2, e=2)
+                dst = by_slot[:, :, u * rows : (u + 1) * rows]
                 if engines[u] == "scalar":
                     nc.scalar.copy(out=dst, in_=src)
                 else:
                     nc.vector.tensor_copy(out=dst, in_=src)
             codes = keep.tile([P, KP], U32, name=f"w1_codes{a}{b}", align_bytes=64)
             scales = keep.tile([P, KP], U8, name=f"w1_scales{a}{b}", align_bytes=64)
-            nc.vector.quantize_mx(out=codes[:].bitcast(FP8X4), scales=scales[:], in_=grouped[:])
+            calls = PACK if a == K_PASSES - 1 else 1
+            width = KP // calls
+            for u in range(calls):
+                cols = slice(u * width, (u + 1) * width)
+                nc.vector.quantize_mx(
+                    out=codes[:, cols].bitcast(FP8X4),
+                    scales=scales[:, cols],
+                    in_=grouped[:, PACK * u * width : PACK * (u + 1) * width],
+                )
             w1_q[a, b] = (codes, scales)
 
         h_acc = {}
@@ -137,8 +154,8 @@ def tile_list_glockenspiel_backward_sweep_kernel(
 
         h_sb = {}
 
-        def h_out(b, t, engines):
-            h_sb[b, t] = keep.tile([P, S], F32, name=f"h_sb{b}{t}")
+        def h_out(b, t, engines, tag):
+            h_sb[b, t] = keep.tile([P, S], F32, name=f"h_sb{b}{t}", tag=tag)
             for half in range(S // BANK):
                 dst = h_sb[b, t][:, half * BANK : (half + 1) * BANK]
                 if engines[half] == "scalar":
@@ -149,7 +166,7 @@ def tile_list_glockenspiel_backward_sweep_kernel(
         x_f32 = [keep.tile([P, PACK, M], F32, name=f"x_f32{b}") for b in range(R_PASSES)]
 
         def pick_x(b, t):
-            nc.vector.tensor_tensor(x_f32[b][:, t, :], h_sb[b, t][:].indirect(pos1_sb[:]), neg_loss[b][:, t, :], ALU.mult)
+            nc.vector.tensor_tensor(x_f32[b][:, t, :], h_sb[b, t][:].indirect(pos1_sb[:]), neg_loss[b, t][:], ALU.mult)
 
         picked = {}
 
@@ -180,8 +197,6 @@ def tile_list_glockenspiel_backward_sweep_kernel(
             nc.vector.quantize_mx(out=codes[:].bitcast(FP8X4), scales=scales[:], in_=grouped[:])
             x_q[b] = (codes, scales)
 
-        w4_sb = keep.tile([P, R_PASSES * H * 2], U8, name="w4_sb", align_bytes=64)
-        w4_sc = keep.tile([P, R_PASSES * H], U8, name="w4_sc", align_bytes=64)
         y_acc = {}
 
         def y_pass(a, b, t):
@@ -208,67 +223,54 @@ def tile_list_glockenspiel_backward_sweep_kernel(
             )
             nc.sync.dma_start(out=out_rows[b, t], in_=dst)
 
-        gather_words(0)
+        gather_words(0, "v0")
         nc.vector.tensor_copy(v_sc[:], tab_sc[:].indirect(offs_sb[:]))
-        round_w1(0, 0, ["scalar"])
-        neg_loss = []
-        for b in range(R_PASSES):
-            tile = keep.tile([P, PACK, M], F32, name=f"neg_loss{b}", tag=f"slot{b}", align_bytes=64)
+        for a in range(K_PASSES):
+            round_w1(a, 0, ["scalar", "scalar"], f"v{a + 1}")
             for t in range(PACK):
-                nc.scalar.activation(
-                    out=tile[:, t, :], in_=loss_sb[:, b, t : t + 1].to_broadcast([P, M]), func=ACT.Copy, scale=-1.0
-                )
-            neg_loss.append(tile)
-
-        gather_words(1)
-        gather_words(2)
-        for g in range(R_PASSES * R_PASSES):
-            nc.gpsimd.tensor_copy(
-                out=w4_sc[:, g * KP : (g + 1) * KP].rearrange("p (t m) -> p t m", t=PACK),
-                in_=w4_sc_raw[:, g * KP : (g + 1) * KP].rearrange("p (m t) -> p t m", t=PACK),
-            )
-        for t in range(PACK):
-            h_pass(0, 0, t)
-        round_w1(1, 0, ["scalar"])
-        for t in range(PACK):
-            h_pass(1, 0, t)
-        round_w1(2, 0, ["vector", "vector"])
-        for t in range(PACK):
-            h_pass(2, 0, t)
+                h_pass(a, 0, t)
+            if a + 1 < K_PASSES:
+                gather_words(a + 1, f"v{a + 1}")
+        w4_sc = keep.tile([P, R_PASSES * H], U8, name="w4_sc", tag="tab1", align_bytes=64)
+        nc.vector.tensor_copy(
+            out=w4_sc[:].rearrange("p (g t m) -> p g t m", t=PACK, m=P),
+            in_=w4_sc_raw[:].rearrange("p (g m t) -> p g t m", t=PACK, m=P),
+        )
+        w4_sb = keep.tile([P, R_PASSES * H * 2], U8, name="w4_sb", tag="v3", align_bytes=64)
         nc.vector.tensor_copy(
             out=w4_sb[:].bitcast(U16).rearrange("p (g t m) -> p g t m", t=PACK, m=P),
             in_=w4_raw[:].bitcast(U16).rearrange("p (g m t) -> p g t m", t=PACK, m=P),
         )
         picked0 = keep.tile([P, PACK, M], F32, name="picked0")
         for t in range(PACK):
-            h_out(0, t, ["vector", "scalar"] if t == 0 else ["scalar", "scalar"])
+            h_out(0, t, ["scalar", "scalar"], f"raw{t - 2}10" if t >= 2 else f"h0{t}")
             pick_x(0, t)
             pick_h(0, t, picked0[:, t, :])
             if t >= 1:
                 a = t - 1
-                round_w1(a, 1, ["scalar", "vector"] if a == K_PASSES - 1 else ["scalar"])
+                round_w1(a, 1, ["scalar"], f"loss0{a}")
                 for u in range(PACK):
                     h_pass(a, 1, u)
         quantize_x(0, round_x(0, "vector"))
 
         for t in range(PACK):
-            h_out(1, t, ["scalar", "scalar"])
+            h_out(1, t, ["scalar", "scalar"], f"h1{t}")
             pick_x(1, t)
         for b in range(R_PASSES):
             for t in range(PACK):
                 y_pass(0, b, t)
         grouped = round_x(1, "scalar")
-        early = keep.tile([P, 2, M], F32, name="picked_early", tag="slot1", align_bytes=64)
-        for t in range(2):
-            pick_h(1, t, early[:, t, :])
+        first = keep.tile([P, M], F32, name="picked_first")
+        pick_h(1, 3, first[:])
+        middle = keep.tile([P, 2, M], F32, name="picked_middle", tag="h13")
+        pick_h(1, 2, middle[:, 0, :])
+        pick_h(1, 1, middle[:, 1, :])
         quantize_x(1, grouped)
-        late = keep.tile([P, 2, M], F32, name="picked_late", tag="xg1", align_bytes=64)
-        for t in range(2, PACK):
-            pick_h(1, t, late[:, t - 2, :])
-        for b in range(R_PASSES):
-            for t in range(PACK):
-                y_pass(1, b, t)
-        for b in range(R_PASSES):
-            for t in range(PACK):
-                tanh_squared(b, t)
-                finish(b, t)
+        last = keep.tile([P, M], F32, name="picked_last", tag="xg1", align_bytes=64)
+        pick_h(1, 0, last[:])
+        order = [(0, t) for t in range(PACK)] + [(1, t) for t in reversed(range(PACK))]
+        for b, t in order:
+            y_pass(1, b, t)
+        for b, t in order:
+            tanh_squared(b, t)
+            finish(b, t)

@@ -1,6 +1,7 @@
 from contextlib import ExitStack
 
 import concourse.mybir as mybir
+from concourse.masks import make_identity
 
 K, H, T, S, M = 1536, 1024, 2048, 1024, 512
 FLOPS = 2 * K * H * S + 2 * H * H * M
@@ -18,11 +19,20 @@ ALU = mybir.AluOpType
 
 P = 128
 PACK = 4
-KP = P * PACK
-K_PASSES = K // KP
-R_PASSES = H // KP
+PASS = P * PACK
+K_PASSES = K // PASS
+R_PASSES = H // PASS
 BANK = 512
-QUADS = 4
+BANKS = 8
+QUADRANT = 32
+SCALE_ROWS = 4
+LIST_GROUP = 16
+RUN = 4
+TILES = H // P
+TILES_PER_PASS = PASS // P
+TILES_PER_CHUNK = 2
+CHUNK = TILES_PER_CHUNK * P
+CHUNKS = H // CHUNK
 
 
 def tile_list_glockenspiel_backward_sweep_kernel(
@@ -31,246 +41,196 @@ def tile_list_glockenspiel_backward_sweep_kernel(
     nc = tc.nc
     with ExitStack() as ctx:
         keep = ctx.enter_context(tc.tile_pool(name="keep", bufs=1))
-        psum = ctx.enter_context(tc.psum_pool(name="psum", bufs=8))
+        psum = ctx.enter_context(tc.psum_pool(name="psum", bufs=BANKS))
 
-        offs_sb = keep.tile([P, S // 16], U16, name="offs_sb")
-        pos1_sb = keep.tile([P, M // 16], U16, name="pos1_sb")
-        pos2_sb = keep.tile([P, M // 16], U16, name="pos2_sb")
+        def sbuf(name, shape, dtype, after=None):
+            return keep.tile(shape, dtype, name=name, tag=after or name, align_bytes=64)
 
-        loss_sb = keep.tile([P, R_PASSES, PACK], F32, name="loss_sb")
-        nc.scalar.dma_start(out=loss_sb[:], in_=lossw.rearrange("(b p t) -> p b t", p=P, t=PACK))
-        tab_sc = keep.tile([P, T], U8, name="tab_sc", align_bytes=64)
+        offs_sb = keep.tile([P, S // LIST_GROUP], U16, name="offs_sb")
+        pos1_sb = keep.tile([P, M // LIST_GROUP], U16, name="pos1_sb")
+        pos2_sb = keep.tile([P, M // LIST_GROUP], U16, name="pos2_sb")
+
+        rows = sbuf("rows", [P, P], F32)
+        nc.gpsimd.memset(rows[:], 0.0)
+        nc.gpsimd.dma_start(out=rows[0:TILES, :], in_=lossw.rearrange("(n p) -> n p", p=P))
+        nc.gpsimd.dma_start(out=rows[TILES : 2 * TILES, :], in_=d.rearrange("(n p) -> n p", p=P))
+        identity = sbuf("identity", [P, P], F32)
+        make_identity(nc, identity[:])
+        turned = psum.tile([P, BANK], F32, name="acc")
+        nc.tensor.transpose(turned[:, 0:P], rows[:], identity[:])
+        factors = sbuf("factors", [P, 2 * TILES], F32)
+        nc.scalar.copy(out=factors[:], in_=turned[:, 0 : 2 * TILES])
+
+        tab_sc = sbuf("tab_sc", [P, T], U8)
         nc.vector.memset(tab_sc[:].bitcast(I32), 0)
-        w4_sc_raw = keep.tile([P, R_PASSES * H], U8, name="w4_sc_raw", align_bytes=64)
-        nc.vector.memset(w4_sc_raw[:].bitcast(I32), 0)
+        w4_sc = sbuf("w4_sc", [P, R_PASSES * H], U8)
+        nc.vector.memset(w4_sc[:].bitcast(I32), 0)
 
-        tab_sb = [keep.tile([P, T], I32, name=f"tab_sb{a}", tag=f"tab{a}", align_bytes=64) for a in range(K_PASSES)]
-        raw = {}
+        tab_sb = [sbuf(f"tab{a}", [P, T], I32) for a in range(K_PASSES)]
+        w1_raw = {}
 
-        def load_tab(a):
-            nc.sync.dma_start(out=tab_sb[a][:], in_=tab_words[a].rearrange("p t i -> p (t i)").bitcast(I32))
-
-        def load_w1(a, b, parts):
-            width = KP // parts
-            raw[a, b] = []
-            for u in range(parts):
-                piece = keep.tile([P, PACK, width], F32, name=f"raw{a}{b}{u}", tag=f"raw{a}{b}{u}")
-                c0 = b * KP + u * width
-                nc.sync.dma_start(
-                    out=piece[:],
-                    in_=w1[a * KP : (a + 1) * KP, c0 : c0 + width].rearrange("(p j) c -> p j c", j=PACK),
-                )
-                raw[a, b].append(piece)
+        def load_w1(a, c):
+            w1_raw[a, c] = sbuf(f"raw{a}{c}", [P, PACK, CHUNK], F32)
+            piece = w1[a * PASS : (a + 1) * PASS, c * CHUNK : (c + 1) * CHUNK]
+            nc.sync.dma_start(out=w1_raw[a, c][:], in_=piece.rearrange("(p j) c -> p j c", j=PACK))
 
         nc.sync.dma_start(offs_sb[:], offs)
-        load_tab(0)
-        load_w1(0, 0, 1)
-        for q in range(QUADS):
-            nc.sync.dma_start(
-                out=tab_sc[32 * q : 32 * q + 4 * K_PASSES, :].bitcast(I32),
-                in_=tab_scales[:, 4 * q : 4 * q + 4, :].bitcast(I32),
-            )
-        load_tab(1)
-        load_w1(1, 0, 1)
-        for q in range(QUADS):
-            nc.sync.dma_start(
-                out=w4_sc_raw[32 * q : 32 * q + 4, :].bitcast(I32).rearrange("r (a n) -> r a n", a=R_PASSES),
-                in_=w4_scales[:, 4 * q : 4 * q + 4, :].bitcast(I32).rearrange("a r n -> r a n"),
-            )
-        load_tab(2)
-        load_w1(2, 0, 2)
+        for a in range(K_PASSES):
+            nc.sync.dma_start(out=tab_sb[a][:], in_=tab_words[a].rearrange("p t i -> p (t i)").bitcast(I32))
+            load_w1(a, 0)
+            if a == 0:
+                for q in range(P // QUADRANT):
+                    nc.sync.dma_start(
+                        out=tab_sc[QUADRANT * q : QUADRANT * q + SCALE_ROWS * K_PASSES, :].bitcast(I32),
+                        in_=tab_scales[:, SCALE_ROWS * q : SCALE_ROWS * (q + 1), :].bitcast(I32),
+                    )
         nc.sync.dma_start(pos1_sb[:], pos1)
         nc.sync.dma_start(pos2_sb[:], pos2)
-        w4_raw = keep.tile([P, R_PASSES * H // 2], I32, name="w4_raw", align_bytes=64)
+        for c in range(1, CHUNKS):
+            for a in range(K_PASSES):
+                load_w1(a, c)
+        w4_sb = sbuf("w4_sb", [P, R_PASSES * H * 2], U8)
         nc.sync.dma_start(
-            out=w4_raw[:].rearrange("p (a n) -> p a n", a=R_PASSES),
+            out=w4_sb[:].bitcast(I32).rearrange("p (a n) -> p a n", a=R_PASSES),
             in_=w4_words.bitcast(I32).rearrange("a p n -> p a n"),
         )
-        load_w1(0, 1, 1)
-        load_w1(1, 1, 1)
-        load_w1(2, 1, 1)
-        d_sb = keep.tile([P, R_PASSES, PACK], F32, name="d_sb")
-        nc.sync.dma_start(out=d_sb[:], in_=d.rearrange("(b p t) -> p b t", p=P, t=PACK))
+        for q in range(P // QUADRANT):
+            nc.sync.dma_start(
+                out=w4_sc[QUADRANT * q : QUADRANT * q + SCALE_ROWS, :]
+                .bitcast(I32)
+                .rearrange("s (a n) -> s a n", a=R_PASSES),
+                in_=w4_scales[:, SCALE_ROWS * q : SCALE_ROWS * (q + 1), :].bitcast(I32).rearrange("a s n -> s a n"),
+            )
 
+        def round_into_words(copy, grouped, planes):
+            copy(
+                out=grouped[:].rearrange("p (g i j) -> p g j i", i=RUN, j=PACK),
+                in_=planes[:].rearrange("p j (g i) -> p g j i", i=RUN),
+            )
 
-        neg_loss = {}
-        for b in range(R_PASSES):
-            for t in range(PACK):
-                neg_loss[b, t] = keep.tile([P, M], F32, name=f"neg_loss{b}{t}", tag=f"loss{b}{t}", align_bytes=64)
-                nc.scalar.activation(
-                    out=neg_loss[b, t][:], in_=loss_sb[:, b, t : t + 1].to_broadcast([P, M]), func=ACT.Copy, scale=-1.0
-                )
+        def quantize(name, grouped, columns):
+            codes = sbuf(f"{name}_codes", [P, columns], U32)
+            scales = sbuf(f"{name}_scales", [P, columns], U8)
+            nc.vector.quantize_mx(out=codes[:].bitcast(FP8X4), scales=scales[:], in_=grouped[:])
+            return codes, scales
 
         v_words = {}
-        v_sc = keep.tile([P, S], U8, name="v_sc", align_bytes=64)
+        v_sc = sbuf("v_sc", [P, S], U8)
 
-        def gather_words(a, tag):
-            v_words[a] = keep.tile([P, S], U32, name=f"v_words{a}", tag=tag, align_bytes=64)
+        def gather_words(a, after):
+            v_words[a] = sbuf(f"v_words{a}", [P, S], U32, after)
             nc.vector.tensor_copy(v_words[a][:], tab_sb[a][:].bitcast(U32).indirect(offs_sb[:]))
-
-        w1_q = {}
-
-        def round_w1(a, b, engines, tag):
-            grouped = keep.tile([P, KP * PACK], BF16, name=f"w1_grouped{a}{b}", tag=tag, align_bytes=64)
-            by_slot = grouped[:].rearrange("p (s e m j) -> p s m j e", s=2, e=2, j=PACK)
-            rows = P // len(raw[a, b])
-            for u, piece in enumerate(raw[a, b]):
-                src = piece[:].rearrange("p j (m s e) -> p s m j e", s=2, e=2)
-                dst = by_slot[:, :, u * rows : (u + 1) * rows]
-                if engines[u] == "scalar":
-                    nc.scalar.copy(out=dst, in_=src)
-                else:
-                    nc.vector.tensor_copy(out=dst, in_=src)
-            codes = keep.tile([P, KP], U32, name=f"w1_codes{a}{b}", align_bytes=64)
-            scales = keep.tile([P, KP], U8, name=f"w1_scales{a}{b}", align_bytes=64)
-            calls = PACK if a == K_PASSES - 1 else 1
-            width = KP // calls
-            for u in range(calls):
-                cols = slice(u * width, (u + 1) * width)
-                nc.vector.quantize_mx(
-                    out=codes[:, cols].bitcast(FP8X4),
-                    scales=scales[:, cols],
-                    in_=grouped[:, PACK * u * width : PACK * (u + 1) * width],
-                )
-            w1_q[a, b] = (codes, scales)
 
         h_acc = {}
 
-        def h_pass(a, b, t):
-            codes, scales = w1_q[a, b]
-            for half in range(S // BANK):
-                if a == 0:
-                    h_acc[b, t, half] = psum.tile([P, BANK], F32, name="acc")
-                cols = slice(half * BANK, (half + 1) * BANK)
-                nc.tensor.matmul_mx(
-                    out=h_acc[b, t, half][:],
-                    lhsT=codes[:, t * P : (t + 1) * P].bitcast(FP8X4),
-                    lhsT_scale=scales[:, t * P : (t + 1) * P],
-                    rhs=v_words[a][:, cols].bitcast(FP8X4),
-                    rhs_scale=v_sc[4 * a : P, cols],
-                    start=(a == 0),
-                    stop=(a == K_PASSES - 1),
-                )
+        def h_pass(a, c, copy=nc.scalar.copy):
+            grouped = sbuf(f"grouped{a}{c}", [P, CHUNK * PACK], BF16)
+            round_into_words(copy, grouped, w1_raw[a, c])
+            codes, scales = quantize(f"w1_{a}{c}", grouped, CHUNK)
+            for u in range(TILES_PER_CHUNK):
+                n = c * TILES_PER_CHUNK + u
+                for half in range(S // BANK):
+                    if a == 0:
+                        h_acc[n, half] = psum.tile([P, BANK], F32, name="acc")
+                    cols = slice(half * BANK, (half + 1) * BANK)
+                    nc.tensor.matmul_mx(
+                        out=h_acc[n, half][:],
+                        lhsT=codes[:, u * P : (u + 1) * P].bitcast(FP8X4),
+                        lhsT_scale=scales[:, u * P : (u + 1) * P],
+                        rhs=v_words[a][:, cols].bitcast(FP8X4),
+                        rhs_scale=v_sc[SCALE_ROWS * a : P, cols],
+                        start=(a == 0),
+                        stop=(a == K_PASSES - 1),
+                    )
 
+        neg_loss = {}
         h_sb = {}
+        h_picked = {}
+        x_planes = [sbuf(f"x_planes{b}", [P, PACK, M], F32) for b in range(R_PASSES)]
 
-        def h_out(b, t, engines, tag):
-            h_sb[b, t] = keep.tile([P, S], F32, name=f"h_sb{b}{t}", tag=tag)
+        def pick_h(n, dst):
+            h_picked[n] = dst
+            nc.vector.tensor_copy(dst, h_sb[n][:].indirect(pos2_sb[:]))
+
+        def h_out(n, after=None):
+            h_sb[n] = sbuf(f"h_sb{n}", [P, S], F32, after)
             for half in range(S // BANK):
-                dst = h_sb[b, t][:, half * BANK : (half + 1) * BANK]
-                if engines[half] == "scalar":
-                    nc.scalar.copy(out=dst, in_=h_acc[b, t, half][:])
-                else:
-                    nc.vector.tensor_copy(out=dst, in_=h_acc[b, t, half][:])
-
-        x_f32 = [keep.tile([P, PACK, M], F32, name=f"x_f32{b}") for b in range(R_PASSES)]
-
-        def pick_x(b, t):
-            nc.vector.tensor_tensor(x_f32[b][:, t, :], h_sb[b, t][:].indirect(pos1_sb[:]), neg_loss[b, t][:], ALU.mult)
-
-        picked = {}
-
-        def pick_h(b, t, dst):
-            picked[b, t] = dst
-            nc.vector.tensor_copy(dst, h_sb[b, t][:].indirect(pos2_sb[:]))
-
-        def tanh_squared(b, t):
-            dst = picked[b, t]
-            nc.scalar.activation(out=dst, in_=dst, func=ACT.Tanh, scale=d_sb[:, b, t : t + 1])
-            nc.scalar.activation(out=dst, in_=dst, func=ACT.Square)
-
-        x_q = {}
-
-        def round_x(b, engine):
-            grouped = keep.tile([P, M * PACK], BF16, name=f"x_grouped{b}", tag=f"xg{b}", align_bytes=64)
-            dst = grouped[:].rearrange("p (c i t) -> p c t i", i=4, t=PACK)
-            src = x_f32[b][:].rearrange("p t (c i) -> p c t i", i=4)
-            if engine == "scalar":
-                nc.scalar.copy(out=dst, in_=src)
-            else:
-                nc.vector.tensor_copy(out=dst, in_=src)
-            return grouped
-
-        def quantize_x(b, grouped):
-            codes = keep.tile([P, M], U32, name=f"x_codes{b}", align_bytes=64)
-            scales = keep.tile([P, M], U8, name=f"x_scales{b}", align_bytes=64)
-            nc.vector.quantize_mx(out=codes[:].bitcast(FP8X4), scales=scales[:], in_=grouped[:])
-            x_q[b] = (codes, scales)
+                nc.scalar.copy(out=h_sb[n][:, half * BANK : (half + 1) * BANK], in_=h_acc[n, half][:])
+            b, q = divmod(n, TILES_PER_PASS)
+            x_rows = sbuf(f"x_rows{n}", [P, M], F32, f"x_rows{q}")
+            nc.vector.tensor_tensor(x_rows[:], h_sb[n][:].indirect(pos1_sb[:]), neg_loss[n][:], ALU.mult)
+            for i in range(PACK):
+                nc.sync.dma_start(out=x_planes[b][QUADRANT * q : QUADRANT * (q + 1), i, :], in_=x_rows[i:P:PACK, :])
+            if b == 0:
+                pick_h(n, picked_first[:, q, :])
 
         y_acc = {}
 
-        def y_pass(a, b, t):
-            if a == 0:
-                y_acc[b, t] = psum.tile([P, M], F32, name="acc")
-            c0 = a * H + (b * PACK + t) * P
-            codes, scales = x_q[a]
-            nc.tensor.matmul_mx(
-                out=y_acc[b, t][:],
-                lhsT=w4_sb[:, 2 * c0 : 2 * (c0 + P)].bitcast(FP4X4),
-                lhsT_scale=w4_sc[:, c0 : c0 + P],
-                rhs=codes[:].bitcast(FP8X4),
-                rhs_scale=scales[:],
-                start=(a == 0),
-                stop=(a == R_PASSES - 1),
-            )
+        def y_pass(b, codes, scales):
+            for n in range(TILES):
+                if b == 0:
+                    y_acc[n] = psum.tile([P, M], F32, name="acc")
+                first = b * H + n * P
+                nc.tensor.matmul_mx(
+                    out=y_acc[n][:],
+                    lhsT=w4_sb[:, 2 * first : 2 * (first + P)].bitcast(FP4X4),
+                    lhsT_scale=w4_sc[:, first : first + P],
+                    rhs=codes[:].bitcast(FP8X4),
+                    rhs_scale=scales[:],
+                    start=(b == 0),
+                    stop=(b == R_PASSES - 1),
+                )
 
-        out_rows = out.rearrange("(b p t) m -> b t p m", p=P, t=PACK)
-
-        def finish(b, t):
-            dst = picked[b, t]
-            nc.vector.scalar_tensor_tensor(
-                out=dst, in0=dst, scalar=1.0, in1=y_acc[b, t][:], op0=ALU.subtract, op1=ALU.mult
-            )
-            nc.sync.dma_start(out=out_rows[b, t], in_=dst)
-
-        gather_words(0, "v0")
+        gather_words(0, None)
         nc.vector.tensor_copy(v_sc[:], tab_sc[:].indirect(offs_sb[:]))
         for a in range(K_PASSES):
-            round_w1(a, 0, ["scalar", "scalar"], f"v{a + 1}")
-            for t in range(PACK):
-                h_pass(a, 0, t)
+            h_pass(a, 0)
             if a + 1 < K_PASSES:
-                gather_words(a + 1, f"v{a + 1}")
-        w4_sc = keep.tile([P, R_PASSES * H], U8, name="w4_sc", tag="tab1", align_bytes=64)
-        nc.vector.tensor_copy(
-            out=w4_sc[:].rearrange("p (g t m) -> p g t m", t=PACK, m=P),
-            in_=w4_sc_raw[:].rearrange("p (g m t) -> p g t m", t=PACK, m=P),
-        )
-        w4_sb = keep.tile([P, R_PASSES * H * 2], U8, name="w4_sb", tag="v3", align_bytes=64)
-        nc.vector.tensor_copy(
-            out=w4_sb[:].bitcast(U16).rearrange("p (g t m) -> p g t m", t=PACK, m=P),
-            in_=w4_raw[:].bitcast(U16).rearrange("p (g m t) -> p g t m", t=PACK, m=P),
-        )
-        picked0 = keep.tile([P, PACK, M], F32, name="picked0")
-        for t in range(PACK):
-            h_out(0, t, ["scalar", "scalar"], f"raw{t - 2}10" if t >= 2 else f"h0{t}")
-            pick_x(0, t)
-            pick_h(0, t, picked0[:, t, :])
-            if t >= 1:
-                a = t - 1
-                round_w1(a, 1, ["scalar"], f"loss0{a}")
-                for u in range(PACK):
-                    h_pass(a, 1, u)
-        quantize_x(0, round_x(0, "vector"))
+                gather_words(a + 1, f"grouped{a}0")
+        h_pass(0, 1)
+        h_pass(1, 1)
+        h_pass(2, 1, copy=nc.vector.tensor_copy)
+        for n in range(TILES):
+            neg_loss[n] = sbuf(f"neg_loss{n}", [P, M], F32)
+            nc.scalar.activation(
+                out=neg_loss[n][:], in_=factors[:, n : n + 1].to_broadcast([P, M]), func=ACT.Copy, scale=-1.0
+            )
 
-        for t in range(PACK):
-            h_out(1, t, ["scalar", "scalar"], f"h1{t}")
-            pick_x(1, t)
-        for b in range(R_PASSES):
-            for t in range(PACK):
-                y_pass(0, b, t)
-        grouped = round_x(1, "scalar")
-        first = keep.tile([P, M], F32, name="picked_first")
-        pick_h(1, 3, first[:])
-        middle = keep.tile([P, 2, M], F32, name="picked_middle", tag="h13")
-        pick_h(1, 2, middle[:, 0, :])
-        pick_h(1, 1, middle[:, 1, :])
-        quantize_x(1, grouped)
-        last = keep.tile([P, M], F32, name="picked_last", tag="xg1", align_bytes=64)
-        pick_h(1, 0, last[:])
-        order = [(0, t) for t in range(PACK)] + [(1, t) for t in reversed(range(PACK))]
-        for b, t in order:
-            y_pass(1, b, t)
-        for b, t in order:
-            tanh_squared(b, t)
-            finish(b, t)
+        picked_first = sbuf("picked_first", [P, TILES_PER_PASS, M], F32)
+        last_rounded = "raw11"
+        for c in range(2, CHUNKS):
+            n = (c - 2) * TILES_PER_CHUNK
+            h_out(n, last_rounded)
+            h_pass(0, c)
+            h_pass(1, c)
+            h_out(n + 1, f"raw1{c}")
+            h_pass(2, c)
+            last_rounded = f"raw2{c}"
+        h_out(TILES_PER_PASS, last_rounded)
+        for n in range(TILES_PER_PASS + 1, TILES):
+            h_out(n)
+
+        x_grouped = [
+            sbuf("x_grouped0", [P, M * PACK], BF16, f"neg_loss{TILES - 1}"),
+            sbuf("x_grouped1", [P, M * PACK], BF16),
+        ]
+        round_into_words(nc.vector.tensor_copy, x_grouped[0], x_planes[0])
+        round_into_words(nc.scalar.copy, x_grouped[1], x_planes[1])
+        picked_second = sbuf("picked_second", [P, TILES_PER_PASS, M], F32, "x_planes0")
+        pick_h(TILES_PER_PASS, picked_second[:, 0, :])
+        y_pass(0, *quantize("x0", x_grouped[0], M))
+        for q in range(1, TILES_PER_PASS):
+            pick_h(TILES_PER_PASS + q, picked_second[:, q, :])
+        y_pass(1, *quantize("x1", x_grouped[1], M))
+
+        result_second = sbuf("result_second", [P, TILES_PER_PASS, M], F32, "x_planes1")
+        result_first = sbuf("result_first", [P, TILES_PER_PASS, M], F32, f"neg_loss{TILES_PER_PASS}")
+        for n in range(TILES):
+            b, q = divmod(n, TILES_PER_PASS)
+            result = (result_first, result_second)[b][:, q, :]
+            nc.scalar.activation(out=result, in_=h_picked[n], func=ACT.Tanh, scale=factors[:, TILES + n : TILES + n + 1])
+            nc.scalar.activation(out=result, in_=result, func=ACT.Square)
+            nc.vector.scalar_tensor_tensor(
+                out=result, in0=result, scalar=1.0, in1=y_acc[n][:], op0=ALU.subtract, op1=ALU.mult
+            )
+            nc.sync.dma_start(out=out[n * P : (n + 1) * P, :], in_=result)

@@ -41,28 +41,22 @@ def tile_list_glockenspiel_backward_sweep_kernel(
     nc = tc.nc
     with ExitStack() as ctx:
         keep = ctx.enter_context(tc.tile_pool(name="keep", bufs=1))
-        psum = ctx.enter_context(tc.psum_pool(name="psum", bufs=BANKS))
+        psum = ctx.enter_context(tc.psum_pool(name="psum", bufs=1))
 
         def sbuf(name, shape, dtype, after=None):
             return keep.tile(shape, dtype, name=name, tag=after or name, align_bytes=64)
+
+        def bank(index):
+            return psum.tile([P, BANK], F32, name=f"bank{index}", tag=f"bank{index}")
 
         offs_sb = keep.tile([P, S // LIST_GROUP], U16, name="offs_sb")
         pos1_sb = keep.tile([P, M // LIST_GROUP], U16, name="pos1_sb")
         pos2_sb = keep.tile([P, M // LIST_GROUP], U16, name="pos2_sb")
 
-        rows = sbuf("rows", [P, P], F32)
-        nc.gpsimd.memset(rows[:], 0.0)
-        nc.gpsimd.dma_start(out=rows[0:TILES, :], in_=lossw.rearrange("(n p) -> n p", p=P))
-        nc.gpsimd.dma_start(out=rows[TILES : 2 * TILES, :], in_=d.rearrange("(n p) -> n p", p=P))
-        identity = sbuf("identity", [P, P], F32)
-        make_identity(nc, identity[:])
-        turned = psum.tile([P, BANK], F32, name="acc")
-        nc.tensor.transpose(turned[:, 0:P], rows[:], identity[:])
-        factors = sbuf("factors", [P, 2 * TILES], F32)
-        nc.scalar.copy(out=factors[:], in_=turned[:, 0 : 2 * TILES])
-
         tab_sc = sbuf("tab_sc", [P, T], U8)
         nc.vector.memset(tab_sc[:].bitcast(I32), 0)
+        rows = sbuf("rows", [P, P], F32)
+        nc.vector.memset(rows[:], 0.0)
         w4_sc = sbuf("w4_sc", [P, R_PASSES * H], U8)
         nc.vector.memset(w4_sc[:].bitcast(I32), 0)
 
@@ -84,6 +78,8 @@ def tile_list_glockenspiel_backward_sweep_kernel(
                         out=tab_sc[QUADRANT * q : QUADRANT * q + SCALE_ROWS * K_PASSES, :].bitcast(I32),
                         in_=tab_scales[:, SCALE_ROWS * q : SCALE_ROWS * (q + 1), :].bitcast(I32),
                     )
+                nc.scalar.dma_start(out=rows[0:TILES, :], in_=lossw.rearrange("(n p) -> n p", p=P))
+                nc.scalar.dma_start(out=rows[TILES : 2 * TILES, :], in_=d.rearrange("(n p) -> n p", p=P))
         nc.sync.dma_start(pos1_sb[:], pos1)
         nc.sync.dma_start(pos2_sb[:], pos2)
         for c in range(1, CHUNKS):
@@ -102,43 +98,49 @@ def tile_list_glockenspiel_backward_sweep_kernel(
                 in_=w4_scales[:, SCALE_ROWS * q : SCALE_ROWS * (q + 1), :].bitcast(I32).rearrange("a s n -> s a n"),
             )
 
+        identity = sbuf("identity", [P, P], F32)
+        make_identity(nc, identity[:])
+        turned = bank(BANKS - 1)
+        nc.tensor.transpose(turned[:, 0:P], rows[:], identity[:])
+        factors = sbuf("factors", [P, 2 * TILES], F32)
+
         def round_into_words(copy, grouped, planes):
             copy(
-                out=grouped[:].rearrange("p (g i j) -> p g j i", i=RUN, j=PACK),
-                in_=planes[:].rearrange("p j (g i) -> p g j i", i=RUN),
+                out=grouped.rearrange("p (g i j) -> p g j i", i=RUN, j=PACK),
+                in_=planes.rearrange("p j (g i) -> p g j i", i=RUN),
             )
-
-        def quantize(name, grouped, columns):
-            codes = sbuf(f"{name}_codes", [P, columns], U32)
-            scales = sbuf(f"{name}_scales", [P, columns], U8)
-            nc.vector.quantize_mx(out=codes[:].bitcast(FP8X4), scales=scales[:], in_=grouped[:])
-            return codes, scales
 
         v_words = {}
         v_sc = sbuf("v_sc", [P, S], U8)
+        halves = range(S // BANK)
 
-        def gather_words(a, after):
-            v_words[a] = sbuf(f"v_words{a}", [P, S], U32, after)
-            nc.vector.tensor_copy(v_words[a][:], tab_sb[a][:].bitcast(U32).indirect(offs_sb[:]))
+        def gather_words(a, half):
+            v_words[a, half] = sbuf(f"v_words{a}{half}", [P, BANK], U32)
+            entries = offs_sb[:, half * BANK // LIST_GROUP : (half + 1) * BANK // LIST_GROUP]
+            nc.vector.tensor_copy(v_words[a, half][:], tab_sb[a][:].bitcast(U32).indirect(entries))
 
+        grouped = {}
         h_acc = {}
 
-        def h_pass(a, c, copy=nc.scalar.copy):
-            grouped = sbuf(f"grouped{a}{c}", [P, CHUNK * PACK], BF16)
-            round_into_words(copy, grouped, w1_raw[a, c])
-            codes, scales = quantize(f"w1_{a}{c}", grouped, CHUNK)
-            for u in range(TILES_PER_CHUNK):
-                n = c * TILES_PER_CHUNK + u
-                for half in range(S // BANK):
+        def round_w1(a, c, copy):
+            grouped[a, c] = sbuf(f"grouped{a}{c}", [P, CHUNK * PACK], BF16)
+            round_into_words(copy, grouped[a, c][:], w1_raw[a, c][:])
+
+        def h_pass(a, c):
+            codes = sbuf(f"w1_codes{a}{c}", [P, CHUNK], U32)
+            scales = sbuf(f"w1_scales{a}{c}", [P, CHUNK], U8)
+            nc.vector.quantize_mx(out=codes[:].bitcast(FP8X4), scales=scales[:], in_=grouped[a, c][:])
+            for half in halves:
+                for u in range(TILES_PER_CHUNK):
+                    n = c * TILES_PER_CHUNK + u
                     if a == 0:
-                        h_acc[n, half] = psum.tile([P, BANK], F32, name="acc")
-                    cols = slice(half * BANK, (half + 1) * BANK)
+                        h_acc[n, half] = bank((2 * n + half) % BANKS)
                     nc.tensor.matmul_mx(
                         out=h_acc[n, half][:],
                         lhsT=codes[:, u * P : (u + 1) * P].bitcast(FP8X4),
                         lhsT_scale=scales[:, u * P : (u + 1) * P],
-                        rhs=v_words[a][:, cols].bitcast(FP8X4),
-                        rhs_scale=v_sc[SCALE_ROWS * a : P, cols],
+                        rhs=v_words[a, half][:].bitcast(FP8X4),
+                        rhs_scale=v_sc[SCALE_ROWS * a : P, half * BANK : (half + 1) * BANK],
                         start=(a == 0),
                         stop=(a == K_PASSES - 1),
                     )
@@ -148,89 +150,127 @@ def tile_list_glockenspiel_backward_sweep_kernel(
         h_picked = {}
         x_planes = [sbuf(f"x_planes{b}", [P, PACK, M], F32) for b in range(R_PASSES)]
 
+        def fill_neg_loss(b, after):
+            filled = sbuf(f"neg_loss{b}", [P, TILES_PER_PASS, M], F32, after)
+            for q in range(TILES_PER_PASS):
+                n = b * TILES_PER_PASS + q
+                neg_loss[n] = filled[:, q, :]
+                nc.scalar.activation(
+                    out=neg_loss[n], in_=factors[:, n : n + 1].to_broadcast([P, M]), func=ACT.Copy, scale=-1.0
+                )
+
+        def h_out(n, after=None):
+            h_sb[n] = sbuf(f"h_sb{n}", [P, S], F32, after)
+            for half in halves:
+                nc.scalar.copy(out=h_sb[n][:, half * BANK : (half + 1) * BANK], in_=h_acc[n, half][:])
+
+        def pick_x(n):
+            b, q = divmod(n, TILES_PER_PASS)
+            x_rows = sbuf(f"x_rows{n}", [P, M], F32)
+            nc.vector.tensor_tensor(x_rows[:], h_sb[n][:].indirect(pos1_sb[:]), neg_loss[n], ALU.mult)
+            nc.sync.dma_start(out=x_planes[b][QUADRANT * q : QUADRANT * (q + 1), :, :], in_=x_rows[:])
+
         def pick_h(n, dst):
             h_picked[n] = dst
             nc.vector.tensor_copy(dst, h_sb[n][:].indirect(pos2_sb[:]))
 
-        def h_out(n, after=None):
-            h_sb[n] = sbuf(f"h_sb{n}", [P, S], F32, after)
-            for half in range(S // BANK):
-                nc.scalar.copy(out=h_sb[n][:, half * BANK : (half + 1) * BANK], in_=h_acc[n, half][:])
-            b, q = divmod(n, TILES_PER_PASS)
-            x_rows = sbuf(f"x_rows{n}", [P, M], F32, f"x_rows{q}")
-            nc.vector.tensor_tensor(x_rows[:], h_sb[n][:].indirect(pos1_sb[:]), neg_loss[n][:], ALU.mult)
-            for i in range(PACK):
-                nc.sync.dma_start(out=x_planes[b][QUADRANT * q : QUADRANT * (q + 1), i, :], in_=x_rows[i:P:PACK, :])
-            if b == 0:
-                pick_h(n, picked_first[:, q, :])
+        x_codes = [sbuf(f"x_codes{b}", [P, M], U32) for b in range(R_PASSES)]
+        x_scales = [sbuf(f"x_scales{b}", [P, M], U8) for b in range(R_PASSES)]
+        x_grouped = {}
+
+        def round_x(b, cols, after):
+            x_grouped[b, cols.start] = sbuf(f"x_grouped{b}{cols.start}", [P, (cols.stop - cols.start) * PACK], BF16, after)
+            round_into_words(nc.scalar.copy, x_grouped[b, cols.start][:], x_planes[b][:, :, cols])
+
+        def quantize_x(b, cols):
+            nc.vector.quantize_mx(
+                out=x_codes[b][:, cols].bitcast(FP8X4), scales=x_scales[b][:, cols], in_=x_grouped[b, cols.start][:]
+            )
 
         y_acc = {}
 
-        def y_pass(b, codes, scales):
+        def y_pass(b):
             for n in range(TILES):
                 if b == 0:
-                    y_acc[n] = psum.tile([P, M], F32, name="acc")
+                    y_acc[n] = bank(n)
                 first = b * H + n * P
                 nc.tensor.matmul_mx(
                     out=y_acc[n][:],
                     lhsT=w4_sb[:, 2 * first : 2 * (first + P)].bitcast(FP4X4),
                     lhsT_scale=w4_sc[:, first : first + P],
-                    rhs=codes[:].bitcast(FP8X4),
-                    rhs_scale=scales[:],
+                    rhs=x_codes[b][:].bitcast(FP8X4),
+                    rhs_scale=x_scales[b][:],
                     start=(b == 0),
                     stop=(b == R_PASSES - 1),
                 )
 
-        gather_words(0, None)
-        nc.vector.tensor_copy(v_sc[:], tab_sc[:].indirect(offs_sb[:]))
+        result = {}
+
+        def square_tanh(n, dst):
+            result[n] = dst
+            nc.scalar.activation(out=dst, in_=h_picked[n], func=ACT.Tanh, scale=factors[:, TILES + n : TILES + n + 1])
+            nc.scalar.activation(out=dst, in_=dst, func=ACT.Square)
+
+        on_scalar, on_vector = nc.scalar.copy, nc.vector.tensor_copy
+
         for a in range(K_PASSES):
+            for half in halves:
+                gather_words(a, half)
+            if a == 0:
+                nc.vector.tensor_copy(v_sc[:], tab_sc[:].indirect(offs_sb[:]))
+            round_w1(a, 0, on_scalar)
             h_pass(a, 0)
-            if a + 1 < K_PASSES:
-                gather_words(a + 1, f"grouped{a}0")
-        h_pass(0, 1)
-        h_pass(1, 1)
-        h_pass(2, 1, copy=nc.vector.tensor_copy)
-        for n in range(TILES):
-            neg_loss[n] = sbuf(f"neg_loss{n}", [P, M], F32)
-            nc.scalar.activation(
-                out=neg_loss[n][:], in_=factors[:, n : n + 1].to_broadcast([P, M]), func=ACT.Copy, scale=-1.0
-            )
+            if a == 0:
+                nc.scalar.copy(out=factors[:], in_=turned[:, 0 : 2 * TILES])
+            if a < R_PASSES:
+                fill_neg_loss(a, f"raw{a}0")
 
-        picked_first = sbuf("picked_first", [P, TILES_PER_PASS, M], F32)
-        last_rounded = "raw11"
-        for c in range(2, CHUNKS):
-            n = (c - 2) * TILES_PER_CHUNK
-            h_out(n, last_rounded)
+        early = 1
+        for c in range(1, CHUNKS):
+            n = (c - 1) * TILES_PER_CHUNK
+            round_w1(0, c, on_scalar)
             h_pass(0, c)
+            round_w1(1, c, on_vector)
+            h_out(n, f"raw0{c}")
             h_pass(1, c)
-            h_out(n + 1, f"raw1{c}")
+            pick_x(n)
+            round_w1(2, c, on_scalar)
             h_pass(2, c)
-            last_rounded = f"raw2{c}"
-        h_out(TILES_PER_PASS, last_rounded)
-        for n in range(TILES_PER_PASS + 1, TILES):
-            h_out(n)
+            if c - 1 < early:
+                pick_h(c - 1, sbuf(f"h_picked{c - 1}", [P, M], F32, f"grouped2{c}")[:])
+            h_out(n + 1, f"raw2{c}")
+            pick_x(n + 1)
+        last = TILES - 1
+        first_cols, second_cols = slice(0, M // 2), slice(M // 2, M)
+        h_out(last - 1)
+        h_out(last)
+        pick_x(last - 1)
+        pick_x(last)
 
-        x_grouped = [
-            sbuf("x_grouped0", [P, M * PACK], BF16, f"neg_loss{TILES - 1}"),
-            sbuf("x_grouped1", [P, M * PACK], BF16),
-        ]
-        round_into_words(nc.vector.tensor_copy, x_grouped[0], x_planes[0])
-        round_into_words(nc.scalar.copy, x_grouped[1], x_planes[1])
-        picked_second = sbuf("picked_second", [P, TILES_PER_PASS, M], F32, "x_planes0")
-        pick_h(TILES_PER_PASS, picked_second[:, 0, :])
-        y_pass(0, *quantize("x0", x_grouped[0], M))
-        for q in range(1, TILES_PER_PASS):
-            pick_h(TILES_PER_PASS + q, picked_second[:, q, :])
-        y_pass(1, *quantize("x1", x_grouped[1], M))
+        round_x(0, first_cols, None)
+        round_x(0, second_cols, None)
+        result_early = sbuf("result_early", [P, TILES_PER_PASS - 1, M], F32, "x_planes0")
+        result_late = sbuf("result_late", [P, TILES_PER_PASS + 1, M], F32, "x_planes1")
+        picked_next = sbuf("picked_next", [P, TILES_PER_PASS - early, M], F32, "raw10")
+        for n in range(early, TILES_PER_PASS):
+            pick_h(n, picked_next[:, n - early, :])
+        quantize_x(0, first_cols)
+        quantize_x(0, second_cols)
+        y_pass(0)
+        for n in range(TILES_PER_PASS - 1):
+            square_tanh(n, result_early[:, n, :])
+        picked_late = sbuf("picked_late", [P, last - TILES_PER_PASS, M], F32, f"x_grouped0{second_cols.start}")
+        for n in range(TILES_PER_PASS, last):
+            pick_h(n, picked_late[:, n - TILES_PER_PASS, :])
+        round_x(1, slice(0, M), None)
+        quantize_x(1, slice(0, M))
+        y_pass(1)
+        pick_h(last, sbuf("picked_last", [P, M], F32, "x_grouped10")[:])
+        for n in range(TILES_PER_PASS - 1, TILES):
+            square_tanh(n, result_late[:, n - TILES_PER_PASS + 1, :])
 
-        result_second = sbuf("result_second", [P, TILES_PER_PASS, M], F32, "x_planes1")
-        result_first = sbuf("result_first", [P, TILES_PER_PASS, M], F32, f"neg_loss{TILES_PER_PASS}")
         for n in range(TILES):
-            b, q = divmod(n, TILES_PER_PASS)
-            result = (result_first, result_second)[b][:, q, :]
-            nc.scalar.activation(out=result, in_=h_picked[n], func=ACT.Tanh, scale=factors[:, TILES + n : TILES + n + 1])
-            nc.scalar.activation(out=result, in_=result, func=ACT.Square)
             nc.vector.scalar_tensor_tensor(
-                out=result, in0=result, scalar=1.0, in1=y_acc[n][:], op0=ALU.subtract, op1=ALU.mult
+                out=result[n], in0=result[n], scalar=1.0, in1=y_acc[n][:], op0=ALU.subtract, op1=ALU.mult
             )
-            nc.sync.dma_start(out=out[n * P : (n + 1) * P, :], in_=result)
+            nc.sync.dma_start(out=out[n * P : (n + 1) * P, :], in_=result[n])

@@ -27,7 +27,7 @@ BANKS = 8
 QUADRANT = 32
 SCALE_ROWS = 4
 LIST_GROUP = 16
-RUN = 4
+RUN = 2
 TILES = H // P
 TILES_PER_PASS = PASS // P
 TILES_PER_CHUNK = 2
@@ -114,10 +114,9 @@ def tile_list_glockenspiel_backward_sweep_kernel(
         v_sc = sbuf("v_sc", [P, S], U8)
         halves = range(S // BANK)
 
-        def gather_words(a, half):
-            v_words[a, half] = sbuf(f"v_words{a}{half}", [P, BANK], U32)
-            entries = offs_sb[:, half * BANK // LIST_GROUP : (half + 1) * BANK // LIST_GROUP]
-            nc.vector.tensor_copy(v_words[a, half][:], tab_sb[a][:].bitcast(U32).indirect(entries))
+        def gather_words(a):
+            v_words[a] = sbuf(f"v_words{a}", [P, S], U32)
+            nc.vector.tensor_copy(v_words[a][:], tab_sb[a][:].bitcast(U32).indirect(offs_sb[:]))
 
         grouped = {}
         h_acc = {}
@@ -130,8 +129,8 @@ def tile_list_glockenspiel_backward_sweep_kernel(
             codes = sbuf(f"w1_codes{a}{c}", [P, CHUNK], U32)
             scales = sbuf(f"w1_scales{a}{c}", [P, CHUNK], U8)
             nc.vector.quantize_mx(out=codes[:].bitcast(FP8X4), scales=scales[:], in_=grouped[a, c][:])
-            for half in halves:
-                for u in range(TILES_PER_CHUNK):
+            for u in range(TILES_PER_CHUNK):
+                for half in halves:
                     n = c * TILES_PER_CHUNK + u
                     if a == 0:
                         h_acc[n, half] = bank((2 * n + half) % BANKS)
@@ -139,7 +138,7 @@ def tile_list_glockenspiel_backward_sweep_kernel(
                         out=h_acc[n, half][:],
                         lhsT=codes[:, u * P : (u + 1) * P].bitcast(FP8X4),
                         lhsT_scale=scales[:, u * P : (u + 1) * P],
-                        rhs=v_words[a, half][:].bitcast(FP8X4),
+                        rhs=v_words[a][:, half * BANK : (half + 1) * BANK].bitcast(FP8X4),
                         rhs_scale=v_sc[SCALE_ROWS * a : P, half * BANK : (half + 1) * BANK],
                         start=(a == 0),
                         stop=(a == K_PASSES - 1),
@@ -178,14 +177,12 @@ def tile_list_glockenspiel_backward_sweep_kernel(
         x_scales = [sbuf(f"x_scales{b}", [P, M], U8) for b in range(R_PASSES)]
         x_grouped = {}
 
-        def round_x(b, cols, after):
-            x_grouped[b, cols.start] = sbuf(f"x_grouped{b}{cols.start}", [P, (cols.stop - cols.start) * PACK], BF16, after)
-            round_into_words(nc.scalar.copy, x_grouped[b, cols.start][:], x_planes[b][:, :, cols])
+        def round_x(b):
+            x_grouped[b] = sbuf(f"x_grouped{b}", [P, M * PACK], BF16)
+            round_into_words(nc.scalar.copy, x_grouped[b][:], x_planes[b][:])
 
-        def quantize_x(b, cols):
-            nc.vector.quantize_mx(
-                out=x_codes[b][:, cols].bitcast(FP8X4), scales=x_scales[b][:, cols], in_=x_grouped[b, cols.start][:]
-            )
+        def quantize_x(b):
+            nc.vector.quantize_mx(out=x_codes[b][:].bitcast(FP8X4), scales=x_scales[b][:], in_=x_grouped[b][:])
 
         y_acc = {}
 
@@ -214,8 +211,7 @@ def tile_list_glockenspiel_backward_sweep_kernel(
         on_scalar, on_vector = nc.scalar.copy, nc.vector.tensor_copy
 
         for a in range(K_PASSES):
-            for half in halves:
-                gather_words(a, half)
+            gather_words(a)
             if a == 0:
                 nc.vector.tensor_copy(v_sc[:], tab_sc[:].indirect(offs_sb[:]))
             round_w1(a, 0, on_scalar)
@@ -225,13 +221,13 @@ def tile_list_glockenspiel_backward_sweep_kernel(
             if a < R_PASSES:
                 fill_neg_loss(a, f"raw{a}0")
 
-        early = 1
+        early = 3
         for c in range(1, CHUNKS):
             n = (c - 1) * TILES_PER_CHUNK
             round_w1(0, c, on_scalar)
             h_pass(0, c)
-            round_w1(1, c, on_vector)
-            h_out(n, f"raw0{c}")
+            round_w1(1, c, on_vector if c == 1 else on_scalar)
+            h_out(n, f"raw{0 if c == 1 else 1}{c}")
             h_pass(1, c)
             pick_x(n)
             round_w1(2, c, on_scalar)
@@ -241,31 +237,28 @@ def tile_list_glockenspiel_backward_sweep_kernel(
             h_out(n + 1, f"raw2{c}")
             pick_x(n + 1)
         last = TILES - 1
-        first_cols, second_cols = slice(0, M // 2), slice(M // 2, M)
         h_out(last - 1)
         h_out(last)
         pick_x(last - 1)
         pick_x(last)
 
-        round_x(0, first_cols, None)
-        round_x(0, second_cols, None)
+        round_x(0)
         result_early = sbuf("result_early", [P, TILES_PER_PASS - 1, M], F32, "x_planes0")
         result_late = sbuf("result_late", [P, TILES_PER_PASS + 1, M], F32, "x_planes1")
         picked_next = sbuf("picked_next", [P, TILES_PER_PASS - early, M], F32, "raw10")
         for n in range(early, TILES_PER_PASS):
             pick_h(n, picked_next[:, n - early, :])
-        quantize_x(0, first_cols)
-        quantize_x(0, second_cols)
+        quantize_x(0)
         y_pass(0)
         for n in range(TILES_PER_PASS - 1):
             square_tanh(n, result_early[:, n, :])
-        picked_late = sbuf("picked_late", [P, last - TILES_PER_PASS, M], F32, f"x_grouped0{second_cols.start}")
+        picked_late = sbuf("picked_late", [P, last - TILES_PER_PASS, M], F32, "x_grouped0")
         for n in range(TILES_PER_PASS, last):
             pick_h(n, picked_late[:, n - TILES_PER_PASS, :])
-        round_x(1, slice(0, M), None)
-        quantize_x(1, slice(0, M))
+        round_x(1)
+        quantize_x(1)
         y_pass(1)
-        pick_h(last, sbuf("picked_last", [P, M], F32, "x_grouped10")[:])
+        pick_h(last, sbuf("picked_last", [P, M], F32, "x_grouped1")[:])
         for n in range(TILES_PER_PASS - 1, TILES):
             square_tanh(n, result_late[:, n - TILES_PER_PASS + 1, :])
 

@@ -70,8 +70,11 @@ def tile_list_glockenspiel_backward_sweep_kernel(
 
         nc.sync.dma_start(offs_sb[:], offs)
         for a in range(K_PASSES):
+            if a == K_PASSES - 1:
+                load_w1(a, 0)
             nc.sync.dma_start(out=tab_sb[a][:], in_=tab_words[a].rearrange("p t i -> p (t i)").bitcast(I32))
-            load_w1(a, 0)
+            if a < K_PASSES - 1:
+                load_w1(a, 0)
             if a == 0:
                 for q in range(P // QUADRANT):
                     nc.sync.dma_start(
@@ -102,7 +105,7 @@ def tile_list_glockenspiel_backward_sweep_kernel(
         make_identity(nc, identity[:])
         turned = bank(BANKS - 1)
         nc.tensor.transpose(turned[:, 0:P], rows[:], identity[:])
-        factors = sbuf("factors", [P, 2 * TILES], F32)
+        factors = sbuf("factors", [P, 2 * TILES], F32, "raw20")
 
         def round_into_words(copy, grouped, planes):
             copy(
@@ -114,9 +117,12 @@ def tile_list_glockenspiel_backward_sweep_kernel(
         v_sc = sbuf("v_sc", [P, S], U8)
         halves = range(S // BANK)
 
-        def gather_words(a):
+        def gather_words(a, pieces):
             v_words[a] = sbuf(f"v_words{a}", [P, S], U32)
-            nc.vector.tensor_copy(v_words[a][:], tab_sb[a][:].bitcast(U32).indirect(offs_sb[:]))
+            width = S // pieces
+            for first in range(0, S, width):
+                entries = offs_sb[:, first // LIST_GROUP : (first + width) // LIST_GROUP]
+                nc.vector.tensor_copy(v_words[a][:, first : first + width], tab_sb[a][:].bitcast(U32).indirect(entries))
 
         grouped = {}
         h_acc = {}
@@ -129,34 +135,26 @@ def tile_list_glockenspiel_backward_sweep_kernel(
             codes = sbuf(f"w1_codes{a}{c}", [P, CHUNK], U32)
             scales = sbuf(f"w1_scales{a}{c}", [P, CHUNK], U8)
             nc.vector.quantize_mx(out=codes[:].bitcast(FP8X4), scales=scales[:], in_=grouped[a, c][:])
-            for u in range(TILES_PER_CHUNK):
-                for half in halves:
-                    n = c * TILES_PER_CHUNK + u
-                    if a == 0:
-                        h_acc[n, half] = bank((2 * n + half) % BANKS)
-                    nc.tensor.matmul_mx(
-                        out=h_acc[n, half][:],
-                        lhsT=codes[:, u * P : (u + 1) * P].bitcast(FP8X4),
-                        lhsT_scale=scales[:, u * P : (u + 1) * P],
-                        rhs=v_words[a][:, half * BANK : (half + 1) * BANK].bitcast(FP8X4),
-                        rhs_scale=v_sc[SCALE_ROWS * a : P, half * BANK : (half + 1) * BANK],
-                        start=(a == 0),
-                        stop=(a == K_PASSES - 1),
-                    )
+            order = [(half, u) for u in range(TILES_PER_CHUNK) for half in halves]
+            if c == 0:
+                order = sorted(order)
+            for half, u in order:
+                n = c * TILES_PER_CHUNK + u
+                if a == 0:
+                    h_acc[n, half] = bank((2 * n + half) % BANKS)
+                nc.tensor.matmul_mx(
+                    out=h_acc[n, half][:],
+                    lhsT=codes[:, u * P : (u + 1) * P].bitcast(FP8X4),
+                    lhsT_scale=scales[:, u * P : (u + 1) * P],
+                    rhs=v_words[a][:, half * BANK : (half + 1) * BANK].bitcast(FP8X4),
+                    rhs_scale=v_sc[SCALE_ROWS * a : P, half * BANK : (half + 1) * BANK],
+                    start=(a == 0),
+                    stop=(a == K_PASSES - 1),
+                )
 
-        neg_loss = {}
         h_sb = {}
         h_picked = {}
-        x_planes = [sbuf(f"x_planes{b}", [P, PACK, M], F32) for b in range(R_PASSES)]
-
-        def fill_neg_loss(b, after):
-            filled = sbuf(f"neg_loss{b}", [P, TILES_PER_PASS, M], F32, after)
-            for q in range(TILES_PER_PASS):
-                n = b * TILES_PER_PASS + q
-                neg_loss[n] = filled[:, q, :]
-                nc.scalar.activation(
-                    out=neg_loss[n], in_=factors[:, n : n + 1].to_broadcast([P, M]), func=ACT.Copy, scale=-1.0
-                )
+        x_planes = [sbuf(f"x_planes{b}", [P, PACK, M], BF16) for b in range(R_PASSES)]
 
         def h_out(n, after=None):
             h_sb[n] = sbuf(f"h_sb{n}", [P, S], F32, after)
@@ -165,8 +163,10 @@ def tile_list_glockenspiel_backward_sweep_kernel(
 
         def pick_x(n):
             b, q = divmod(n, TILES_PER_PASS)
-            x_rows = sbuf(f"x_rows{n}", [P, M], F32)
-            nc.vector.tensor_tensor(x_rows[:], h_sb[n][:].indirect(pos1_sb[:]), neg_loss[n], ALU.mult)
+            carried = sbuf(f"carried{n}", [P, M], F32)
+            nc.vector.tensor_copy(carried[:], h_sb[n][:].indirect(pos1_sb[:]))
+            x_rows = sbuf(f"x_rows{n}", [P, M], BF16)
+            nc.gpsimd.tensor_scalar(x_rows[:], carried[:], factors[:, n : n + 1], -1.0, ALU.mult, ALU.mult)
             nc.sync.dma_start(out=x_planes[b][QUADRANT * q : QUADRANT * (q + 1), :, :], in_=x_rows[:])
 
         def pick_h(n, dst):
@@ -206,28 +206,29 @@ def tile_list_glockenspiel_backward_sweep_kernel(
         def square_tanh(n, dst):
             result[n] = dst
             nc.scalar.activation(out=dst, in_=h_picked[n], func=ACT.Tanh, scale=factors[:, TILES + n : TILES + n + 1])
-            nc.scalar.activation(out=dst, in_=dst, func=ACT.Square)
+            if n < ahead:
+                nc.gpsimd.tensor_tensor(dst, dst, dst, ALU.mult)
+            else:
+                nc.scalar.activation(out=dst, in_=dst, func=ACT.Square)
 
         on_scalar, on_vector = nc.scalar.copy, nc.vector.tensor_copy
 
         for a in range(K_PASSES):
-            gather_words(a)
+            round_w1(a, 0, on_scalar)
+            gather_words(a, len(halves) if a == K_PASSES - 1 else 1)
             if a == 0:
                 nc.vector.tensor_copy(v_sc[:], tab_sc[:].indirect(offs_sb[:]))
-            round_w1(a, 0, on_scalar)
             h_pass(a, 0)
-            if a == 0:
-                nc.scalar.copy(out=factors[:], in_=turned[:, 0 : 2 * TILES])
-            if a < R_PASSES:
-                fill_neg_loss(a, f"raw{a}0")
+        nc.scalar.copy(out=factors[:], in_=turned[:, 0 : 2 * TILES])
 
         early = 3
+        ahead = 5
         for c in range(1, CHUNKS):
             n = (c - 1) * TILES_PER_CHUNK
             round_w1(0, c, on_scalar)
             h_pass(0, c)
-            round_w1(1, c, on_vector if c == 1 else on_scalar)
-            h_out(n, f"raw{0 if c == 1 else 1}{c}")
+            round_w1(1, c, on_scalar if c == 1 else on_vector)
+            h_out(n, f"raw0{c}")
             h_pass(1, c)
             pick_x(n)
             round_w1(2, c, on_scalar)
@@ -243,24 +244,26 @@ def tile_list_glockenspiel_backward_sweep_kernel(
         pick_x(last)
 
         round_x(0)
-        result_early = sbuf("result_early", [P, TILES_PER_PASS - 1, M], F32, "x_planes0")
-        result_late = sbuf("result_late", [P, TILES_PER_PASS + 1, M], F32, "x_planes1")
-        picked_next = sbuf("picked_next", [P, TILES_PER_PASS - early, M], F32, "raw10")
+        result_early = sbuf("result_early", [P, ahead, M], F32, "x_planes0")
+        result_late = sbuf("result_late", [P, TILES - ahead, M], F32, "x_planes1")
+        picked_next = sbuf("picked_next", [P, TILES_PER_PASS - early, M], F32, f"carried{last - 1}")
         for n in range(early, TILES_PER_PASS):
             pick_h(n, picked_next[:, n - early, :])
         quantize_x(0)
         y_pass(0)
-        for n in range(TILES_PER_PASS - 1):
+        for n in range(TILES_PER_PASS):
             square_tanh(n, result_early[:, n, :])
         picked_late = sbuf("picked_late", [P, last - TILES_PER_PASS, M], F32, "x_grouped0")
         for n in range(TILES_PER_PASS, last):
             pick_h(n, picked_late[:, n - TILES_PER_PASS, :])
+            if n < ahead:
+                square_tanh(n, result_early[:, n, :])
         round_x(1)
         quantize_x(1)
         y_pass(1)
         pick_h(last, sbuf("picked_last", [P, M], F32, "x_grouped1")[:])
-        for n in range(TILES_PER_PASS - 1, TILES):
-            square_tanh(n, result_late[:, n - TILES_PER_PASS + 1, :])
+        for n in range(ahead, TILES):
+            square_tanh(n, result_late[:, n - ahead, :])
 
         for n in range(TILES):
             nc.vector.scalar_tensor_tensor(

@@ -131,6 +131,17 @@ def tile_list_glockenspiel_backward_sweep_kernel(
             grouped[a, c] = sbuf(f"grouped{a}{c}", [P, CHUNK * PACK], BF16)
             round_into_words(copy, grouped[a, c][:], w1_raw[a, c][:])
 
+        def round_w1_on_gpsimd(a, c, after=None):
+            grouped[a, c] = sbuf(f"grouped{a}{c}", [P, CHUNK * PACK], BF16, after)
+            nc.gpsimd.tensor_scalar(
+                grouped[a, c][:].rearrange("p (c j) -> p c j", j=PACK),
+                w1_raw[a, c][:].rearrange("p j c -> p c j"),
+                1.0,
+                0.0,
+                ALU.mult,
+                ALU.add,
+            )
+
         def h_pass(a, c):
             codes = sbuf(f"w1_codes{a}{c}", [P, CHUNK], U32)
             scales = sbuf(f"w1_scales{a}{c}", [P, CHUNK], U8)
@@ -154,24 +165,37 @@ def tile_list_glockenspiel_backward_sweep_kernel(
 
         h_sb = {}
         h_picked = {}
-        x_planes = [sbuf(f"x_planes{b}", [P, PACK, M], BF16) for b in range(R_PASSES)]
+        x_cols = [[slice(0, M)], [slice(0, M // 2), slice(M // 2, M)]]
+        x_planes = {
+            (b, cols.start): sbuf(f"x_planes{b}{cols.start}", [P, PACK, cols.stop - cols.start], BF16)
+            for b in range(R_PASSES)
+            for cols in x_cols[b]
+        }
 
-        def h_out(n, after=None):
-            h_sb[n] = sbuf(f"h_sb{n}", [P, S], F32, after)
-            for half in halves:
-                nc.scalar.copy(out=h_sb[n][:, half * BANK : (half + 1) * BANK], in_=h_acc[n, half][:])
+        def h_out(c, after):
+            pair = sbuf(f"h_pair{c}", [P, TILES_PER_CHUNK, S], F32, after)
+            for u in range(TILES_PER_CHUNK):
+                n = c * TILES_PER_CHUNK + u
+                h_sb[n] = pair[:, u, :]
+                for half in halves:
+                    nc.scalar.copy(out=h_sb[n][:, half * BANK : (half + 1) * BANK], in_=h_acc[n, half][:])
 
-        def pick_x(n):
+        def pick_x(n, pieces):
             b, q = divmod(n, TILES_PER_PASS)
-            carried = sbuf(f"carried{n}", [P, M], F32)
-            nc.vector.tensor_copy(carried[:], h_sb[n][:].indirect(pos1_sb[:]))
-            x_rows = sbuf(f"x_rows{n}", [P, M], BF16)
-            nc.gpsimd.tensor_scalar(x_rows[:], carried[:], factors[:, n : n + 1], -1.0, ALU.mult, ALU.mult)
-            nc.sync.dma_start(out=x_planes[b][QUADRANT * q : QUADRANT * (q + 1), :, :], in_=x_rows[:])
+            x_rows = sbuf(f"x_rows{n}", [P, M], BF16, {1: "raw02", 2: "raw03"}.get(n))
+            for cols in pieces:
+                entries = pos1_sb[:, cols.start // LIST_GROUP : cols.stop // LIST_GROUP]
+                carried = sbuf(f"carried{n}_{cols.start}", [P, cols.stop - cols.start], F32)
+                nc.vector.tensor_copy(carried[:], h_sb[n].indirect(entries))
+                nc.gpsimd.tensor_scalar(x_rows[:, cols], carried[:], factors[:, n : n + 1], -1.0, ALU.mult, ALU.mult)
+            for cols in x_cols[b]:
+                nc.sync.dma_start(
+                    out=x_planes[b, cols.start][QUADRANT * q : QUADRANT * (q + 1), :, :], in_=x_rows[:, cols]
+                )
 
         def pick_h(n, dst):
             h_picked[n] = dst
-            nc.vector.tensor_copy(dst, h_sb[n][:].indirect(pos2_sb[:]))
+            nc.vector.tensor_copy(dst, h_sb[n].indirect(pos2_sb[:]))
 
         x_codes = [sbuf(f"x_codes{b}", [P, M], U32) for b in range(R_PASSES)]
         x_scales = [sbuf(f"x_scales{b}", [P, M], U8) for b in range(R_PASSES)]
@@ -179,7 +203,9 @@ def tile_list_glockenspiel_backward_sweep_kernel(
 
         def round_x(b):
             x_grouped[b] = sbuf(f"x_grouped{b}", [P, M * PACK], BF16)
-            round_into_words(nc.scalar.copy, x_grouped[b][:], x_planes[b][:])
+            for cols in x_cols[b]:
+                words = x_grouped[b][:, cols.start * PACK : cols.stop * PACK]
+                round_into_words(nc.scalar.copy, words, x_planes[b, cols.start][:])
 
         def quantize_x(b):
             nc.vector.quantize_mx(out=x_codes[b][:].bitcast(FP8X4), scales=x_scales[b][:], in_=x_grouped[b][:])
@@ -206,7 +232,7 @@ def tile_list_glockenspiel_backward_sweep_kernel(
         def square_tanh(n, dst):
             result[n] = dst
             nc.scalar.activation(out=dst, in_=h_picked[n], func=ACT.Tanh, scale=factors[:, TILES + n : TILES + n + 1])
-            if n < ahead:
+            if n < squared_on_gpsimd:
                 nc.gpsimd.tensor_tensor(dst, dst, dst, ALU.mult)
             else:
                 nc.scalar.activation(out=dst, in_=dst, func=ACT.Square)
@@ -221,49 +247,56 @@ def tile_list_glockenspiel_backward_sweep_kernel(
             h_pass(a, 0)
         nc.scalar.copy(out=factors[:], in_=turned[:, 0 : 2 * TILES])
 
-        early = 3
-        ahead = 5
-        for c in range(1, CHUNKS):
-            n = (c - 1) * TILES_PER_CHUNK
-            round_w1(0, c, on_scalar)
+        whole = x_cols[0]
+        last = TILES - 1
+        squared_on_gpsimd = 3
+
+        round_w1(0, 1, on_scalar)
+        h_pass(0, 1)
+        round_w1(1, 1, on_vector)
+        h_pass(1, 1)
+        round_w1_on_gpsimd(2, 1)
+        def pick_h_behind(n, after):
+            pick_h(n, sbuf(f"picked{n}", [P, M], F32, after)[:])
+
+        h_out(0, "raw01")
+        pick_x(0, whole)
+        h_pass(2, 1)
+        pick_h_behind(0, "raw21")
+        for c in range(2, CHUNKS):
+            round_w1_on_gpsimd(0, c, f"grouped2{c - 1}")
+            for n in range(TILES_PER_CHUNK * (c - 2), TILES_PER_CHUNK * (c - 1)):
+                if n > 0:
+                    pick_x(n, whole)
             h_pass(0, c)
-            round_w1(1, c, on_scalar if c == 1 else on_vector)
-            h_out(n, f"raw0{c}")
+            round_w1(1, c, on_scalar)
             h_pass(1, c)
-            pick_x(n)
+            pick_h_behind(c - 1, f"raw1{c}")
             round_w1(2, c, on_scalar)
             h_pass(2, c)
-            if c - 1 < early:
-                pick_h(c - 1, sbuf(f"h_picked{c - 1}", [P, M], F32, f"grouped2{c}")[:])
-            h_out(n + 1, f"raw2{c}")
-            pick_x(n + 1)
-        last = TILES - 1
-        h_out(last - 1)
-        h_out(last)
-        pick_x(last - 1)
-        pick_x(last)
+            h_out(c - 1, f"raw2{c}")
+        h_out(CHUNKS - 1, None)
+        for n in range(TILES_PER_PASS, TILES):
+            pick_x(n, x_cols[1] if n == last else whole)
 
+        early = CHUNKS - 1
+        picked_next = sbuf("picked_next", [P, M], F32, f"carried{last}_0")
+        pick_h(early, picked_next[:])
         round_x(0)
-        result_early = sbuf("result_early", [P, ahead, M], F32, "x_planes0")
-        result_late = sbuf("result_late", [P, TILES - ahead, M], F32, "x_planes1")
-        picked_next = sbuf("picked_next", [P, TILES_PER_PASS - early, M], F32, f"carried{last - 1}")
-        for n in range(early, TILES_PER_PASS):
-            pick_h(n, picked_next[:, n - early, :])
         quantize_x(0)
         y_pass(0)
-        for n in range(TILES_PER_PASS):
-            square_tanh(n, result_early[:, n, :])
-        picked_late = sbuf("picked_late", [P, last - TILES_PER_PASS, M], F32, "x_grouped0")
-        for n in range(TILES_PER_PASS, last):
-            pick_h(n, picked_late[:, n - TILES_PER_PASS, :])
-            if n < ahead:
-                square_tanh(n, result_early[:, n, :])
+        behind_x0 = sbuf("behind_x0", [P, early + 3, M], F32, "x_planes00")
+        for n in range(early):
+            square_tanh(n, behind_x0[:, n, :])
+        for n in range(early + 1, last):
+            pick_h(n, behind_x0[:, n - 1, :])
         round_x(1)
         quantize_x(1)
         y_pass(1)
-        pick_h(last, sbuf("picked_last", [P, M], F32, "x_grouped1")[:])
-        for n in range(ahead, TILES):
-            square_tanh(n, result_late[:, n - ahead, :])
+        behind_x1 = sbuf("behind_x1", [P, TILES - early + 1, M], F32, f"x_planes1{M // 2}")
+        pick_h(last, behind_x1[:, 0, :])
+        for n in range(early, TILES):
+            square_tanh(n, behind_x1[:, n - early + 1, :])
 
         for n in range(TILES):
             nc.vector.scalar_tensor_tensor(

@@ -131,7 +131,7 @@ def tile_list_glockenspiel_backward_sweep_kernel(
             grouped[a, c] = sbuf(f"grouped{a}{c}", [P, CHUNK * PACK], BF16)
             round_into_words(copy, grouped[a, c][:], w1_raw[a, c][:])
 
-        def round_w1_on_gpsimd(a, c, after=None):
+        def round_w1_on_gpsimd(a, c, after):
             grouped[a, c] = sbuf(f"grouped{a}{c}", [P, CHUNK * PACK], BF16, after)
             nc.gpsimd.tensor_scalar(
                 grouped[a, c][:].rearrange("p (c j) -> p c j", j=PACK),
@@ -180,12 +180,12 @@ def tile_list_glockenspiel_backward_sweep_kernel(
                 for half in halves:
                     nc.scalar.copy(out=h_sb[n][:, half * BANK : (half + 1) * BANK], in_=h_acc[n, half][:])
 
-        def pick_x(n, pieces):
+        def pick_x(n, pieces, after=None):
             b, q = divmod(n, TILES_PER_PASS)
-            x_rows = sbuf(f"x_rows{n}", [P, M], BF16, {1: "raw02", 2: "raw03"}.get(n))
+            x_rows = sbuf(f"x_rows{n}", [P, M], BF16, {0: "w1_codes21", 1: "w1_scales21", 2: "raw03"}.get(n))
             for cols in pieces:
                 entries = pos1_sb[:, cols.start // LIST_GROUP : cols.stop // LIST_GROUP]
-                carried = sbuf(f"carried{n}_{cols.start}", [P, cols.stop - cols.start], F32)
+                carried = sbuf(f"carried{n}_{cols.start}", [P, cols.stop - cols.start], F32, after)
                 nc.vector.tensor_copy(carried[:], h_sb[n].indirect(entries))
                 nc.gpsimd.tensor_scalar(x_rows[:, cols], carried[:], factors[:, n : n + 1], -1.0, ALU.mult, ALU.mult)
             for cols in x_cols[b]:
@@ -229,13 +229,14 @@ def tile_list_glockenspiel_backward_sweep_kernel(
 
         result = {}
 
-        def square_tanh(n, dst):
-            result[n] = dst
+        def square_tanh(n, dst, squared=None):
             nc.scalar.activation(out=dst, in_=h_picked[n], func=ACT.Tanh, scale=factors[:, TILES + n : TILES + n + 1])
-            if n < squared_on_gpsimd:
-                nc.gpsimd.tensor_tensor(dst, dst, dst, ALU.mult)
-            else:
+            if squared is None:
+                result[n] = dst
                 nc.scalar.activation(out=dst, in_=dst, func=ACT.Square)
+            else:
+                result[n] = squared
+                nc.gpsimd.tensor_tensor(squared, dst, dst, ALU.mult)
 
         on_scalar, on_vector = nc.scalar.copy, nc.vector.tensor_copy
 
@@ -249,32 +250,38 @@ def tile_list_glockenspiel_backward_sweep_kernel(
 
         whole = x_cols[0]
         last = TILES - 1
-        squared_on_gpsimd = 3
 
         round_w1(0, 1, on_scalar)
         h_pass(0, 1)
-        round_w1(1, 1, on_vector)
+        round_w1(1, 1, on_scalar)
         h_pass(1, 1)
-        round_w1_on_gpsimd(2, 1)
+        round_w1(2, 1, on_vector)
+        h_pass(2, 1)
         def pick_h_behind(n, after):
             pick_h(n, sbuf(f"picked{n}", [P, M], F32, after)[:])
 
-        h_out(0, "raw01")
+        round_w1_on_gpsimd(0, 2, "grouped21")
+        h_out(0, "raw11")
         pick_x(0, whole)
-        h_pass(2, 1)
-        pick_h_behind(0, "raw21")
-        for c in range(2, CHUNKS):
-            round_w1_on_gpsimd(0, c, f"grouped2{c - 1}")
-            for n in range(TILES_PER_CHUNK * (c - 2), TILES_PER_CHUNK * (c - 1)):
-                if n > 0:
-                    pick_x(n, whole)
-            h_pass(0, c)
-            round_w1(1, c, on_scalar)
-            h_pass(1, c)
-            pick_h_behind(c - 1, f"raw1{c}")
-            round_w1(2, c, on_scalar)
-            h_pass(2, c)
-            h_out(c - 1, f"raw2{c}")
+        pick_h_behind(0, None)
+        pick_x(1, whole)
+        h_pass(0, 2)
+        pick_h_behind(1, "raw02")
+        for a in range(1, K_PASSES):
+            round_w1(a, 2, on_scalar)
+            h_pass(a, 2)
+        h_out(1, "raw22")
+
+        round_w1_on_gpsimd(0, 3, "grouped22")
+        pick_x(2, whole)
+        pick_h_behind(2, None)
+        h_pass(0, 3)
+        round_w1(1, 3, on_scalar)
+        h_pass(1, 3)
+        pick_x(3, whole, "raw13")
+        round_w1(2, 3, on_scalar)
+        h_pass(2, 3)
+        h_out(2, "raw23")
         h_out(CHUNKS - 1, None)
         for n in range(TILES_PER_PASS, TILES):
             pick_x(n, x_cols[1] if n == last else whole)
@@ -286,8 +293,9 @@ def tile_list_glockenspiel_backward_sweep_kernel(
         quantize_x(0)
         y_pass(0)
         behind_x0 = sbuf("behind_x0", [P, early + 3, M], F32, "x_planes00")
+        squares = sbuf("squares", [P, early, M], F32, "x_grouped0")
         for n in range(early):
-            square_tanh(n, behind_x0[:, n, :])
+            square_tanh(n, behind_x0[:, n, :], squares[:, n, :])
         for n in range(early + 1, last):
             pick_h(n, behind_x0[:, n - 1, :])
         round_x(1)
@@ -299,7 +307,9 @@ def tile_list_glockenspiel_backward_sweep_kernel(
             square_tanh(n, behind_x1[:, n - early + 1, :])
 
         for n in range(TILES):
-            nc.vector.scalar_tensor_tensor(
-                out=result[n], in0=result[n], scalar=1.0, in1=y_acc[n][:], op0=ALU.subtract, op1=ALU.mult
-            )
-            nc.sync.dma_start(out=out[n * P : (n + 1) * P, :], in_=result[n])
+            for cols in x_cols[1] if n == last else whole:
+                part = result[n][:, cols]
+                nc.vector.scalar_tensor_tensor(
+                    out=part, in0=part, scalar=1.0, in1=y_acc[n][:, cols], op0=ALU.subtract, op1=ALU.mult
+                )
+                nc.sync.dma_start(out=out[n * P : (n + 1) * P, cols], in_=part)

@@ -117,12 +117,12 @@ def tile_list_glockenspiel_backward_sweep_kernel(
         v_sc = sbuf("v_sc", [P, S], U8)
         halves = range(S // BANK)
 
-        def gather_words(a, pieces):
-            v_words[a] = sbuf(f"v_words{a}", [P, S], U32)
-            width = S // pieces
-            for first in range(0, S, width):
-                entries = offs_sb[:, first // LIST_GROUP : (first + width) // LIST_GROUP]
-                nc.vector.tensor_copy(v_words[a][:, first : first + width], tab_sb[a][:].bitcast(U32).indirect(entries))
+        def gather_words(a, cols):
+            words = sbuf(f"v_words{a}{cols.start}", [P, cols.stop - cols.start], U32)
+            entries = offs_sb[:, cols.start // LIST_GROUP : cols.stop // LIST_GROUP]
+            nc.vector.tensor_copy(words[:], tab_sb[a][:].bitcast(U32).indirect(entries))
+            for first in range(cols.start, cols.stop, BANK):
+                v_words[a, first // BANK] = words[:, first - cols.start : first - cols.start + BANK]
 
         grouped = {}
         h_acc = {}
@@ -142,11 +142,21 @@ def tile_list_glockenspiel_backward_sweep_kernel(
                 ALU.add,
             )
 
-        def h_pass(a, c):
+        w1_mx = {}
+
+        def quantize_w1(a, c):
             codes = sbuf(f"w1_codes{a}{c}", [P, CHUNK], U32)
             scales = sbuf(f"w1_scales{a}{c}", [P, CHUNK], U8)
             nc.vector.quantize_mx(out=codes[:].bitcast(FP8X4), scales=scales[:], in_=grouped[a, c][:])
-            order = [(half, u) for u in range(TILES_PER_CHUNK) for half in halves]
+            w1_mx[a, c] = codes, scales
+
+        def h_pass(a, c):
+            quantize_w1(a, c)
+            multiply(a, c)
+
+        def multiply(a, c, tiles=range(TILES_PER_CHUNK)):
+            codes, scales = w1_mx[a, c]
+            order = [(half, u) for u in tiles for half in halves]
             if c == 0:
                 order = sorted(order)
             for half, u in order:
@@ -157,7 +167,7 @@ def tile_list_glockenspiel_backward_sweep_kernel(
                     out=h_acc[n, half][:],
                     lhsT=codes[:, u * P : (u + 1) * P].bitcast(FP8X4),
                     lhsT_scale=scales[:, u * P : (u + 1) * P],
-                    rhs=v_words[a][:, half * BANK : (half + 1) * BANK].bitcast(FP8X4),
+                    rhs=v_words[a, half].bitcast(FP8X4),
                     rhs_scale=v_sc[SCALE_ROWS * a : P, half * BANK : (half + 1) * BANK],
                     start=(a == 0),
                     stop=(a == K_PASSES - 1),
@@ -165,7 +175,7 @@ def tile_list_glockenspiel_backward_sweep_kernel(
 
         h_sb = {}
         h_picked = {}
-        x_cols = [[slice(0, M)], [slice(0, M // 2), slice(M // 2, M)]]
+        x_cols = [[slice(0, M // 2), slice(M // 2, M)]] * R_PASSES
         x_planes = {
             (b, cols.start): sbuf(f"x_planes{b}{cols.start}", [P, PACK, cols.stop - cols.start], BF16)
             for b in range(R_PASSES)
@@ -173,21 +183,24 @@ def tile_list_glockenspiel_backward_sweep_kernel(
         }
 
         def h_out(c, after):
-            pair = sbuf(f"h_pair{c}", [P, TILES_PER_CHUNK, S], F32, after)
+            pair = sbuf(f"h_pair{c}", [P, TILES_PER_CHUNK * S + M], F32, after)
             for u in range(TILES_PER_CHUNK):
                 n = c * TILES_PER_CHUNK + u
-                h_sb[n] = pair[:, u, :]
+                h_sb[n] = pair[:, u * S : (u + 1) * S]
                 for half in halves:
                     nc.scalar.copy(out=h_sb[n][:, half * BANK : (half + 1) * BANK], in_=h_acc[n, half][:])
+            return pair[:, TILES_PER_CHUNK * S :]
 
-        def pick_x(n, pieces, after=None):
+        def pick_x(n, pieces, place=None):
             b, q = divmod(n, TILES_PER_PASS)
-            x_rows = sbuf(f"x_rows{n}", [P, M], BF16, {0: "w1_codes21", 1: "w1_scales21", 2: "raw03"}.get(n))
+            x_rows = sbuf(f"x_rows{n}", [P, M], BF16, {0: "w1_codes21", 1: "w1_scales21", 2: "raw13"}.get(n))
             for cols in pieces:
                 entries = pos1_sb[:, cols.start // LIST_GROUP : cols.stop // LIST_GROUP]
-                carried = sbuf(f"carried{n}_{cols.start}", [P, cols.stop - cols.start], F32, after)
-                nc.vector.tensor_copy(carried[:], h_sb[n].indirect(entries))
-                nc.gpsimd.tensor_scalar(x_rows[:, cols], carried[:], factors[:, n : n + 1], -1.0, ALU.mult, ALU.mult)
+                carried = place
+                if place is None:
+                    carried = sbuf(f"carried{n}_{cols.start}", [P, cols.stop - cols.start], F32)[:]
+                nc.vector.tensor_copy(carried, h_sb[n].indirect(entries))
+                nc.gpsimd.tensor_scalar(x_rows[:, cols], carried, factors[:, n : n + 1], -1.0, ALU.mult, ALU.mult)
             for cols in x_cols[b]:
                 nc.sync.dma_start(
                     out=x_planes[b, cols.start][QUADRANT * q : QUADRANT * (q + 1), :, :], in_=x_rows[:, cols]
@@ -242,13 +255,14 @@ def tile_list_glockenspiel_backward_sweep_kernel(
 
         for a in range(K_PASSES):
             round_w1(a, 0, on_scalar)
-            gather_words(a, len(halves) if a == K_PASSES - 1 else 1)
+            for cols in [slice(0, BANK), slice(BANK, S)] if a == K_PASSES - 1 else [slice(0, S)]:
+                gather_words(a, cols)
             if a == 0:
                 nc.vector.tensor_copy(v_sc[:], tab_sc[:].indirect(offs_sb[:]))
             h_pass(a, 0)
         nc.scalar.copy(out=factors[:], in_=turned[:, 0 : 2 * TILES])
 
-        whole = x_cols[0]
+        whole = [slice(0, M)]
         last = TILES - 1
 
         round_w1(0, 1, on_scalar)
@@ -264,52 +278,72 @@ def tile_list_glockenspiel_backward_sweep_kernel(
         h_out(0, "raw11")
         pick_x(0, whole)
         pick_h_behind(0, None)
-        pick_x(1, whole)
         h_pass(0, 2)
-        pick_h_behind(1, "raw02")
+        pick_x(1, whole, sbuf("carried1", [P, M], F32, "raw02")[:])
         for a in range(1, K_PASSES):
             round_w1(a, 2, on_scalar)
-            h_pass(a, 2)
-        h_out(1, "raw22")
+            quantize_w1(a, 2)
+        for u in range(TILES_PER_CHUNK):
+            for a in range(1, K_PASSES):
+                multiply(a, 2, [u])
+        pick_h(1, h_out(1, "raw22"))
 
-        round_w1_on_gpsimd(0, 3, "grouped22")
+        round_w1_on_gpsimd(1, 3, "grouped22")
         pick_x(2, whole)
-        pick_h_behind(2, None)
+        round_w1(0, 3, on_scalar)
         h_pass(0, 3)
-        round_w1(1, 3, on_scalar)
-        h_pass(1, 3)
-        pick_x(3, whole, "raw13")
         round_w1(2, 3, on_scalar)
-        h_pass(2, 3)
-        h_out(2, "raw23")
+        for a in range(1, K_PASSES):
+            quantize_w1(a, 3)
+        for u in range(TILES_PER_CHUNK):
+            for a in range(1, K_PASSES):
+                multiply(a, 3, [u])
+        pick_x(3, whole, h_out(2, "raw23"))
         h_out(CHUNKS - 1, None)
         for n in range(TILES_PER_PASS, TILES):
             pick_x(n, x_cols[1] if n == last else whole)
 
-        early = CHUNKS - 1
-        picked_next = sbuf("picked_next", [P, M], F32, f"carried{last}_0")
-        pick_h(early, picked_next[:])
-        round_x(0)
-        quantize_x(0)
-        y_pass(0)
-        behind_x0 = sbuf("behind_x0", [P, early + 3, M], F32, "x_planes00")
-        squares = sbuf("squares", [P, early, M], F32, "x_grouped0")
-        for n in range(early):
-            square_tanh(n, behind_x0[:, n, :], squares[:, n, :])
-        for n in range(early + 1, last):
-            pick_h(n, behind_x0[:, n - 1, :])
-        round_x(1)
-        quantize_x(1)
-        y_pass(1)
-        behind_x1 = sbuf("behind_x1", [P, TILES - early + 1, M], F32, f"x_planes1{M // 2}")
-        pick_h(last, behind_x1[:, 0, :])
-        for n in range(early, TILES):
-            square_tanh(n, behind_x1[:, n - early + 1, :])
-
-        for n in range(TILES):
+        def finish(n):
+            if n < finished_on_gpsimd:
+                neg_y = sbuf(f"neg_y{n}", [P, M], F32, f"carried{n}_0")
+                nc.scalar.copy(out=neg_y[:], in_=y_acc[n][:])
+                nc.gpsimd.tensor_tensor(result[n], result[n], neg_y[:], ALU.mult)
+                nc.sync.dma_start(out=out[n * P : (n + 1) * P, :], in_=result[n])
+                return
             for cols in x_cols[1] if n == last else whole:
                 part = result[n][:, cols]
                 nc.vector.scalar_tensor_tensor(
                     out=part, in0=part, scalar=1.0, in1=y_acc[n][:, cols], op0=ALU.subtract, op1=ALU.mult
                 )
                 nc.sync.dma_start(out=out[n * P : (n + 1) * P, cols], in_=part)
+
+        early = 2
+        finished_on_gpsimd = 1
+        pick_h_behind(early, f"carried{last}_0")
+        round_x(0)
+        quantize_x(0)
+        y_pass(0)
+        behind_x0 = sbuf("behind_x0", [P, 5, M], F32, f"x_planes0{M // 2}")
+        for n in range(early + 1):
+            tanh = behind_x0[:, n, :] if n else sbuf("tanh0", [P, M], F32, "x_planes00")[:]
+            square_tanh(n, tanh, behind_x0[:, n, :])
+            if n < finished_on_gpsimd:
+                nc.gpsimd.tensor_scalar(result[n], result[n], 1.0, -1.0, ALU.mult, ALU.add)
+        pick_h(3, behind_x0[:, 3, :])
+        pick_h_behind(4, "x_planes00")
+        pick_h(5, behind_x0[:, 4, :])
+        round_x(1)
+        quantize_x(1)
+        y_pass(1)
+        behind_x1 = sbuf("behind_x1", [P, 6, M], F32, f"x_planes1{M // 2}")
+        pick_h(last - 1, behind_x1[:, 5, :])
+        square_tanh(3, behind_x1[:, 0, :])
+        finish(0)
+        square_tanh(4, behind_x1[:, 1, :], behind_x1[:, 1, :])
+        finish(1)
+        finish(2)
+        pick_h_behind(last, "x_planes00")
+        for n in range(5, TILES):
+            square_tanh(n, behind_x1[:, n - 3, :])
+        for n in range(3, TILES):
+            finish(n)

@@ -83,11 +83,13 @@ def tile_list_glockenspiel_backward_sweep_kernel(
                     )
                 nc.scalar.dma_start(out=rows[0:TILES, :], in_=lossw.rearrange("(n p) -> n p", p=P))
                 nc.scalar.dma_start(out=rows[TILES : 2 * TILES, :], in_=d.rearrange("(n p) -> n p", p=P))
-        nc.sync.dma_start(pos1_sb[:], pos1)
-        nc.sync.dma_start(pos2_sb[:], pos2)
         for c in range(1, CHUNKS):
             for a in range(K_PASSES):
                 load_w1(a, c)
+                if (a, c) == (0, 1):
+                    nc.sync.dma_start(pos1_sb[:], pos1)
+                if (a, c) == (0, 2):
+                    nc.sync.dma_start(pos2_sb[:], pos2)
         w4_sb = sbuf("w4_sb", [P, R_PASSES * H * 2], U8)
         nc.sync.dma_start(
             out=w4_sb[:].bitcast(I32).rearrange("p (a n) -> p a n", a=R_PASSES),
@@ -105,7 +107,7 @@ def tile_list_glockenspiel_backward_sweep_kernel(
         make_identity(nc, identity[:])
         turned = bank(BANKS - 1)
         nc.tensor.transpose(turned[:, 0:P], rows[:], identity[:])
-        factors = sbuf("factors", [P, 2 * TILES], F32, "raw20")
+        factors = sbuf("factors", [P, 2 * TILES], F32, "raw00")
 
         def round_into_words(copy, grouped, planes):
             copy(
@@ -131,8 +133,8 @@ def tile_list_glockenspiel_backward_sweep_kernel(
             grouped[a, c] = sbuf(f"grouped{a}{c}", [P, CHUNK * PACK], BF16)
             round_into_words(copy, grouped[a, c][:], w1_raw[a, c][:])
 
-        def round_w1_on_gpsimd(a, c, after):
-            grouped[a, c] = sbuf(f"grouped{a}{c}", [P, CHUNK * PACK], BF16, after)
+        def round_w1_on_gpsimd(a, c, place=None):
+            grouped[a, c] = place if place is not None else sbuf(f"grouped{a}{c}", [P, CHUNK * PACK], BF16)
             nc.gpsimd.tensor_scalar(
                 grouped[a, c][:].rearrange("p (c j) -> p c j", j=PACK),
                 w1_raw[a, c][:].rearrange("p j c -> p c j"),
@@ -144,24 +146,26 @@ def tile_list_glockenspiel_backward_sweep_kernel(
 
         w1_mx = {}
 
-        def quantize_w1(a, c):
-            codes = sbuf(f"w1_codes{a}{c}", [P, CHUNK], U32)
+        def quantize_w1(a, c, place=None):
+            codes = place if place is not None else sbuf(f"w1_codes{a}{c}", [P, CHUNK], U32)
             scales = sbuf(f"w1_scales{a}{c}", [P, CHUNK], U8)
             nc.vector.quantize_mx(out=codes[:].bitcast(FP8X4), scales=scales[:], in_=grouped[a, c][:])
             w1_mx[a, c] = codes, scales
+
+        pass_order = [(0, 1, 2)] * CHUNKS
 
         def h_pass(a, c):
             quantize_w1(a, c)
             multiply(a, c)
 
-        def multiply(a, c, tiles=range(TILES_PER_CHUNK)):
+        def multiply(a, c, tiles=range(TILES_PER_CHUNK), parts=halves):
             codes, scales = w1_mx[a, c]
-            order = [(half, u) for u in tiles for half in halves]
+            order = [(half, u) for u in tiles for half in parts]
             if c == 0:
                 order = sorted(order)
             for half, u in order:
                 n = c * TILES_PER_CHUNK + u
-                if a == 0:
+                if a == pass_order[c][0]:
                     h_acc[n, half] = bank((2 * n + half) % BANKS)
                 nc.tensor.matmul_mx(
                     out=h_acc[n, half][:],
@@ -169,8 +173,8 @@ def tile_list_glockenspiel_backward_sweep_kernel(
                     lhsT_scale=scales[:, u * P : (u + 1) * P],
                     rhs=v_words[a, half].bitcast(FP8X4),
                     rhs_scale=v_sc[SCALE_ROWS * a : P, half * BANK : (half + 1) * BANK],
-                    start=(a == 0),
-                    stop=(a == K_PASSES - 1),
+                    start=(a == pass_order[c][0]),
+                    stop=(a == pass_order[c][-1]),
                 )
 
         h_sb = {}
@@ -182,29 +186,41 @@ def tile_list_glockenspiel_backward_sweep_kernel(
             for cols in x_cols[b]
         }
 
-        def h_out(c, after):
-            pair = sbuf(f"h_pair{c}", [P, TILES_PER_CHUNK * S + M], F32, after)
-            for u in range(TILES_PER_CHUNK):
+        def h_out(c, after, pair=None):
+            if pair is None:
+                pair = sbuf(f"h_pair{c}", [P, TILES_PER_CHUNK * S], F32, after)
+            order = [(half, u) for u in range(TILES_PER_CHUNK) for half in halves]
+            if c == 0:
+                order = sorted(order)
+            for half, u in order:
                 n = c * TILES_PER_CHUNK + u
                 h_sb[n] = pair[:, u * S : (u + 1) * S]
-                for half in halves:
-                    nc.scalar.copy(out=h_sb[n][:, half * BANK : (half + 1) * BANK], in_=h_acc[n, half][:])
-            return pair[:, TILES_PER_CHUNK * S :]
+                nc.scalar.copy(out=h_sb[n][:, half * BANK : (half + 1) * BANK], in_=h_acc[n, half][:])
 
-        def pick_x(n, pieces, place=None):
+        carried = {}
+
+        def gather_x(n, cols, place):
+            carried[n, cols.start] = place
+            entries = pos1_sb[:, cols.start // LIST_GROUP : cols.stop // LIST_GROUP]
+            nc.vector.tensor_copy(place, h_sb[n].indirect(entries))
+
+        def send_x(n, cols, x_rows, scalar_engine=False):
             b, q = divmod(n, TILES_PER_PASS)
-            x_rows = sbuf(f"x_rows{n}", [P, M], BF16, {0: "w1_codes21", 1: "w1_scales21", 2: "raw13"}.get(n))
-            for cols in pieces:
-                entries = pos1_sb[:, cols.start // LIST_GROUP : cols.stop // LIST_GROUP]
-                carried = place
-                if place is None:
-                    carried = sbuf(f"carried{n}_{cols.start}", [P, cols.stop - cols.start], F32)[:]
-                nc.vector.tensor_copy(carried, h_sb[n].indirect(entries))
-                nc.gpsimd.tensor_scalar(x_rows[:, cols], carried, factors[:, n : n + 1], -1.0, ALU.mult, ALU.mult)
-            for cols in x_cols[b]:
-                nc.sync.dma_start(
-                    out=x_planes[b, cols.start][QUADRANT * q : QUADRANT * (q + 1), :, :], in_=x_rows[:, cols]
-                )
+            if scalar_engine:
+                nc.scalar.activation(out=x_rows, in_=carried[n, cols.start], func=ACT.Copy, scale=factors[:, n : n + 1])
+            else:
+                nc.gpsimd.tensor_scalar(x_rows, carried[n, cols.start], factors[:, n : n + 1], 0.0, ALU.mult, ALU.add)
+            for part in x_cols[b]:
+                if cols.start <= part.start < cols.stop:
+                    nc.sync.dma_start(
+                        out=x_planes[b, part.start][QUADRANT * q : QUADRANT * (q + 1), :, :],
+                        in_=x_rows[:, part.start - cols.start : part.stop - cols.start],
+                    )
+
+        def pick_x(n, cols, after=None, rows_after=None):
+            width = cols.stop - cols.start
+            gather_x(n, cols, sbuf(f"carried{n}_{cols.start}", [P, width], F32, after)[:])
+            send_x(n, cols, sbuf(f"x_rows{n}_{cols.start}", [P, width], BF16, rows_after)[:])
 
         def pick_h(n, dst):
             h_picked[n] = dst
@@ -214,8 +230,8 @@ def tile_list_glockenspiel_backward_sweep_kernel(
         x_scales = [sbuf(f"x_scales{b}", [P, M], U8) for b in range(R_PASSES)]
         x_grouped = {}
 
-        def round_x(b):
-            x_grouped[b] = sbuf(f"x_grouped{b}", [P, M * PACK], BF16)
+        def round_x(b, after=None):
+            x_grouped[b] = sbuf(f"x_grouped{b}", [P, M * PACK], BF16, after)
             for cols in x_cols[b]:
                 words = x_grouped[b][:, cols.start * PACK : cols.stop * PACK]
                 round_into_words(nc.scalar.copy, words, x_planes[b, cols.start][:])
@@ -225,8 +241,10 @@ def tile_list_glockenspiel_backward_sweep_kernel(
 
         y_acc = {}
 
+        finish_order = (0, 1, 2, 3, 7, 4, 5, 6)
+
         def y_pass(b):
-            for n in range(TILES):
+            for n in finish_order:
                 if b == 0:
                     y_acc[n] = bank(n)
                 first = b * H + n * P
@@ -242,8 +260,11 @@ def tile_list_glockenspiel_backward_sweep_kernel(
 
         result = {}
 
-        def square_tanh(n, dst, squared=None):
+        def tanh(n, dst):
             nc.scalar.activation(out=dst, in_=h_picked[n], func=ACT.Tanh, scale=factors[:, TILES + n : TILES + n + 1])
+
+        def square_tanh(n, dst, squared=None):
+            tanh(n, dst)
             if squared is None:
                 result[n] = dst
                 nc.scalar.activation(out=dst, in_=dst, func=ACT.Square)
@@ -251,99 +272,120 @@ def tile_list_glockenspiel_backward_sweep_kernel(
                 result[n] = squared
                 nc.gpsimd.tensor_tensor(squared, dst, dst, ALU.mult)
 
-        on_scalar, on_vector = nc.scalar.copy, nc.vector.tensor_copy
+        on_scalar = nc.scalar.copy
 
         for a in range(K_PASSES):
             round_w1(a, 0, on_scalar)
+            if a == 0:
+                nc.scalar.activation(out=factors[:, 0:TILES], in_=turned[:, 0:TILES], func=ACT.Copy, scale=-1.0)
+                nc.scalar.copy(out=factors[:, TILES : 2 * TILES], in_=turned[:, TILES : 2 * TILES])
+            if a == K_PASSES - 1:
+                quantize_w1(a, 0)
             for cols in [slice(0, BANK), slice(BANK, S)] if a == K_PASSES - 1 else [slice(0, S)]:
                 gather_words(a, cols)
             if a == 0:
                 nc.vector.tensor_copy(v_sc[:], tab_sc[:].indirect(offs_sb[:]))
-            h_pass(a, 0)
-        nc.scalar.copy(out=factors[:], in_=turned[:, 0 : 2 * TILES])
+            if a < K_PASSES - 1:
+                quantize_w1(a, 0)
+            multiply(a, 0)
 
-        whole = [slice(0, M)]
+        whole = slice(0, M)
         last = TILES - 1
 
-        round_w1(0, 1, on_scalar)
-        h_pass(0, 1)
-        round_w1(1, 1, on_scalar)
-        h_pass(1, 1)
-        round_w1(2, 1, on_vector)
-        h_pass(2, 1)
         def pick_h_behind(n, after):
             pick_h(n, sbuf(f"picked{n}", [P, M], F32, after)[:])
 
-        round_w1_on_gpsimd(0, 2, "grouped21")
-        h_out(0, "raw11")
-        pick_x(0, whole)
-        pick_h_behind(0, None)
+        def multiply_by_tiles(c, passes):
+            for u in range(TILES_PER_CHUNK):
+                for half in halves:
+                    for a in passes:
+                        multiply(a, c, [u], [half])
+
+        def room(name, slots, after):
+            tile = sbuf(name, [P, slots * M], F32, after)
+            return [tile[:, i * M : (i + 1) * M] for i in range(slots)]
+
+        round_w1_on_gpsimd(0, 1)
+        h_out(0, None)
+        h_pass(0, 1)
+        behind = room("behind01", 2, "grouped01")
+        round_w1_on_gpsimd(1, 1, behind[1].bitcast(BF16))
+        gather_x(0, whole, behind[0])
+        h_pass(1, 1)
+        send_x(0, whole, sbuf("x_rows0", [P, M], BF16)[:])
+        round_w1(2, 1, on_scalar)
+        gather_x(1, whole, sbuf("carried1", [P, M], F32, "raw21")[:])
+
+        round_w1(0, 2, on_scalar)
+        quantize_w1(2, 1, sbuf("w1_codes21", [P, CHUNK], U32, "raw02"))
+        multiply(2, 1)
         h_pass(0, 2)
-        pick_x(1, whole, sbuf("carried1", [P, M], F32, "raw02")[:])
-        for a in range(1, K_PASSES):
-            round_w1(a, 2, on_scalar)
-            quantize_w1(a, 2)
-        for u in range(TILES_PER_CHUNK):
-            for a in range(1, K_PASSES):
-                multiply(a, 2, [u])
-        pick_h(1, h_out(1, "raw22"))
+        behind = room("behind21", 3, "grouped21")
+        pick_h(0, behind[0])
+        pick_h(1, behind[1])
+        send_x(1, whole, behind[2].bitcast(BF16)[:, 0:M])
+        round_w1(1, 2, on_scalar)
+        round_w1_on_gpsimd(2, 2)
+        h_out(1, "raw12")
 
-        round_w1_on_gpsimd(1, 3, "grouped22")
-        pick_x(2, whole)
-        round_w1(0, 3, on_scalar)
-        h_pass(0, 3)
+        quantize_w1(1, 2, sbuf("w1_codes12", [P, CHUNK], U32, "raw22"))
+        quantize_w1(2, 2)
+        multiply_by_tiles(2, (1, 2))
+        behind = room("behind12", 2, "grouped12")
+        gather_x(2, whole, behind[0])
+        gather_x(3, whole, behind[1])
+        round_w1_on_gpsimd(0, 3, sbuf("grouped03", [P, CHUNK * PACK], BF16, "grouped22"))
+        send_x(2, whole, sbuf("x_rows2", [P, M], BF16, "raw03")[:])
+        round_w1(1, 3, on_scalar)
+
+        quantize_w1(0, 3, sbuf("w1_codes03", [P, CHUNK], U32, "raw13"))
+        quantize_w1(1, 3)
+        multiply_by_tiles(3, (0, 1))
+        behind = room("behind03", 2, "grouped22")
+        pick_h(2, behind[0])
+        send_x(3, whole, behind[1].bitcast(BF16)[:, 0:M])
         round_w1(2, 3, on_scalar)
-        for a in range(1, K_PASSES):
-            quantize_w1(a, 3)
-        for u in range(TILES_PER_CHUNK):
-            for a in range(1, K_PASSES):
-                multiply(a, 3, [u])
-        pick_x(3, whole, h_out(2, "raw23"))
-        h_out(CHUNKS - 1, None)
-        for n in range(TILES_PER_PASS, TILES):
-            pick_x(n, x_cols[1] if n == last else whole)
+        h_pass(2, 3)
+        h_out(2, "raw23")
+        behind = room("carried45", 2, None)
+        for n in (4, 5):
+            gather_x(n, whole, behind[n - 4])
+            send_x(n, whole, sbuf(f"x_rows{n}", [P, M], BF16)[:])
 
-        def finish(n):
-            if n < finished_on_gpsimd:
-                neg_y = sbuf(f"neg_y{n}", [P, M], F32, f"carried{n}_0")
-                nc.scalar.copy(out=neg_y[:], in_=y_acc[n][:])
-                nc.gpsimd.tensor_tensor(result[n], result[n], neg_y[:], ALU.mult)
-                nc.sync.dma_start(out=out[n * P : (n + 1) * P, :], in_=result[n])
-                return
-            for cols in x_cols[1] if n == last else whole:
+        h_out(CHUNKS - 1, None)
+        pick_x(last - 1, whole)
+        for cols in x_cols[1]:
+            pick_x(last, cols)
+        pick_h_behind(last, None)
+
+        round_x(0, "w1_codes23")
+        quantize_x(0)
+        y_pass(0)
+        behind = room("behind_x0", 2, f"x_planes0{M // 2}")
+        late_squares = room("late_squares", 2, f"carried{last}_{M // 2}")
+        for n in (0, 1):
+            square_tanh(n, behind[n], late_squares[n])
+        behind = room("behind_tanh0", 3, "grouped21")
+        for n in (3, 4, 5):
+            pick_h(n, behind[n - 3])
+        round_x(1)
+        quantize_x(1)
+        y_pass(1)
+        behind = room("behind_x1", 6, f"x_planes1{M // 2}")
+        square_tanh(2, behind[5], behind[5])
+        pick_h_behind(6, "grouped22")
+        square_tanh(3, behind[0], behind[0])
+        tanh(last, behind[1])
+        square_tanh(4, behind[2], behind[2])
+        result[last] = behind[1]
+        nc.scalar.activation(out=behind[1], in_=behind[1], func=ACT.Square)
+        square_tanh(5, behind[3])
+        square_tanh(6, behind[4])
+
+        for n in finish_order:
+            for cols in x_cols[1] if n == finish_order[-1] else [whole]:
                 part = result[n][:, cols]
                 nc.vector.scalar_tensor_tensor(
                     out=part, in0=part, scalar=1.0, in1=y_acc[n][:, cols], op0=ALU.subtract, op1=ALU.mult
                 )
                 nc.sync.dma_start(out=out[n * P : (n + 1) * P, cols], in_=part)
-
-        early = 2
-        finished_on_gpsimd = 1
-        pick_h_behind(early, f"carried{last}_0")
-        round_x(0)
-        quantize_x(0)
-        y_pass(0)
-        behind_x0 = sbuf("behind_x0", [P, 5, M], F32, f"x_planes0{M // 2}")
-        for n in range(early + 1):
-            tanh = behind_x0[:, n, :] if n else sbuf("tanh0", [P, M], F32, "x_planes00")[:]
-            square_tanh(n, tanh, behind_x0[:, n, :])
-            if n < finished_on_gpsimd:
-                nc.gpsimd.tensor_scalar(result[n], result[n], 1.0, -1.0, ALU.mult, ALU.add)
-        pick_h(3, behind_x0[:, 3, :])
-        pick_h_behind(4, "x_planes00")
-        pick_h(5, behind_x0[:, 4, :])
-        round_x(1)
-        quantize_x(1)
-        y_pass(1)
-        behind_x1 = sbuf("behind_x1", [P, 6, M], F32, f"x_planes1{M // 2}")
-        pick_h(last - 1, behind_x1[:, 5, :])
-        square_tanh(3, behind_x1[:, 0, :])
-        finish(0)
-        square_tanh(4, behind_x1[:, 1, :], behind_x1[:, 1, :])
-        finish(1)
-        finish(2)
-        pick_h_behind(last, "x_planes00")
-        for n in range(5, TILES):
-            square_tanh(n, behind_x1[:, n - 3, :])
-        for n in range(3, TILES):
-            finish(n)

@@ -320,13 +320,14 @@ def tile_list_glockenspiel_backward_sweep_kernel(
         quantize_w1(2, 1, sbuf("w1_codes21", [P, CHUNK], U32, "raw02"))
         multiply(2, 1)
         h_pass(0, 2)
-        behind = room("behind21", 3, "grouped21")
+        behind = room("behind21", 2, "grouped21")
         pick_h(0, behind[0])
         pick_h(1, behind[1])
-        send_x(1, whole, behind[2].bitcast(BF16)[:, 0:M])
         round_w1(1, 2, on_scalar)
         round_w1_on_gpsimd(2, 2)
-        h_out(1, "raw12")
+        pair1 = sbuf("h_pair1", [P, TILES_PER_CHUNK * S + M // 2], F32, "raw12")
+        h_out(1, None, pair1)
+        send_x(1, whole, pair1[:, TILES_PER_CHUNK * S :].bitcast(BF16), True)
 
         quantize_w1(1, 2, sbuf("w1_codes12", [P, CHUNK], U32, "raw22"))
         quantize_w1(2, 2)
@@ -335,7 +336,6 @@ def tile_list_glockenspiel_backward_sweep_kernel(
         gather_x(2, whole, behind[0])
         gather_x(3, whole, behind[1])
         round_w1_on_gpsimd(0, 3, sbuf("grouped03", [P, CHUNK * PACK], BF16, "grouped22"))
-        send_x(2, whole, sbuf("x_rows2", [P, M], BF16, "raw03")[:])
         round_w1(1, 3, on_scalar)
 
         quantize_w1(0, 3, sbuf("w1_codes03", [P, CHUNK], U32, "raw13"))
@@ -343,9 +343,10 @@ def tile_list_glockenspiel_backward_sweep_kernel(
         multiply_by_tiles(3, (0, 1))
         behind = room("behind03", 2, "grouped22")
         pick_h(2, behind[0])
-        send_x(3, whole, behind[1].bitcast(BF16)[:, 0:M])
+        send_x(2, whole, behind[1].bitcast(BF16)[:, 0:M])
         round_w1(2, 3, on_scalar)
         h_pass(2, 3)
+        send_x(3, whole, sbuf("x_rows3", [P, M], BF16, "grouped23")[:])
         h_out(2, "raw23")
         behind = room("carried45", 2, None)
         for n in (4, 5):
@@ -362,7 +363,7 @@ def tile_list_glockenspiel_backward_sweep_kernel(
         quantize_x(0)
         y_pass(0)
         behind = room("behind_x0", 2, f"x_planes0{M // 2}")
-        late_squares = room("late_squares", 2, f"carried{last}_{M // 2}")
+        late_squares = room("late_squares", 2, "w1_codes23")
         for n in (0, 1):
             square_tanh(n, behind[n], late_squares[n])
         behind = room("behind_tanh0", 3, "grouped21")
@@ -372,13 +373,11 @@ def tile_list_glockenspiel_backward_sweep_kernel(
         quantize_x(1)
         y_pass(1)
         behind = room("behind_x1", 6, f"x_planes1{M // 2}")
-        square_tanh(2, behind[5], behind[5])
+        square_tanh(2, behind[5], sbuf("square2", [P, M], F32, "x_grouped1")[:])
         pick_h_behind(6, "grouped22")
         square_tanh(3, behind[0], behind[0])
-        tanh(last, behind[1])
-        square_tanh(4, behind[2], behind[2])
-        result[last] = behind[1]
-        nc.scalar.activation(out=behind[1], in_=behind[1], func=ACT.Square)
+        square_tanh(last, behind[1])
+        square_tanh(4, behind[2])
         square_tanh(5, behind[3])
         square_tanh(6, behind[4])
 

@@ -33,6 +33,7 @@ TILES_PER_PASS = PASS // P
 TILES_PER_CHUNK = 2
 CHUNK = TILES_PER_CHUNK * P
 CHUNKS = H // CHUNK
+RAW03 = 4 * (CHUNK + S)
 
 
 def tile_list_glockenspiel_backward_sweep_kernel(
@@ -41,6 +42,7 @@ def tile_list_glockenspiel_backward_sweep_kernel(
     nc = tc.nc
     with ExitStack() as ctx:
         keep = ctx.enter_context(tc.tile_pool(name="keep", bufs=1))
+        shared = ctx.enter_context(tc.tile_pool(name="shared", bufs=1))
         psum = ctx.enter_context(tc.psum_pool(name="psum", bufs=1))
 
         def sbuf(name, shape, dtype, after=None):
@@ -64,7 +66,12 @@ def tile_list_glockenspiel_backward_sweep_kernel(
         w1_raw = {}
 
         def load_w1(a, c):
-            w1_raw[a, c] = sbuf(f"raw{a}{c}", [P, PACK, CHUNK], F32)
+            if (a, c) == (1, 2):
+                w1_raw[a, c] = shared.tile([P, PACK, CHUNK], F32, name="raw12", offset=0, align_bytes=64)
+            elif (a, c) == (0, 3):
+                w1_raw[a, c] = shared.tile([P, PACK, CHUNK], F32, name="raw03", offset=RAW03, align_bytes=64)
+            else:
+                w1_raw[a, c] = sbuf(f"raw{a}{c}", [P, PACK, CHUNK], F32)
             piece = w1[a * PASS : (a + 1) * PASS, c * CHUNK : (c + 1) * CHUNK]
             nc.sync.dma_start(out=w1_raw[a, c][:], in_=piece.rearrange("(p j) c -> p j c", j=PACK))
 
@@ -197,6 +204,10 @@ def tile_list_glockenspiel_backward_sweep_kernel(
                 h_sb[n] = pair[:, u * S : (u + 1) * S]
                 nc.scalar.copy(out=h_sb[n][:, half * BANK : (half + 1) * BANK], in_=h_acc[n, half][:])
 
+        def tile_out(n):
+            for half in halves:
+                nc.scalar.copy(out=h_sb[n][:, half * BANK : (half + 1) * BANK], in_=h_acc[n, half][:])
+
         carried = {}
 
         def gather_x(n, cols, place):
@@ -316,39 +327,41 @@ def tile_list_glockenspiel_backward_sweep_kernel(
         round_w1(2, 1, on_scalar)
         gather_x(1, whole, sbuf("carried1", [P, M], F32, "raw21")[:])
 
+        h_pass(2, 1)
+        send_x(1, whole, sbuf("x_rows1", [P, M], BF16, "grouped21")[:])
         round_w1(0, 2, on_scalar)
-        quantize_w1(2, 1, sbuf("w1_codes21", [P, CHUNK], U32, "raw02"))
-        multiply(2, 1)
-        h_pass(0, 2)
-        behind = room("behind21", 2, "grouped21")
-        pick_h(0, behind[0])
-        pick_h(1, behind[1])
+        pick_h_behind(0, "raw02")
         round_w1(1, 2, on_scalar)
-        round_w1_on_gpsimd(2, 2)
-        pair1 = sbuf("h_pair1", [P, TILES_PER_CHUNK * S + M // 2], F32, "raw12")
-        h_out(1, None, pair1)
-        send_x(1, whole, pair1[:, TILES_PER_CHUNK * S :].bitcast(BF16), True)
 
-        quantize_w1(1, 2, sbuf("w1_codes12", [P, CHUNK], U32, "raw22"))
-        quantize_w1(2, 2)
-        multiply_by_tiles(2, (1, 2))
-        behind = room("behind12", 2, "grouped12")
-        gather_x(2, whole, behind[0])
-        gather_x(3, whole, behind[1])
-        round_w1_on_gpsimd(0, 3, sbuf("grouped03", [P, CHUNK * PACK], BF16, "grouped22"))
-        round_w1(1, 3, on_scalar)
+        quantize_w1(0, 2, shared.tile([P, CHUNK], U32, name="w1_codes02", offset=0, align_bytes=64))
+        quantize_w1(1, 2)
+        multiply_by_tiles(2, (0, 1))
+        behind = room("behind02", 2, "grouped02")
+        round_w1_on_gpsimd(2, 2, sbuf("grouped22", [P, CHUNK * PACK], BF16, "grouped12"))
+        pick_h(1, behind[0])
+        h_sb[2] = shared.tile([P, S], F32, name="h2", offset=4 * CHUNK, align_bytes=64)[:]
+        tile_out(2)
+        gather_x(2, whole, behind[1])
+        round_w1(0, 3, on_scalar)
 
-        quantize_w1(0, 3, sbuf("w1_codes03", [P, CHUNK], U32, "raw13"))
-        quantize_w1(1, 3)
-        multiply_by_tiles(3, (0, 1))
-        behind = room("behind03", 2, "grouped22")
+        quantize_w1(2, 2, shared.tile([P, CHUNK], U32, name="w1_codes22", offset=RAW03, align_bytes=64))
+        multiply(2, 2)
+        h_pass(0, 3)
+        h_sb[3] = shared.tile([P, S], F32, name="h3", offset=RAW03 + 4 * CHUNK, align_bytes=64)[:]
+        tile_out(3)
+        behind = room("behind22", 3, "grouped12")
         pick_h(2, behind[0])
-        send_x(2, whole, behind[1].bitcast(BF16)[:, 0:M])
-        round_w1(2, 3, on_scalar)
-        h_pass(2, 3)
+        gather_x(3, whole, behind[1])
+        send_x(2, whole, behind[2].bitcast(BF16)[:, 0:M])
+        round_w1(1, 3, on_scalar)
+        round_w1_on_gpsimd(2, 3)
+
+        quantize_w1(1, 3, sbuf("w1_codes13", [P, CHUNK], U32, "raw23"))
+        quantize_w1(2, 3)
+        multiply_by_tiles(3, (1, 2))
         send_x(3, whole, sbuf("x_rows3", [P, M], BF16, "grouped23")[:])
-        h_out(2, "raw23")
-        behind = room("carried45", 2, None)
+        h_out(2, "raw13")
+        behind = room("carried45", 2, "grouped13")
         for n in (4, 5):
             gather_x(n, whole, behind[n - 4])
             send_x(n, whole, sbuf(f"x_rows{n}", [P, M], BF16)[:])
@@ -366,7 +379,7 @@ def tile_list_glockenspiel_backward_sweep_kernel(
         late_squares = room("late_squares", 2, "w1_codes23")
         for n in (0, 1):
             square_tanh(n, behind[n], late_squares[n])
-        behind = room("behind_tanh0", 3, "grouped21")
+        behind = room("behind_tanh0", 3, "raw02")
         for n in (3, 4, 5):
             pick_h(n, behind[n - 3])
         round_x(1)
@@ -374,7 +387,7 @@ def tile_list_glockenspiel_backward_sweep_kernel(
         y_pass(1)
         behind = room("behind_x1", 6, f"x_planes1{M // 2}")
         square_tanh(2, behind[5], sbuf("square2", [P, M], F32, "x_grouped1")[:])
-        pick_h_behind(6, "grouped22")
+        pick_h_behind(6, "grouped12")
         square_tanh(3, behind[0], behind[0])
         square_tanh(last, behind[1])
         square_tanh(4, behind[2])

@@ -33,6 +33,7 @@ TILES_PER_PASS = PASS // P
 TILES_PER_CHUNK = 2
 CHUNK = TILES_PER_CHUNK * P
 CHUNKS = H // CHUNK
+LAST_CUT = 3 * M // 4
 RAW03 = 4 * (CHUNK + S)
 
 
@@ -116,10 +117,10 @@ def tile_list_glockenspiel_backward_sweep_kernel(
         nc.tensor.transpose(turned[:, 0:P], rows[:], identity[:])
         factors = sbuf("factors", [P, 2 * TILES], F32, "raw00")
 
-        def round_into_words(copy, grouped, planes):
+        def round_into_words(copy, grouped, planes, run):
             copy(
-                out=grouped.rearrange("p (g i j) -> p g j i", i=RUN, j=PACK),
-                in_=planes.rearrange("p j (g i) -> p g j i", i=RUN),
+                out=grouped.rearrange("p (g i j) -> p g j i", i=run, j=PACK),
+                in_=planes.rearrange("p j (g i) -> p g j i", i=run),
             )
 
         v_words = {}
@@ -138,7 +139,7 @@ def tile_list_glockenspiel_backward_sweep_kernel(
 
         def round_w1(a, c, copy):
             grouped[a, c] = sbuf(f"grouped{a}{c}", [P, CHUNK * PACK], BF16)
-            round_into_words(copy, grouped[a, c][:], w1_raw[a, c][:])
+            round_into_words(copy, grouped[a, c][:], w1_raw[a, c][:], RUN)
 
         def round_w1_on_gpsimd(a, c, place=None):
             grouped[a, c] = place if place is not None else sbuf(f"grouped{a}{c}", [P, CHUNK * PACK], BF16)
@@ -197,8 +198,6 @@ def tile_list_glockenspiel_backward_sweep_kernel(
             if pair is None:
                 pair = sbuf(f"h_pair{c}", [P, TILES_PER_CHUNK * S], F32, after)
             order = [(half, u) for u in range(TILES_PER_CHUNK) for half in halves]
-            if c == 0:
-                order = sorted(order)
             for half, u in order:
                 n = c * TILES_PER_CHUNK + u
                 h_sb[n] = pair[:, u * S : (u + 1) * S]
@@ -245,7 +244,7 @@ def tile_list_glockenspiel_backward_sweep_kernel(
             x_grouped[b] = sbuf(f"x_grouped{b}", [P, M * PACK], BF16, after)
             for cols in x_cols[b]:
                 words = x_grouped[b][:, cols.start * PACK : cols.stop * PACK]
-                round_into_words(nc.scalar.copy, words, x_planes[b, cols.start][:])
+                round_into_words(nc.scalar.copy, words, x_planes[b, cols.start][:], 2 * RUN)
 
         def quantize_x(b):
             nc.vector.quantize_mx(out=x_codes[b][:].bitcast(FP8X4), scales=x_scales[b][:], in_=x_grouped[b][:])
@@ -316,17 +315,17 @@ def tile_list_glockenspiel_backward_sweep_kernel(
             tile = sbuf(name, [P, slots * M], F32, after)
             return [tile[:, i * M : (i + 1) * M] for i in range(slots)]
 
-        round_w1_on_gpsimd(0, 1)
-        h_out(0, None)
-        h_pass(0, 1)
+        round_w1(0, 1, on_scalar)
+        h_out(0, "raw01")
+        round_w1(1, 1, nc.vector.tensor_copy)
+        quantize_w1(0, 1, sbuf("w1_codes01", [P, CHUNK], U32, "raw11"))
+        quantize_w1(1, 1)
+        multiply_by_tiles(1, (0, 1))
         behind = room("behind01", 2, "grouped01")
-        round_w1_on_gpsimd(1, 1, behind[1].bitcast(BF16))
         gather_x(0, whole, behind[0])
-        h_pass(1, 1)
         send_x(0, whole, sbuf("x_rows0", [P, M], BF16)[:])
+        gather_x(1, whole, behind[1])
         round_w1(2, 1, on_scalar)
-        gather_x(1, whole, sbuf("carried1", [P, M], F32, "raw21")[:])
-
         h_pass(2, 1)
         send_x(1, whole, sbuf("x_rows1", [P, M], BF16, "grouped21")[:])
         round_w1(0, 2, on_scalar)
@@ -347,19 +346,20 @@ def tile_list_glockenspiel_backward_sweep_kernel(
         quantize_w1(2, 2, shared.tile([P, CHUNK], U32, name="w1_codes22", offset=RAW03, align_bytes=64))
         multiply(2, 2)
         h_pass(0, 3)
-        h_sb[3] = shared.tile([P, S], F32, name="h3", offset=RAW03 + 4 * CHUNK, align_bytes=64)[:]
+        third = shared.tile([P, S + M // 2], F32, name="h3", offset=RAW03 + 4 * CHUNK, align_bytes=64)
+        h_sb[3] = third[:, 0:S]
         tile_out(3)
-        behind = room("behind22", 3, "grouped12")
+        send_x(2, whole, third[:, S:].bitcast(BF16), True)
+        behind = room("behind22", 2, "grouped12")
         pick_h(2, behind[0])
         gather_x(3, whole, behind[1])
-        send_x(2, whole, behind[2].bitcast(BF16)[:, 0:M])
         round_w1(1, 3, on_scalar)
-        round_w1_on_gpsimd(2, 3)
+        round_w1_on_gpsimd(2, 3, sbuf("grouped23", [P, CHUNK * PACK], BF16, "grouped03"))
 
         quantize_w1(1, 3, sbuf("w1_codes13", [P, CHUNK], U32, "raw23"))
         quantize_w1(2, 3)
         multiply_by_tiles(3, (1, 2))
-        send_x(3, whole, sbuf("x_rows3", [P, M], BF16, "grouped23")[:])
+        send_x(3, whole, sbuf("x_rows3", [P, M], BF16, "grouped03")[:])
         h_out(2, "raw13")
         behind = room("carried45", 2, "grouped13")
         for n in (4, 5):
@@ -391,11 +391,11 @@ def tile_list_glockenspiel_backward_sweep_kernel(
         square_tanh(3, behind[0], behind[0])
         square_tanh(last, behind[1])
         square_tanh(4, behind[2])
-        square_tanh(5, behind[3])
+        square_tanh(5, behind[3], behind[3])
         square_tanh(6, behind[4])
 
         for n in finish_order:
-            for cols in x_cols[1] if n == finish_order[-1] else [whole]:
+            for cols in [slice(0, LAST_CUT), slice(LAST_CUT, M)] if n == finish_order[-1] else [whole]:
                 part = result[n][:, cols]
                 nc.vector.scalar_tensor_tensor(
                     out=part, in0=part, scalar=1.0, in1=y_acc[n][:, cols], op0=ALU.subtract, op1=ALU.mult

@@ -35,6 +35,7 @@ CHUNK = TILES_PER_CHUNK * P
 CHUNKS = H // CHUNK
 LAST_CUT = 3 * M // 4
 RAW03 = 4 * (CHUNK + S)
+PLANES = 2 * RAW03 + 1024 + 3072
 
 
 def tile_list_glockenspiel_backward_sweep_kernel(
@@ -113,6 +114,8 @@ def tile_list_glockenspiel_backward_sweep_kernel(
 
         identity = sbuf("identity", [P, P], F32)
         make_identity(nc, identity[:])
+        identity16 = sbuf("identity16", [P, P], BF16)
+        nc.gpsimd.tensor_copy(identity16[:], identity[:])
         turned = bank(BANKS - 1)
         nc.tensor.transpose(turned[:, 0:P], rows[:], identity[:])
         factors = sbuf("factors", [P, 2 * TILES], F32, "raw00")
@@ -188,11 +191,14 @@ def tile_list_glockenspiel_backward_sweep_kernel(
         h_sb = {}
         h_picked = {}
         x_cols = [[slice(0, M // 2), slice(M // 2, M)]] * R_PASSES
+        def placed(name, shape, dtype, offset):
+            return shared.tile(shape, dtype, name=name, offset=offset, align_bytes=64)
+
         x_planes = {
-            (b, cols.start): sbuf(f"x_planes{b}{cols.start}", [P, PACK, cols.stop - cols.start], BF16)
-            for b in range(R_PASSES)
-            for cols in x_cols[b]
+            (0, 0): placed("x_planes00", [P, PACK, M // 2], BF16, PLANES),
+            (0, M // 2): sbuf("x_planes01", [P, PACK, M // 2], BF16),
         }
+        late_rows = {}
 
         def h_out(c, after, pair=None):
             if pair is None:
@@ -220,6 +226,10 @@ def tile_list_glockenspiel_backward_sweep_kernel(
                 nc.scalar.activation(out=x_rows, in_=carried[n, cols.start], func=ACT.Copy, scale=factors[:, n : n + 1])
             else:
                 nc.gpsimd.tensor_scalar(x_rows, carried[n, cols.start], factors[:, n : n + 1], 0.0, ALU.mult, ALU.add)
+            if b == 1:
+                for first in range(cols.start, cols.stop, P):
+                    late_rows[q, first // P] = x_rows[:, first - cols.start : first - cols.start + P]
+                return
             for part in x_cols[b]:
                 if cols.start <= part.start < cols.stop:
                     nc.sync.dma_start(
@@ -236,27 +246,22 @@ def tile_list_glockenspiel_backward_sweep_kernel(
             h_picked[n] = dst
             nc.vector.tensor_copy(dst, h_sb[n].indirect(pos2_sb[:]))
 
-        x_codes = [sbuf(f"x_codes{b}", [P, M], U32) for b in range(R_PASSES)]
-        x_scales = [sbuf(f"x_scales{b}", [P, M], U8) for b in range(R_PASSES)]
+        x_codes = {}
+        x_scales = {1: sbuf("x_scales1", [P, M], U8)}
         x_grouped = {}
 
-        def round_x(b, after=None):
-            x_grouped[b] = sbuf(f"x_grouped{b}", [P, M * PACK], BF16, after)
-            for cols in x_cols[b]:
-                words = x_grouped[b][:, cols.start * PACK : cols.stop * PACK]
-                round_into_words(nc.scalar.copy, words, x_planes[b, cols.start][:], 2 * RUN)
-
-        def quantize_x(b):
+        def quantize_x(b, after=None):
+            x_codes[b] = sbuf(f"x_codes{b}", [P, M], U32, after)
             nc.vector.quantize_mx(out=x_codes[b][:].bitcast(FP8X4), scales=x_scales[b][:], in_=x_grouped[b][:])
 
         y_acc = {}
 
-        finish_order = (0, 1, 2, 3, 7, 4, 5, 6)
+        finish_order = (0, 1, 2, 3, 4, 7, 6, 5)
 
-        def y_pass(b):
-            for n in finish_order:
+        def y_products():
+            for place, n, b in [(place, n, b) for place, n in enumerate(finish_order) for b in range(R_PASSES)]:
                 if b == 0:
-                    y_acc[n] = bank(n)
+                    y_acc[n] = bank((place + 6) % BANKS)
                 first = b * H + n * P
                 nc.tensor.matmul_mx(
                     out=y_acc[n][:],
@@ -372,32 +377,80 @@ def tile_list_glockenspiel_backward_sweep_kernel(
             pick_x(last, cols)
         pick_h_behind(last, None)
 
-        round_x(0, "w1_codes23")
-        quantize_x(0)
-        y_pass(0)
-        behind = room("behind_x0", 2, f"x_planes0{M // 2}")
-        late_squares = room("late_squares", 2, "w1_codes23")
-        for n in (0, 1):
-            square_tanh(n, behind[n], late_squares[n])
-        behind = room("behind_tanh0", 3, "raw02")
-        for n in (3, 4, 5):
-            pick_h(n, behind[n - 3])
-        round_x(1)
-        quantize_x(1)
-        y_pass(1)
-        behind = room("behind_x1", 6, f"x_planes1{M // 2}")
-        square_tanh(2, behind[5], sbuf("square2", [P, M], F32, "x_grouped1")[:])
-        pick_h_behind(6, "grouped12")
-        square_tanh(3, behind[0], behind[0])
-        square_tanh(last, behind[1])
-        square_tanh(4, behind[2])
-        square_tanh(5, behind[3], behind[3])
-        square_tanh(6, behind[4])
+        x_halves = [
+            sbuf("x_grouped0", [P, M * PACK], BF16, "w1_codes23"),
+        ]
+        x_grouped[0] = x_halves[0]
+        first_half, second_half = x_cols[0]
+        round_into_words(on_scalar, x_grouped[0][:, 0 : M // 2 * PACK], x_planes[0, 0][:], 2 * RUN)
+        early_tanh = placed("early_tanh", [P, 2 * M], F32, PLANES + 1792)
+        early = [early_tanh[:, 0:M], early_tanh[:, M : 2 * M]]
+        tanh(1, early[1])
+        tanh(0, early[0])
 
-        for n in finish_order:
+        blocks = M // P
+        across_all = placed("across", [P, (blocks - 1) * 2 * P], F32, PLANES + 256 - 3072)
+        across = [across_all[:, j * 2 * P : (j + 1) * 2 * P] for j in range(blocks - 1)]
+        across.append(placed("last_turned", [P, 2 * P], F32, PLANES + 256)[:])
+        x_grouped[1] = sbuf("x_grouped1", [P, M * PACK], BF16)
+        for j in range(blocks):
+            first_turn = psum.tile([P, PASS], BF16, name=f"first_turn{j}", tag=f"bank{j}")
+            for q in range(TILES_PER_PASS):
+                nc.tensor.transpose(first_turn[:, q * P : (q + 1) * P], late_rows[q, j], identity16[:])
+            nc.scalar.copy(
+                out=across[j].rearrange("m (u p) -> m u p", u=2),
+                in_=first_turn[:].bitcast(F32).rearrange("m (p u) -> m u p", u=2),
+            )
+        for pair in range(blocks // 2):
+            second_turn = bank(blocks + pair)
+            for j in range(2):
+                words = across[2 * pair + j]
+                for u in range(2):
+                    place = second_turn[:, (2 * j + u) * P : (2 * j + u + 1) * P]
+                    nc.tensor.transpose(place, words[:, u * P : (u + 1) * P], identity[:])
+            nc.scalar.copy(
+                out=x_grouped[1][:].bitcast(F32)[:, pair * BANK : (pair + 1) * BANK].rearrange("p (j m u) -> p j m u", j=2, u=2),
+                in_=second_turn[:].rearrange("p (j u m) -> p j m u", j=2, u=2),
+            )
+
+        nc.gpsimd.tensor_scalar(
+            x_grouped[0][:, M // 2 * PACK :].rearrange("p (c j) -> p c j", j=PACK),
+            x_planes[0, M // 2][:].rearrange("p j c -> p c j"),
+            1.0,
+            0.0,
+            ALU.mult,
+            ALU.add,
+        )
+        behind = room("behind_tanh1", 2, "grouped02")
+        for n in (3, 4):
+            pick_h(n, behind[n - 3])
+        result[0] = sbuf("square0", [P, M], F32)[:]
+        nc.gpsimd.tensor_tensor(result[0], early[0], early[0], ALU.mult)
+        x_scales[0] = placed("x_scales0", [P, M], U8, PLANES + 256)
+        quantize_x(0)
+        quantize_x(1)
+        y_products()
+        behind = room("behind_x0", 8, "w1_codes23")
+        behind_x1 = room("behind_x1", 2, "x_grouped1")
+        result[1] = behind[1]
+        nc.scalar.activation(out=result[1], in_=early[1], func=ACT.Square)
+        late_picks = placed("late_picks", [P, 2 * M], F32, PLANES + 4864)
+        for n in (5, 6):
+            pick_h(n, late_picks[:, (n - 5) * M : (n - 4) * M])
+        square_tanh(2, behind[2])
+        square_tanh(3, behind[3], behind_x1[1])
+        square_tanh(last, behind[7], behind[7])
+        square_tanh(4, behind[4])
+
+        def finish(n):
             for cols in [slice(0, LAST_CUT), slice(LAST_CUT, M)] if n == finish_order[-1] else [whole]:
                 part = result[n][:, cols]
                 nc.vector.scalar_tensor_tensor(
                     out=part, in0=part, scalar=1.0, in1=y_acc[n][:, cols], op0=ALU.subtract, op1=ALU.mult
                 )
                 nc.sync.dma_start(out=out[n * P : (n + 1) * P, cols], in_=part)
+
+        square_tanh(5, behind[5], behind[5])
+        square_tanh(6, behind[6])
+        for n in finish_order:
+            finish(n)

@@ -261,7 +261,7 @@ def tile_list_glockenspiel_backward_sweep_kernel(
         def y_products():
             for place, n, b in [(place, n, b) for place, n in enumerate(finish_order) for b in range(R_PASSES)]:
                 if b == 0:
-                    y_acc[n] = bank((place + 6) % BANKS)
+                    y_acc[n] = bank((place + 7) % BANKS)
                 first = b * H + n * P
                 nc.tensor.matmul_mx(
                     out=y_acc[n][:],
@@ -401,16 +401,17 @@ def tile_list_glockenspiel_backward_sweep_kernel(
                 out=across[j].rearrange("m (u p) -> m u p", u=2),
                 in_=first_turn[:].bitcast(F32).rearrange("m (p u) -> m u p", u=2),
             )
-        for pair in range(blocks // 2):
-            second_turn = bank(blocks + pair)
-            for j in range(2):
-                words = across[2 * pair + j]
+        for index, group in enumerate([(0, 1), (2,), (3,)]):
+            second_turn = bank(blocks + index)
+            for i, j in enumerate(group):
                 for u in range(2):
-                    place = second_turn[:, (2 * j + u) * P : (2 * j + u + 1) * P]
-                    nc.tensor.transpose(place, words[:, u * P : (u + 1) * P], identity[:])
+                    place = second_turn[:, (2 * i + u) * P : (2 * i + u + 1) * P]
+                    nc.tensor.transpose(place, across[j][:, u * P : (u + 1) * P], identity[:])
+            width = 2 * P * len(group)
+            first = 2 * P * group[0]
             nc.scalar.copy(
-                out=x_grouped[1][:].bitcast(F32)[:, pair * BANK : (pair + 1) * BANK].rearrange("p (j m u) -> p j m u", j=2, u=2),
-                in_=second_turn[:].rearrange("p (j u m) -> p j m u", j=2, u=2),
+                out=x_grouped[1][:].bitcast(F32)[:, first : first + width].rearrange("p (j m u) -> p j m u", m=P, u=2),
+                in_=second_turn[:, 0:width].rearrange("p (j u m) -> p j m u", m=P, u=2),
             )
 
         nc.gpsimd.tensor_scalar(
@@ -430,13 +431,12 @@ def tile_list_glockenspiel_backward_sweep_kernel(
         quantize_x(0)
         quantize_x(1)
         y_products()
-        behind = room("behind_x0", 8, "w1_codes23")
+        behind = room("behind_x0", 10, "w1_codes23")
         behind_x1 = room("behind_x1", 2, "x_grouped1")
         result[1] = behind[1]
         nc.scalar.activation(out=result[1], in_=early[1], func=ACT.Square)
-        late_picks = placed("late_picks", [P, 2 * M], F32, PLANES + 4864)
         for n in (5, 6):
-            pick_h(n, late_picks[:, (n - 5) * M : (n - 4) * M])
+            pick_h(n, behind[n + 3])
         square_tanh(2, behind[2])
         square_tanh(3, behind[3], behind_x1[1])
         square_tanh(last, behind[7], behind[7])

@@ -425,14 +425,14 @@ def tile_list_glockenspiel_backward_sweep_kernel(
         behind = room("behind_tanh1", 2, "grouped02")
         for n in (3, 4):
             pick_h(n, behind[n - 3])
-        result[0] = sbuf("square0", [P, M], F32)[:]
-        nc.gpsimd.tensor_tensor(result[0], early[0], early[0], ALU.mult)
         x_scales[0] = placed("x_scales0", [P, M], U8, PLANES + 256)
         quantize_x(0)
         quantize_x(1)
         y_products()
         behind = room("behind_x0", 10, "w1_codes23")
         behind_x1 = room("behind_x1", 2, "x_grouped1")
+        result[0] = behind_x1[0]
+        nc.gpsimd.tensor_tensor(result[0], early[0], early[0], ALU.mult)
         result[1] = behind[1]
         nc.scalar.activation(out=result[1], in_=early[1], func=ACT.Square)
         for n in (5, 6):

@@ -34,6 +34,7 @@ TILES_PER_CHUNK = 2
 CHUNK = TILES_PER_CHUNK * P
 CHUNKS = H // CHUNK
 LAST_CUT = 3 * M // 4
+SCALE_FIRST = 16
 RAW03 = 4 * (CHUNK + S)
 PLANES = 2 * RAW03 + 1024 + 3072
 
@@ -58,11 +59,19 @@ def tile_list_glockenspiel_backward_sweep_kernel(
         pos2_sb = keep.tile([P, M // LIST_GROUP], U16, name="pos2_sb")
 
         tab_sc = sbuf("tab_sc", [P, T], U8)
-        nc.vector.memset(tab_sc[:].bitcast(I32), 0)
+        rows_per_pass = PASS // QUADRANT
+        pairs_end = SCALE_FIRST + 2 * rows_per_pass
+        rows_end = pairs_end + rows_per_pass
+        nc.vector.memset(tab_sc[0:SCALE_FIRST, :].bitcast(I32), 0)
+        nc.vector.memset(tab_sc[rows_end:P, :].bitcast(I32), 0)
+        v_sc01 = sbuf("v_sc01", [P, 2 * S], U8)
+        v_sc2 = sbuf("v_sc2", [P, S], U8)
+        v_sc = [v_sc01[:, 0:S], v_sc01[:, S : 2 * S], v_sc2[:]]
         rows = sbuf("rows", [P, P], F32)
-        nc.vector.memset(rows[:], 0.0)
+        nc.gpsimd.memset(rows[:], 0.0)
         w4_sc = sbuf("w4_sc", [P, R_PASSES * H], U8)
-        nc.vector.memset(w4_sc[:].bitcast(I32), 0)
+        for plane in (v_sc01, v_sc2, w4_sc):
+            nc.gpsimd.memset(plane[:].bitcast(I32), 0)
 
         tab_sb = [sbuf(f"tab{a}", [P, T], I32) for a in range(K_PASSES)]
         w1_raw = {}
@@ -77,21 +86,37 @@ def tile_list_glockenspiel_backward_sweep_kernel(
             piece = w1[a * PASS : (a + 1) * PASS, c * CHUNK : (c + 1) * CHUNK]
             nc.sync.dma_start(out=w1_raw[a, c][:], in_=piece.rearrange("(p j) c -> p j c", j=PACK))
 
-        nc.sync.dma_start(offs_sb[:], offs)
-        for a in range(K_PASSES):
-            if a == K_PASSES - 1:
-                load_w1(a, 0)
+        def load_table(a):
             nc.sync.dma_start(out=tab_sb[a][:], in_=tab_words[a].rearrange("p t i -> p (t i)").bitcast(I32))
-            if a < K_PASSES - 1:
-                load_w1(a, 0)
-            if a == 0:
-                for q in range(P // QUADRANT):
-                    nc.sync.dma_start(
-                        out=tab_sc[QUADRANT * q : QUADRANT * q + SCALE_ROWS * K_PASSES, :].bitcast(I32),
-                        in_=tab_scales[:, SCALE_ROWS * q : SCALE_ROWS * (q + 1), :].bitcast(I32),
-                    )
-                nc.scalar.dma_start(out=rows[0:TILES, :], in_=lossw.rearrange("(n p) -> n p", p=P))
-                nc.scalar.dma_start(out=rows[TILES : 2 * TILES, :], in_=d.rearrange("(n p) -> n p", p=P))
+
+        nc.sync.dma_start(offs_sb[:], offs)
+        nc.sync.dma_start(
+            out=tab_sc[SCALE_FIRST:pairs_end, :].bitcast(I32),
+            in_=tab_scales[0:2].bitcast(I32).rearrange("a r t -> r a t"),
+        )
+        nc.sync.dma_start(out=tab_sc[pairs_end:rows_end, :].bitcast(I32), in_=tab_scales[2].bitcast(I32))
+        load_table(0)
+        load_w1(0, 0)
+        nc.scalar.dma_start(out=rows[0:TILES, :], in_=lossw.rearrange("(n p) -> n p", p=P))
+        nc.scalar.dma_start(out=rows[TILES : 2 * TILES, :], in_=d.rearrange("(n p) -> n p", p=P))
+        load_table(1)
+        picked_rows = sbuf("picked_rows", [P, S], U8)
+        nc.vector.tensor_copy(picked_rows[:], tab_sc[:].indirect(offs_sb[:]))
+        for q in range(P // QUADRANT):
+            first = SCALE_FIRST + 2 * SCALE_ROWS * q
+            nc.sync.dma_start(
+                out=v_sc01[QUADRANT * q : QUADRANT * q + SCALE_ROWS, :].bitcast(I32),
+                in_=picked_rows[first : first + 2 * SCALE_ROWS, :].bitcast(I32),
+            )
+        load_w1(1, 0)
+        load_w1(2, 0)
+        load_table(2)
+        for q in range(P // QUADRANT):
+            first = pairs_end + SCALE_ROWS * q
+            nc.sync.dma_start(
+                out=v_sc2[QUADRANT * q : QUADRANT * q + SCALE_ROWS, :].bitcast(I32),
+                in_=picked_rows[first : first + SCALE_ROWS, :].bitcast(I32),
+            )
         for c in range(1, CHUNKS):
             for a in range(K_PASSES):
                 load_w1(a, c)
@@ -127,7 +152,6 @@ def tile_list_glockenspiel_backward_sweep_kernel(
             )
 
         v_words = {}
-        v_sc = sbuf("v_sc", [P, S], U8)
         halves = range(S // BANK)
 
         def gather_words(a, cols):
@@ -183,7 +207,7 @@ def tile_list_glockenspiel_backward_sweep_kernel(
                     lhsT=codes[:, u * P : (u + 1) * P].bitcast(FP8X4),
                     lhsT_scale=scales[:, u * P : (u + 1) * P],
                     rhs=v_words[a, half].bitcast(FP8X4),
-                    rhs_scale=v_sc[SCALE_ROWS * a : P, half * BANK : (half + 1) * BANK],
+                    rhs_scale=v_sc[a][:, half * BANK : (half + 1) * BANK],
                     start=(a == pass_order[c][0]),
                     stop=(a == pass_order[c][-1]),
                 )
@@ -298,8 +322,6 @@ def tile_list_glockenspiel_backward_sweep_kernel(
                 quantize_w1(a, 0)
             for cols in [slice(0, BANK), slice(BANK, S)] if a == K_PASSES - 1 else [slice(0, S)]:
                 gather_words(a, cols)
-            if a == 0:
-                nc.vector.tensor_copy(v_sc[:], tab_sc[:].indirect(offs_sb[:]))
             if a < K_PASSES - 1:
                 quantize_w1(a, 0)
             multiply(a, 0)

@@ -36,7 +36,7 @@ CHUNKS = H // CHUNK
 LAST_CUT = 3 * M // 4
 SCALE_FIRST = 16
 RAW03 = 4 * (CHUNK + S)
-PLANES = 2 * RAW03 + 1024 + 3072
+PLANES = 2 * RAW03 + 2048 + 3072
 
 
 def tile_list_glockenspiel_backward_sweep_kernel(
@@ -103,6 +103,13 @@ def tile_list_glockenspiel_backward_sweep_kernel(
         picked_rows = sbuf("picked_rows", [P, S], U8)
         nc.vector.tensor_copy(picked_rows[:], tab_sc[:].indirect(offs_sb[:]))
         for q in range(P // QUADRANT):
+            first = pairs_end + SCALE_ROWS * q
+            nc.sync.dma_start(
+                out=v_sc2[QUADRANT * q : QUADRANT * q + SCALE_ROWS, :].bitcast(I32),
+                in_=picked_rows[first : first + SCALE_ROWS, :].bitcast(I32),
+            )
+        load_table(2)
+        for q in range(P // QUADRANT):
             first = SCALE_FIRST + 2 * SCALE_ROWS * q
             nc.sync.dma_start(
                 out=v_sc01[QUADRANT * q : QUADRANT * q + SCALE_ROWS, :].bitcast(I32),
@@ -110,13 +117,6 @@ def tile_list_glockenspiel_backward_sweep_kernel(
             )
         load_w1(1, 0)
         load_w1(2, 0)
-        load_table(2)
-        for q in range(P // QUADRANT):
-            first = pairs_end + SCALE_ROWS * q
-            nc.sync.dma_start(
-                out=v_sc2[QUADRANT * q : QUADRANT * q + SCALE_ROWS, :].bitcast(I32),
-                in_=picked_rows[first : first + SCALE_ROWS, :].bitcast(I32),
-            )
         for c in range(1, CHUNKS):
             for a in range(K_PASSES):
                 load_w1(a, c)
@@ -313,18 +313,33 @@ def tile_list_glockenspiel_backward_sweep_kernel(
 
         on_scalar = nc.scalar.copy
 
-        for a in range(K_PASSES):
-            round_w1(a, 0, on_scalar)
-            if a == 0:
-                nc.scalar.activation(out=factors[:, 0:TILES], in_=turned[:, 0:TILES], func=ACT.Copy, scale=-1.0)
-                nc.scalar.copy(out=factors[:, TILES : 2 * TILES], in_=turned[:, TILES : 2 * TILES])
-            if a == K_PASSES - 1:
-                quantize_w1(a, 0)
-            for cols in [slice(0, BANK), slice(BANK, S)] if a == K_PASSES - 1 else [slice(0, S)]:
-                gather_words(a, cols)
-            if a < K_PASSES - 1:
-                quantize_w1(a, 0)
-            multiply(a, 0)
+        round_w1(0, 0, on_scalar)
+        nc.scalar.activation(out=factors[:, 0:TILES], in_=turned[:, 0:TILES], func=ACT.Copy, scale=-1.0)
+        nc.scalar.copy(out=factors[:, TILES : 2 * TILES], in_=turned[:, TILES : 2 * TILES])
+        gather_words(0, slice(0, S))
+        h_pass(0, 0)
+        gather_words(1, slice(0, S))
+        gather_words(2, slice(0, S))
+        by_tile = {}
+        for a in (1, 2):
+            for u in range(TILES_PER_CHUNK):
+                by_tile[a, u] = sbuf(f"grouped{a}0{u}", [P, P * PACK], BF16)
+                round_into_words(on_scalar, by_tile[a, u][:], w1_raw[a, 0][:, :, u * P : (u + 1) * P], RUN)
+        for u in range(TILES_PER_CHUNK):
+            for a in (1, 2):
+                codes = sbuf(f"w1_codes{a}0{u}", [P, P], U32, "raw20" if (a, u) == (1, 1) else None)
+                scales = sbuf(f"w1_scales{a}0{u}", [P, P], U8)
+                nc.vector.quantize_mx(out=codes[:].bitcast(FP8X4), scales=scales[:], in_=by_tile[a, u][:])
+                for half in halves:
+                    nc.tensor.matmul_mx(
+                        out=h_acc[u, half][:],
+                        lhsT=codes[:].bitcast(FP8X4),
+                        lhsT_scale=scales[:],
+                        rhs=v_words[a, half].bitcast(FP8X4),
+                        rhs_scale=v_sc[a][:, half * BANK : (half + 1) * BANK],
+                        start=False,
+                        stop=(a == K_PASSES - 1),
+                    )
 
         whole = slice(0, M)
         last = TILES - 1
@@ -342,21 +357,20 @@ def tile_list_glockenspiel_backward_sweep_kernel(
             tile = sbuf(name, [P, slots * M], F32, after)
             return [tile[:, i * M : (i + 1) * M] for i in range(slots)]
 
-        round_w1(0, 1, on_scalar)
-        h_out(0, "raw01")
-        round_w1(1, 1, nc.vector.tensor_copy)
-        quantize_w1(0, 1, sbuf("w1_codes01", [P, CHUNK], U32, "raw11"))
-        quantize_w1(1, 1)
-        multiply_by_tiles(1, (0, 1))
-        behind = room("behind01", 2, "grouped01")
-        gather_x(0, whole, behind[0])
-        send_x(0, whole, sbuf("x_rows0", [P, M], BF16)[:])
-        gather_x(1, whole, behind[1])
-        round_w1(2, 1, on_scalar)
-        h_pass(2, 1)
-        send_x(1, whole, sbuf("x_rows1", [P, M], BF16, "grouped21")[:])
+        round_w1(0, 1, nc.vector.tensor_copy)
+        h_pass(0, 1)
+        h_out(0, None)
+        round_w1_on_gpsimd(1, 1, sbuf("grouped11", [P, CHUNK * PACK], BF16, "grouped01"))
+        gather_x(0, whole, sbuf("carried0", [P, M], F32)[:])
+        gather_x(1, whole, sbuf("carried1", [P, M], F32)[:])
+        grouped[2, 1] = sbuf("grouped21", [P, CHUNK * PACK], BF16, "w1_codes201")
+        round_into_words(on_scalar, grouped[2, 1][:], w1_raw[2, 1][:], RUN)
+        quantize_w1(1, 1, sbuf("w1_codes11", [P, CHUNK], U32, "raw21"))
+        quantize_w1(2, 1)
+        multiply_by_tiles(1, (1, 2))
+        send_x(0, whole, sbuf("x_rows0", [P, M], BF16, "w1_codes201")[:])
+        pick_h_behind(0, "grouped01")
         round_w1(0, 2, on_scalar)
-        pick_h_behind(0, "raw02")
         round_w1(1, 2, on_scalar)
 
         quantize_w1(0, 2, shared.tile([P, CHUNK], U32, name="w1_codes02", offset=0, align_bytes=64))
@@ -373,10 +387,11 @@ def tile_list_glockenspiel_backward_sweep_kernel(
         quantize_w1(2, 2, shared.tile([P, CHUNK], U32, name="w1_codes22", offset=RAW03, align_bytes=64))
         multiply(2, 2)
         h_pass(0, 3)
-        third = shared.tile([P, S + M // 2], F32, name="h3", offset=RAW03 + 4 * CHUNK, align_bytes=64)
+        third = shared.tile([P, S + M], F32, name="h3", offset=RAW03 + 4 * CHUNK, align_bytes=64)
         h_sb[3] = third[:, 0:S]
         tile_out(3)
-        send_x(2, whole, third[:, S:].bitcast(BF16), True)
+        send_x(1, whole, third[:, S : S + M // 2].bitcast(BF16), True)
+        send_x(2, whole, third[:, S + M // 2 :].bitcast(BF16), True)
         behind = room("behind22", 2, "grouped12")
         pick_h(2, behind[0])
         gather_x(3, whole, behind[1])

@@ -435,8 +435,8 @@ def tile_list_glockenspiel_backward_sweep_kernel(
             for q in range(TILES_PER_PASS):
                 nc.tensor.transpose(first_turn[:, q * P : (q + 1) * P], late_rows[q, j], identity16[:])
             nc.scalar.copy(
-                out=across[j].rearrange("m (u p) -> m u p", u=2),
-                in_=first_turn[:].bitcast(F32).rearrange("m (p u) -> m u p", u=2),
+                out=across[j].rearrange("m (u p) -> m p u", u=2),
+                in_=first_turn[:].bitcast(F32).rearrange("m (p u) -> m p u", u=2),
             )
         for index, group in enumerate([(0, 1), (2,), (3,)]):
             second_turn = bank(blocks + index)

from contextlib import ExitStack

import concourse.mybir as mybir
from concourse.masks import make_identity

K, H, T, S, M = 1536, 1024, 2048, 1024, 512
FLOPS = 2 * K * H * S + 2 * H * H * M

F32 = mybir.dt.float32
BF16 = mybir.dt.bfloat16
I32 = mybir.dt.int32
U32 = mybir.dt.uint32
U16 = mybir.dt.uint16
U8 = mybir.dt.uint8
FP8X4 = mybir.dt.float8_e4m3fn_x4
FP4X4 = mybir.dt.float4_e2m1fn_x4
ACT = mybir.ActivationFunctionType
ALU = mybir.AluOpType

P = 128
PACK = 4
PASS = P * PACK
K_PASSES = K // PASS
R_PASSES = H // PASS
BANK = 512
BANKS = 8
QUADRANT = 32
SCALE_ROWS = 4
LIST_GROUP = 16
RUN = 2
TILES = H // P
TILES_PER_PASS = PASS // P
TILES_PER_CHUNK = 2
CHUNK = TILES_PER_CHUNK * P
CHUNKS = H // CHUNK
LAST_CUT = 3 * M // 4
SCALE_FIRST = 16
RAW03 = 4 * (CHUNK + S)
PLANES = 2 * RAW03 + 2048 + 3072


def tile_list_glockenspiel_backward_sweep_kernel(
    tc, tab_words, tab_scales, offs, pos1, pos2, w1, lossw, w4_words, w4_scales, d, out
):
    nc = tc.nc
    with ExitStack() as ctx:
        keep = ctx.enter_context(tc.tile_pool(name="keep", bufs=1))
        shared = ctx.enter_context(tc.tile_pool(name="shared", bufs=1))
        psum = ctx.enter_context(tc.psum_pool(name="psum", bufs=1))

        def sbuf(name, shape, dtype, after=None):
            return keep.tile(shape, dtype, name=name, tag=after or name, align_bytes=64)

        def bank(index):
            return psum.tile([P, BANK], F32, name=f"bank{index}", tag=f"bank{index}")

        offs_sb = keep.tile([P, S // LIST_GROUP], U16, name="offs_sb")
        pos1_sb = keep.tile([P, M // LIST_GROUP], U16, name="pos1_sb")
        pos2_sb = keep.tile([P, M // LIST_GROUP], U16, name="pos2_sb")

        tab_sc = sbuf("tab_sc", [P, T], U8)
        rows_per_pass = PASS // QUADRANT
        pairs_end = SCALE_FIRST + 2 * rows_per_pass
        rows_end = pairs_end + rows_per_pass
        nc.vector.memset(tab_sc[0:SCALE_FIRST, :].bitcast(I32), 0)
        nc.vector.memset(tab_sc[rows_end:P, :].bitcast(I32), 0)
        v_sc01 = sbuf("v_sc01", [P, 2 * S], U8)
        v_sc2 = sbuf("v_sc2", [P, S], U8)
        v_sc = [v_sc01[:, 0:S], v_sc01[:, S : 2 * S], v_sc2[:]]
        rows = sbuf("rows", [P, P], F32)
        nc.gpsimd.memset(rows[:], 0.0)
        w4_sc = sbuf("w4_sc", [P, R_PASSES * H], U8)
        for plane in (v_sc01, v_sc2, w4_sc):
            nc.gpsimd.memset(plane[:].bitcast(I32), 0)

        tab_sb = [sbuf(f"tab{a}", [P, T], I32) for a in range(K_PASSES)]
        w1_raw = {}

        def load_w1(a, c):
            if (a, c) == (1, 2):
                w1_raw[a, c] = shared.tile([P, PACK, CHUNK], F32, name="raw12", offset=0, align_bytes=64)
            elif (a, c) == (0, 3):
                w1_raw[a, c] = shared.tile([P, PACK, CHUNK], F32, name="raw03", offset=RAW03, align_bytes=64)
            else:
                w1_raw[a, c] = sbuf(f"raw{a}{c}", [P, PACK, CHUNK], F32)
            piece = w1[a * PASS : (a + 1) * PASS, c * CHUNK : (c + 1) * CHUNK]
            nc.sync.dma_start(out=w1_raw[a, c][:], in_=piece.rearrange("(p j) c -> p j c", j=PACK))

        def load_table(a):
            nc.sync.dma_start(out=tab_sb[a][:], in_=tab_words[a].rearrange("p t i -> p (t i)").bitcast(I32))

        nc.sync.dma_start(offs_sb[:], offs)
        nc.sync.dma_start(
            out=tab_sc[SCALE_FIRST:pairs_end, :].bitcast(I32),
            in_=tab_scales[0:2].bitcast(I32).rearrange("a r t -> r a t"),
        )
        nc.sync.dma_start(out=tab_sc[pairs_end:rows_end, :].bitcast(I32), in_=tab_scales[2].bitcast(I32))
        load_table(0)
        load_w1(0, 0)
        nc.scalar.dma_start(out=rows[0:TILES, :], in_=lossw.rearrange("(n p) -> n p", p=P))
        nc.scalar.dma_start(out=rows[TILES : 2 * TILES, :], in_=d.rearrange("(n p) -> n p", p=P))
        load_table(1)
        picked_rows = sbuf("picked_rows", [P, S], U8)
        nc.vector.tensor_copy(picked_rows[:], tab_sc[:].indirect(offs_sb[:]))
        for q in range(P // QUADRANT):
            first = pairs_end + SCALE_ROWS * q
            nc.sync.dma_start(
                out=v_sc2[QUADRANT * q : QUADRANT * q + SCALE_ROWS, :].bitcast(I32),
                in_=picked_rows[first : first + SCALE_ROWS, :].bitcast(I32),
            )
        load_table(2)
        for q in range(P // QUADRANT):
            first = SCALE_FIRST + 2 * SCALE_ROWS * q
            nc.sync.dma_start(
                out=v_sc01[QUADRANT * q : QUADRANT * q + SCALE_ROWS, :].bitcast(I32),
                in_=picked_rows[first : first + 2 * SCALE_ROWS, :].bitcast(I32),
            )
        load_w1(1, 0)
        load_w1(2, 0)
        for c in range(1, CHUNKS):
            for a in range(K_PASSES):
                load_w1(a, c)
                if (a, c) == (0, 1):
                    nc.sync.dma_start(pos1_sb[:], pos1)
                if (a, c) == (0, 2):
                    nc.sync.dma_start(pos2_sb[:], pos2)
        w4_sb = sbuf("w4_sb", [P, R_PASSES * H * 2], U8)
        nc.sync.dma_start(
            out=w4_sb[:].bitcast(I32).rearrange("p (a n) -> p a n", a=R_PASSES),
            in_=w4_words.bitcast(I32).rearrange("a p n -> p a n"),
        )
        for q in range(P // QUADRANT):
            nc.sync.dma_start(
                out=w4_sc[QUADRANT * q : QUADRANT * q + SCALE_ROWS, :]
                .bitcast(I32)
                .rearrange("s (a n) -> s a n", a=R_PASSES),
                in_=w4_scales[:, SCALE_ROWS * q : SCALE_ROWS * (q + 1), :].bitcast(I32).rearrange("a s n -> s a n"),
            )

        identity = sbuf("identity", [P, P], F32)
        make_identity(nc, identity[:])
        identity16 = sbuf("identity16", [P, P], BF16)
        nc.gpsimd.tensor_copy(identity16[:], identity[:])
        turned = bank(BANKS - 1)
        nc.tensor.transpose(turned[:, 0:P], rows[:], identity[:])
        factors = sbuf("factors", [P, 2 * TILES], F32, "raw00")

        def round_into_words(copy, grouped, planes, run):
            copy(
                out=grouped.rearrange("p (g i j) -> p g j i", i=run, j=PACK),
                in_=planes.rearrange("p j (g i) -> p g j i", i=run),
            )

        v_words = {}
        halves = range(S // BANK)

        def gather_words(a, cols):
            words = sbuf(f"v_words{a}{cols.start}", [P, cols.stop - cols.start], U32)
            entries = offs_sb[:, cols.start // LIST_GROUP : cols.stop // LIST_GROUP]
            nc.vector.tensor_copy(words[:], tab_sb[a][:].bitcast(U32).indirect(entries))
            for first in range(cols.start, cols.stop, BANK):
                v_words[a, first // BANK] = words[:, first - cols.start : first - cols.start + BANK]

        grouped = {}
        h_acc = {}

        def round_w1(a, c, copy):
            grouped[a, c] = sbuf(f"grouped{a}{c}", [P, CHUNK * PACK], BF16)
            round_into_words(copy, grouped[a, c][:], w1_raw[a, c][:], RUN)

        def round_w1_on_gpsimd(a, c, place=None):
            grouped[a, c] = place if place is not None else sbuf(f"grouped{a}{c}", [P, CHUNK * PACK], BF16)
            nc.gpsimd.tensor_scalar(
                grouped[a, c][:].rearrange("p (c j) -> p c j", j=PACK),
                w1_raw[a, c][:].rearrange("p j c -> p c j"),
                1.0,
                0.0,
                ALU.mult,
                ALU.add,
            )

        w1_mx = {}

        def quantize_w1(a, c, place=None):
            codes = place if place is not None else sbuf(f"w1_codes{a}{c}", [P, CHUNK], U32)
            scales = sbuf(f"w1_scales{a}{c}", [P, CHUNK], U8)
            nc.vector.quantize_mx(out=codes[:].bitcast(FP8X4), scales=scales[:], in_=grouped[a, c][:])
            w1_mx[a, c] = codes, scales

        pass_order = [(0, 1, 2)] * CHUNKS

        def h_pass(a, c):
            quantize_w1(a, c)
            multiply(a, c)

        def multiply(a, c, tiles=range(TILES_PER_CHUNK), parts=halves):
            codes, scales = w1_mx[a, c]
            order = [(half, u) for u in tiles for half in parts]
            if c == 0:
                order = sorted(order)
            for half, u in order:
                n = c * TILES_PER_CHUNK + u
                if a == pass_order[c][0]:
                    h_acc[n, half] = bank((2 * n + half) % BANKS)
                nc.tensor.matmul_mx(
                    out=h_acc[n, half][:],
                    lhsT=codes[:, u * P : (u + 1) * P].bitcast(FP8X4),
                    lhsT_scale=scales[:, u * P : (u + 1) * P],
                    rhs=v_words[a, half].bitcast(FP8X4),
                    rhs_scale=v_sc[a][:, half * BANK : (half + 1) * BANK],
                    start=(a == pass_order[c][0]),
                    stop=(a == pass_order[c][-1]),
                )

        h_sb = {}
        h_picked = {}
        x_cols = [[slice(0, M // 2), slice(M // 2, M)]] * R_PASSES
        def placed(name, shape, dtype, offset):
            return shared.tile(shape, dtype, name=name, offset=offset, align_bytes=64)

        x_planes = {
            (0, 0): placed("x_planes00", [P, PACK, M // 2], BF16, PLANES),
            (0, M // 2): sbuf("x_planes01", [P, PACK, M // 2], BF16),
        }
        late_rows = {}

        def h_out(c, after, pair=None):
            if pair is None:
                pair = sbuf(f"h_pair{c}", [P, TILES_PER_CHUNK * S], F32, after)
            order = [(half, u) for u in range(TILES_PER_CHUNK) for half in halves]
            for half, u in order:
                n = c * TILES_PER_CHUNK + u
                h_sb[n] = pair[:, u * S : (u + 1) * S]
                nc.scalar.copy(out=h_sb[n][:, half * BANK : (half + 1) * BANK], in_=h_acc[n, half][:])

        def tile_out(n):
            for half in halves:
                nc.scalar.copy(out=h_sb[n][:, half * BANK : (half + 1) * BANK], in_=h_acc[n, half][:])

        carried = {}

        def gather_x(n, cols, place):
            carried[n, cols.start] = place
            entries = pos1_sb[:, cols.start // LIST_GROUP : cols.stop // LIST_GROUP]
            nc.vector.tensor_copy(place, h_sb[n].indirect(entries))

        def send_x(n, cols, x_rows, scalar_engine=False):
            b, q = divmod(n, TILES_PER_PASS)
            if scalar_engine:
                nc.scalar.activation(out=x_rows, in_=carried[n, cols.start], func=ACT.Copy, scale=factors[:, n : n + 1])
            else:
                nc.gpsimd.tensor_scalar(x_rows, carried[n, cols.start], factors[:, n : n + 1], 0.0, ALU.mult, ALU.add)
            if b == 1:
                for first in range(cols.start, cols.stop, P):
                    late_rows[q, first // P] = x_rows[:, first - cols.start : first - cols.start + P]
                return
            for part in x_cols[b]:
                if cols.start <= part.start < cols.stop:
                    nc.sync.dma_start(
                        out=x_planes[b, part.start][QUADRANT * q : QUADRANT * (q + 1), :, :],
                        in_=x_rows[:, part.start - cols.start : part.stop - cols.start],
                    )

        def pick_x(n, cols, after=None, rows_after=None):
            width = cols.stop - cols.start
            gather_x(n, cols, sbuf(f"carried{n}_{cols.start}", [P, width], F32, after)[:])
            send_x(n, cols, sbuf(f"x_rows{n}_{cols.start}", [P, width], BF16, rows_after)[:])

        def pick_h(n, dst):
            h_picked[n] = dst
            nc.vector.tensor_copy(dst, h_sb[n].indirect(pos2_sb[:]))

        x_codes = {}
        x_scales = {1: sbuf("x_scales1", [P, M], U8)}
        x_grouped = {}

        def quantize_x(b, after=None):
            x_codes[b] = sbuf(f"x_codes{b}", [P, M], U32, after)
            nc.vector.quantize_mx(out=x_codes[b][:].bitcast(FP8X4), scales=x_scales[b][:], in_=x_grouped[b][:])

        y_acc = {}

        finish_order = (0, 1, 2, 3, 4, 7, 6, 5)

        def y_products():
            for place, n, b in [(place, n, b) for place, n in enumerate(finish_order) for b in range(R_PASSES)]:
                if b == 0:
                    y_acc[n] = bank((place + 7) % BANKS)
                first = b * H + n * P
                nc.tensor.matmul_mx(
                    out=y_acc[n][:],
                    lhsT=w4_sb[:, 2 * first : 2 * (first + P)].bitcast(FP4X4),
                    lhsT_scale=w4_sc[:, first : first + P],
                    rhs=x_codes[b][:].bitcast(FP8X4),
                    rhs_scale=x_scales[b][:],
                    start=(b == 0),
                    stop=(b == R_PASSES - 1),
                )

        result = {}

        def tanh(n, dst):
            nc.scalar.activation(out=dst, in_=h_picked[n], func=ACT.Tanh, scale=factors[:, TILES + n : TILES + n + 1])

        def square_tanh(n, dst, squared=None):
            tanh(n, dst)
            if squared is None:
                result[n] = dst
                nc.scalar.activation(out=dst, in_=dst, func=ACT.Square)
            else:
                result[n] = squared
                nc.gpsimd.tensor_tensor(squared, dst, dst, ALU.mult)

        on_scalar = nc.scalar.copy

        round_w1(0, 0, on_scalar)
        nc.scalar.activation(out=factors[:, 0:TILES], in_=turned[:, 0:TILES], func=ACT.Copy, scale=-1.0)
        nc.scalar.copy(out=factors[:, TILES : 2 * TILES], in_=turned[:, TILES : 2 * TILES])
        gather_words(0, slice(0, S))
        h_pass(0, 0)
        gather_words(1, slice(0, S))
        gather_words(2, slice(0, S))
        by_tile = {}
        for a in (1, 2):
            for u in range(TILES_PER_CHUNK):
                by_tile[a, u] = sbuf(f"grouped{a}0{u}", [P, P * PACK], BF16)
                round_into_words(on_scalar, by_tile[a, u][:], w1_raw[a, 0][:, :, u * P : (u + 1) * P], RUN)
        for u in range(TILES_PER_CHUNK):
            for a in (1, 2):
                codes = sbuf(f"w1_codes{a}0{u}", [P, P], U32, "raw20" if (a, u) == (1, 1) else None)
                scales = sbuf(f"w1_scales{a}0{u}", [P, P], U8)
                nc.vector.quantize_mx(out=codes[:].bitcast(FP8X4), scales=scales[:], in_=by_tile[a, u][:])
                for half in halves:
                    nc.tensor.matmul_mx(
                        out=h_acc[u, half][:],
                        lhsT=codes[:].bitcast(FP8X4),
                        lhsT_scale=scales[:],
                        rhs=v_words[a, half].bitcast(FP8X4),
                        rhs_scale=v_sc[a][:, half * BANK : (half + 1) * BANK],
                        start=False,
                        stop=(a == K_PASSES - 1),
                    )

        whole = slice(0, M)
        last = TILES - 1

        def pick_h_behind(n, after):
            pick_h(n, sbuf(f"picked{n}", [P, M], F32, after)[:])

        def multiply_by_tiles(c, passes):
            for u in range(TILES_PER_CHUNK):
                for half in halves:
                    for a in passes:
                        multiply(a, c, [u], [half])

        def room(name, slots, after):
            tile = sbuf(name, [P, slots * M], F32, after)
            return [tile[:, i * M : (i + 1) * M] for i in range(slots)]

        round_w1(0, 1, nc.vector.tensor_copy)
        h_pass(0, 1)
        h_out(0, None)
        round_w1_on_gpsimd(1, 1, sbuf("grouped11", [P, CHUNK * PACK], BF16, "grouped01"))
        gather_x(0, whole, sbuf("carried0", [P, M], F32)[:])
        gather_x(1, whole, sbuf("carried1", [P, M], F32)[:])
        grouped[2, 1] = sbuf("grouped21", [P, CHUNK * PACK], BF16, "w1_codes201")
        round_into_words(on_scalar, grouped[2, 1][:], w1_raw[2, 1][:], RUN)
        quantize_w1(1, 1, sbuf("w1_codes11", [P, CHUNK], U32, "raw21"))
        quantize_w1(2, 1)
        multiply_by_tiles(1, (1, 2))
        send_x(0, whole, sbuf("x_rows0", [P, M], BF16, "w1_codes201")[:])
        pick_h_behind(0, "grouped01")
        round_w1(0, 2, on_scalar)
        round_w1(1, 2, on_scalar)

        quantize_w1(0, 2, shared.tile([P, CHUNK], U32, name="w1_codes02", offset=0, align_bytes=64))
        quantize_w1(1, 2)
        multiply_by_tiles(2, (0, 1))
        behind = room("behind02", 2, "grouped02")
        round_w1_on_gpsimd(2, 2, sbuf("grouped22", [P, CHUNK * PACK], BF16, "grouped12"))
        pick_h(1, behind[0])
        h_sb[2] = shared.tile([P, S], F32, name="h2", offset=4 * CHUNK, align_bytes=64)[:]
        tile_out(2)
        gather_x(2, whole, behind[1])
        round_w1(0, 3, on_scalar)

        quantize_w1(2, 2, shared.tile([P, CHUNK], U32, name="w1_codes22", offset=RAW03, align_bytes=64))
        multiply(2, 2)
        h_pass(0, 3)
        third = shared.tile([P, S + M], F32, name="h3", offset=RAW03 + 4 * CHUNK, align_bytes=64)
        h_sb[3] = third[:, 0:S]
        tile_out(3)
        send_x(1, whole, third[:, S : S + M // 2].bitcast(BF16), True)
        send_x(2, whole, third[:, S + M // 2 :].bitcast(BF16), True)
        behind = room("behind22", 2, "grouped12")
        pick_h(2, behind[0])
        gather_x(3, whole, behind[1])
        round_w1(1, 3, on_scalar)
        round_w1_on_gpsimd(2, 3, sbuf("grouped23", [P, CHUNK * PACK], BF16, "grouped03"))

        quantize_w1(1, 3, sbuf("w1_codes13", [P, CHUNK], U32, "raw23"))
        quantize_w1(2, 3)
        multiply_by_tiles(3, (1, 2))
        send_x(3, whole, sbuf("x_rows3", [P, M], BF16, "grouped03")[:])
        h_out(2, "raw13")
        behind = room("carried45", 2, "grouped13")
        for n in (4, 5):
            gather_x(n, whole, behind[n - 4])
            send_x(n, whole, sbuf(f"x_rows{n}", [P, M], BF16)[:])

        h_out(CHUNKS - 1, None)
        pick_x(last - 1, whole)
        for cols in x_cols[1]:
            pick_x(last, cols)
        pick_h_behind(last, None)

        x_halves = [
            sbuf("x_grouped0", [P, M * PACK], BF16, "w1_codes23"),
        ]
        x_grouped[0] = x_halves[0]
        first_half, second_half = x_cols[0]
        round_into_words(on_scalar, x_grouped[0][:, 0 : M // 2 * PACK], x_planes[0, 0][:], 2 * RUN)
        early_tanh = placed("early_tanh", [P, 2 * M], F32, PLANES + 1792)
        early = [early_tanh[:, 0:M], early_tanh[:, M : 2 * M]]
        tanh(1, early[1])
        tanh(0, early[0])

        blocks = M // P
        across_all = placed("across", [P, (blocks - 1) * 2 * P], F32, PLANES + 256 - 3072)
        across = [across_all[:, j * 2 * P : (j + 1) * 2 * P] for j in range(blocks - 1)]
        across.append(placed("last_turned", [P, 2 * P], F32, PLANES + 256)[:])
        x_grouped[1] = sbuf("x_grouped1", [P, M * PACK], BF16)
        for j in range(blocks):
            first_turn = psum.tile([P, PASS], BF16, name=f"first_turn{j}", tag=f"bank{j}")
            for q in range(TILES_PER_PASS):
                nc.tensor.transpose(first_turn[:, q * P : (q + 1) * P], late_rows[q, j], identity16[:])
            nc.scalar.copy(
                out=across[j].rearrange("m (u p) -> m p u", u=2),
                in_=first_turn[:].bitcast(F32).rearrange("m (p u) -> m p u", u=2),
            )
        for index, group in enumerate([(0, 1), (2,), (3,)]):
            second_turn = bank(blocks + index)
            for i, j in enumerate(group):
                for u in range(2):
                    place = second_turn[:, (2 * i + u) * P : (2 * i + u + 1) * P]
                    nc.tensor.transpose(place, across[j][:, u * P : (u + 1) * P], identity[:])
            width = 2 * P * len(group)
            first = 2 * P * group[0]
            nc.scalar.copy(
                out=x_grouped[1][:].bitcast(F32)[:, first : first + width].rearrange("p (j m u) -> p j m u", m=P, u=2),
                in_=second_turn[:, 0:width].rearrange("p (j u m) -> p j m u", m=P, u=2),
            )

        nc.gpsimd.tensor_scalar(
            x_grouped[0][:, M // 2 * PACK :].rearrange("p (c j) -> p c j", j=PACK),
            x_planes[0, M // 2][:].rearrange("p j c -> p c j"),
            1.0,
            0.0,
            ALU.mult,
            ALU.add,
        )
        behind = room("behind_tanh1", 2, "grouped02")
        for n in (3, 4):
            pick_h(n, behind[n - 3])
        x_scales[0] = placed("x_scales0", [P, M], U8, PLANES + 256)
        quantize_x(0)
        quantize_x(1)
        y_products()
        behind = room("behind_x0", 10, "w1_codes23")
        behind_x1 = room("behind_x1", 2, "x_grouped1")
        result[0] = behind_x1[0]
        nc.gpsimd.tensor_tensor(result[0], early[0], early[0], ALU.mult)
        result[1] = behind[1]
        nc.scalar.activation(out=result[1], in_=early[1], func=ACT.Square)
        for n in (5, 6):
            pick_h(n, behind[n + 3])
        square_tanh(2, behind[2])
        square_tanh(3, behind[3], behind_x1[1])
        square_tanh(last, behind[7], behind[7])
        square_tanh(4, behind[4])

        def finish(n):
            for cols in [slice(0, LAST_CUT), slice(LAST_CUT, M)] if n == finish_order[-1] else [whole]:
                part = result[n][:, cols]
                nc.vector.scalar_tensor_tensor(
                    out=part, in0=part, scalar=1.0, in1=y_acc[n][:, cols], op0=ALU.subtract, op1=ALU.mult
                )
                nc.sync.dma_start(out=out[n * P : (n + 1) * P, cols], in_=part)

        square_tanh(5, behind[5], behind[5])
        square_tanh(6, behind[6])
        for n in finish_order:
            finish(n)
